import numpy as np, ml_dtypes
CORES = [24,25,26,27,28,29,30,31]
N = 8
import mx_ref
BF = ml_dtypes.bfloat16
def cols(t, e):
    v = np.concatenate([t.reshape(128, -1, 4), np.zeros((128, 1, 4), BF)], axis=1)
    return np.ascontiguousarray(v[:, e]).reshape(128, -1)
def pick(q, e):
    c = np.concatenate([q[0].reshape(128, -1, 4), np.zeros((128, 1, 4), np.uint8)], axis=1); s = np.concatenate([q[1], np.ones((16, 1), np.uint8)], axis=1)
    return (np.ascontiguousarray(c[:, e].reshape(128, -1)), np.ascontiguousarray(s[:, e]))
def join(*qs):
    return (np.concatenate([q[0] for q in qs], axis=1), np.concatenate([q[1] for q in qs], axis=1))
def put(q, e, v):
    c, s = q[0].reshape(128, -1, 4).copy(), q[1].copy(); c[:, e] = v[0].reshape(128, -1, 4); s[:, e] = v[1]
    return (c.reshape(128, -1), s)
def pk(c, s):
    return (np.ascontiguousarray(c), mx_ref.live(s))
def emit(q):
    return q[0], q[1]
def decode(q):
    o = []
    for b in range(4):
        e = np.zeros((128, 128, 4), np.float32); e[np.arange(128), np.arange(128), b] = 1
        o.append(mx_ref.matmul(mx_ref.quantize(e.reshape(128, 512).astype(BF)), q))
    return np.stack(o, axis=2).reshape(128, -1)
def f(rng, *shape):
    return mx_ref.flush((rng.standard_normal(shape, dtype=np.float32) * np.exp2(rng.integers(-2, 3, shape[:-1] + (1,)))).astype(BF))
def wide(rng, *shape, cols=0):
    v = rng.standard_normal(shape, dtype=np.float32) * np.exp2(rng.integers(-12, 13, shape)).astype(np.float32)
    if cols: v *= np.repeat(np.exp2(rng.integers(-cols, cols + 1, shape[:-2] + (1, shape[-1] // 4))) * (rng.random(shape[:-2] + (1, shape[-1] // 4)) > 0.0625), 4, axis=-1).astype(np.float32)
    return mx_ref.flush(v.astype(BF))
P, K, O = 256, 64, 1
def big(v):
    v = np.array(v.astype(np.float32))
    v[np.abs(v) < np.float32(2.0 ** -16)] = 0
    return v.astype(BF)
def sized(t, a):
    return big(t.astype(np.float32) * np.repeat(np.asarray(a, np.float32), 4, axis=-1))
def query(rng):
    v = np.zeros((N, 128, 512), BF)
    v[:, :, :4] = f(rng, 1, 128, 4)
    return v
def plain(rng):
    return {"lv": big(f(rng, N, 128, 4 * P)), "dm": big(f(rng, N, 128, 4 * P)), "nz": big(f(rng, N, 128, 4 * P)), "u": query(rng), "z": query(rng), "w": f(rng, N, 128, 512 * O)}
def positive(d):
    return {k: v if k == "w" else np.abs(v.astype(np.float32)).astype(BF) for k, v in d.items()}
def onto(t, e, rng):
    at, far = np.arange(N * P), e[e >= P]
    free = rng.permutation(np.setdiff1d(np.arange(P), e))[:far.size]
    at[free], at[far] = far, free
    return np.stack(np.split(cols(np.concatenate(t, axis=1), at), N, axis=1))
def setup_inputs(rng):
    return plain(rng)
def setup_inputs_ties(rng):
    d = plain(rng)
    for k in ("lv", "dm", "nz"):
        v = big((1 + rng.random((128, 48))) * 2.0 ** 27)
        d[k] = np.stack([big(cols(v, rng.permutation(np.arange(P) % 12)).astype(np.float32) * np.repeat(1 - 2 * rng.integers(0, 2, P), 4)) for r in range(N)])
    for k in ("u", "z"): d[k][:, :, :4] = big((1 + rng.random((1, 128, 4))) * 2.0 ** 29)
    return d
def setup_inputs_one(rng):
    d = positive(plain(rng))
    a, b = rng.permutation(N)[:2]
    g, h = np.ones((N, P)), np.ones((N, P))
    g[a, rng.permutation(P)[:K]] = 2.0 ** -8
    g[b, rng.permutation(P)[:K]] = 2.0 ** -4
    h[b, rng.permutation(P)[:K]] = 2.0 ** 8
    h[a, rng.permutation(P)[:K]] = 2.0 ** 4
    d["lv"], d["dm"] = sized(d["lv"], g[:, None]), sized(d["dm"], h[:, None])
    return d
def setup_inputs_again(rng):
    d = positive(plain(rng))
    n, top = K // N, (np.arange(128) < 64)[None, :, None]
    lt, lb, dt, db, nt = np.ones((5, N, P))
    for r in range(N):
        at, to = rng.permutation(P), rng.permutation(P)
        lt[r, at[:n]], lt[r, at[n:2 * n]] = 2.0 ** -6, 2.0 ** -3
        lb[r, at[:n:2]] = 2.0 ** 8
        nt[r, at[:n // 2]], nt[r, at[n // 2:n]] = 2.0 ** -8, 2.0 ** 4
        dt[r, to[:n]] = 2.0 ** -8
        db[r, to[:n]], db[r, to[n:2 * n]] = 2.0 ** 6, 2.0 ** 3
    d["lv"] = sized(d["lv"], np.where(top, lt[:, None], lb[:, None]))
    d["dm"] = sized(d["dm"], np.where(top, dt[:, None], db[:, None]))
    d["nz"] = sized(d["nz"], np.where(top, nt[:, None], 1.0))
    d["u"], d["z"] = big(d["u"].astype(np.float32) * top), big(d["z"].astype(np.float32) * ~top)
    return d
def setup_inputs_zero(rng):
    d = plain(rng)
    g, h, e = np.ones((3, N, P))
    for r in range(N):
        g[r, rng.permutation(P)[:3 * K // (2 * N)]] = 0
        h[r, rng.permutation(P)[K // (2 * N):]] = 0
        e[r, rng.permutation(P)[:P // 2]] = 0
    d["lv"], d["dm"], d["nz"] = sized(d["lv"], g[:, None]), sized(d["dm"], h[:, None]), sized(d["nz"], e[:, None])
    return d
def setup_inputs_spread(rng):
    d = plain(rng)
    d["lv"] = sized(wide(rng, N, 128, 4 * P), 32 * np.exp2(rng.integers(-6, 7, (N, 1, P))))
    for k in ("dm", "nz"): d[k] = sized(wide(rng, N, 128, 4 * P, cols=6), np.full((1, 1, P), 32.0))
    for k in ("u", "z"): d[k] = sized(d[k], np.full((1, 1, 128), 2.0 ** 24))
    low = np.concatenate([score(d["u"][r], mx_ref.quantize(np.ascontiguousarray(d["lv"][r]))) for r in range(N)])
    high = np.concatenate([score(d["z"][r], mx_ref.quantize(np.ascontiguousarray(d["dm"][r]))) for r in range(N)])
    d["lv"] = onto(d["lv"], np.argsort(low, kind="stable")[:K], rng)
    d["dm"] = onto(d["dm"], np.argsort(-high, kind="stable")[:K], rng)
    return d
def check_inputs(d):
    b = []
    for k, lo, hi in (("lv", -16, 28), ("dm", -16, 28), ("nz", -16, 28), ("u", -30, 30), ("z", -30, 30), ("w", -30, 30)):
        v = np.abs(d[k].astype(np.float32))
        if not (np.isfinite(v).all() and ((v == 0) | (v >= 2.0 ** lo) & (v <= 2.0 ** hi)).all()): b.append("a value of " + k)
    for k in ("u", "z"):
        v = d[k].astype(np.float32)
        if (v[:, :, 4:] != 0).any(): b.append(k + " has numbers behind its column 0")
        if (v != v[:1]).any(): b.append(k + " isn't the same on all ranks")
    return b
def score(t, q):
    return np.abs(mx_ref.matmul(mx_ref.quantize(np.ascontiguousarray(t)), q)[0]) + np.float32(0)
def reference(lv, dm, nz, u, z, w):
    L = [mx_ref.quantize(np.ascontiguousarray(lv[r])) for r in range(N)]
    X = [mx_ref.quantize(np.ascontiguousarray(dm[r])) for r in range(N)]
    noise = join(*[mx_ref.quantize(np.ascontiguousarray(nz[r])) for r in range(N)])
    oc, osc = np.zeros((N, 128, 8 * P), np.uint8), np.zeros((N, 16, 2 * P), np.uint8)
    sw, lw, y = np.zeros((N, 2, K), np.float32), np.zeros((N, 2, K), np.float32), np.zeros((N, 128, O * P), np.float32)
    for t in range(2):
        low = np.argsort(np.concatenate([score(u[r], L[r]) for r in range(N)]), kind="stable")[:K]
        high = np.argsort(-np.concatenate([score(z[r], X[r]) for r in range(N)]), kind="stable")[:K]
        lw[:, t], sw[:, t] = low, high
        gone, come = pick(join(*L), low), pick(join(*X), high)
        v = decode(come) * np.float32(0.5) + decode(pick(noise, low)) * np.float32(0.5)
        new = mx_ref.quantize(np.ascontiguousarray(v.astype(BF)))
        for r in range(N):
            a, b = np.flatnonzero(low // P == r), np.flatnonzero(high // P == r)
            L[r] = put(L[r], low[a] - P * r, pick(new, a))
            X[r] = put(X[r], high[b] - P * r, pick(gone, b))
    for r in range(N):
        oc[r], osc[r] = emit(join(L[r], X[r]))
        for o in range(O):
            y[r, :, P * o:P * o + P] = mx_ref.matmul(mx_ref.quantize(np.ascontiguousarray(w[r][:, 512 * o:512 * o + 512])), L[r])
    return {"oc": oc, "osc": osc, "sw": sw, "lw": lw, "y": y}

@@ -1,0 +1,556 @@
+from concourse.bass import DstId, RemoteDMATransfer
+from concourse.mybir import dt, AluOpType, AxisListType, ActivationFunctionType as AF
+
+N, P, K = 8, 256, 64
+PEERS = N - 1
+HS = K // N
+
+SCRATCH, VIEW = {}, {}
+SEMAPHORES = ["qv", "qs", "qt", "qg", "ls", "ak1", "ak2", "ai1", "ai2", "azc", "azs", "ahc", "ahs", "awc", "aws", "anum"] + ["d%d" % i for i in range(48)]
+
+
+def _sb(name, w, d):
+    SCRATCH[name] = ("sbuf", [128, w], d)
+    VIEW[name] = (name, 0, w)
+
+
+def _codes(name, w):
+    _sb(name, w, "float8_e4m3fn_x4")
+    _sb(name + "s", w, "uint8")
+
+
+def _pool(name, d, parts):
+    at = 0
+    for n, w in parts:
+        VIEW[n] = (name, at, w)
+        at += (w + 15) // 16 * 16
+    SCRATCH[name] = ("sbuf", [128, at], d)
+
+
+for _n, _w in (("TL", 1024), ("TX", 1024), ("TN", 1024), ("TW", 512), ("U4", 4), ("Z4", 4), ("UT", 1024), ("ZT", 1024), ("ONE", 192),
+               ("ZB", 192), ("CO", 1536), ("WT", 2048), ("ET", 2048), ("EYE", 128), ("CTL", 1024), ("CTX", 1024), ("OT", 512), ("HT", 512)):
+    _sb(_n, _w, "bfloat16")
+_pool("BB", "bfloat16", (("EQK", 256), ("MM", 448), ("EQ", 512), ("EQN", 64)))
+_pool("FC", "float32", (("CC", 16), ("IROW", 64), ("N16", 128), ("M16", 128), ("CROW", 4), ("KC", 4), ("CW8", 8), ("HALF", 1), ("B28", 28),
+                        ("HB", 7), ("IC", 2), ("SGN", 32), ("DCOL", 1), ("BROW", 128), ("ROWI", 512)))
+_pool("FD", "float32", (("AC", 4), ("RLA", 256), ("RXA", 256), ("RML", 256), ("RMX", 256)))
+_pool("FB", "float32", (("PRD", 256), ("JK", 1088), ("PM", 128), ("P64", 64), ("P32", 32), ("P16", 16), ("P8", 8), ("K1S", 1), ("OKC", 2),
+                        ("KR", 224), ("KW", 224), ("XC", 2), ("XR", 64), ("Y", 64), ("TY", 64), ("G", 128), ("MU", 512), ("FLD", 8), ("FM", 4),
+                        ("FO", 8), ("FP", 8), ("VT", 128), ("VM", 128), ("VU", 128), ("PN", 64), ("NA", 2), ("NB", 2), ("V28", 28), ("V29", 28),
+                        ("W12", 12), ("W4", 8), ("W5", 4), ("AB", 8), ("V7", 7), ("V8", 8), ("VS", 1), ("VX", 1), ("HL8", 8)))
+for _n, _w in (("NUM", 2), ("NL", 14), ("RES", 4), ("YO", 256)):
+    _sb(_n, _w, "float32")
+for _t in "12":
+    for _n, _w in (("K1_", 1), ("KL", 7), ("ROW", 512), ("LST", 32)):
+        _sb(_n + _t, _w, "float32")
+    for _n, _w in (("INFO", 4), ("IL", 28)):
+        _sb(_n + _t, _w, "uint16")
+    _pool("UB" + _t, "uint16", tuple((_n + _t, _w) for _n, _w in (("PIU", 8), ("ZU", 4), ("NU", 4), ("LAB", 8), ("PLU", 32), ("HLU", 8))))
+    _codes("Z" + _t, K)
+    _codes("LXV" + _t, 2 * P + K + 128)
+    _codes("B" + _t, 128)
+    _codes("N" + _t, 128)
+_sb("PI", 1, "int32")
+_sb("II", 5, "int32")
+for _n, _w in (("UQ", 256), ("ZQ", 256), ("LX1", 512), ("LX2", 512), ("LX3", 512), ("NQ", 256), ("WQ", 128), ("COQ", 384), ("WTQ", 512), ("EC", 512),
+               ("CQL", 256), ("CQX", 256), ("OQ", 128), ("WIN1", PEERS * K + 2 * P), ("WIN2", K + 128 + 2 * P), ("HW", 96)):
+    _codes(_n, _w)
+PSUM = {"pA": 1, "pB": 1, "pC": 1, "pD": 4, "pE": 1}
+for _n in PSUM:
+    SCRATCH[_n] = ("psum", [128, 512 * PSUM[_n]], "float32")
+    VIEW[_n] = (_n, 0, 512 * PSUM[_n])
+
+ADD, SUB, MUL, MAX, MIN = AluOpType.add, AluOpType.subtract, AluOpType.mult, AluOpType.max, AluOpType.min
+GT, GE, LT, LE, EQL = AluOpType.is_gt, AluOpType.is_ge, AluOpType.is_lt, AluOpType.is_le, AluOpType.is_equal
+
+
+def R(name, c0=0, c1=None, p0=0, p1=128, step=1):
+    buf, at, width = VIEW[name]
+    return (buf, at + c0, at + (width if c1 is None else c1), p0, p1, step)
+
+
+def overlap(a, b):
+    if a[4] <= b[3] or b[4] <= a[3] or a[2] <= b[1] or b[2] <= a[1]:
+        return False
+    return not (a[5] == b[5] and a[5] > 1 and (a[1] - b[1]) % a[5])
+
+
+def covers(a, b):
+    return a[5] == 1 and a[1] <= b[1] and a[2] >= b[2] and a[3] <= b[3] and a[4] >= b[4]
+
+
+def bank(r):
+    return (r[0], r[1] // 512 * 512, (r[2] + 511) // 512 * 512, 0, 128, 1) if r[0] in PSUM else r
+
+
+def rank_program(g, core, T, topo):
+    rank = T.rank_of(core)
+    if rank is None:
+        return
+    peers = [r for r in range(N) if r != rank]
+    queues = {"v": g.vector, "s": g.scalar, "t": g.tensor, "g": g, "y": g.sync}
+    hist, known, count, total = {}, {q: {} for q in queues}, {q: 0 for q in queues}, {}
+    seq, ndma = [0], [0]
+
+    def waits(q, reads, writes, adds=False):
+        need = []
+        for r in reads:
+            b, ps = bank(r), r[0] in PSUM
+            for kind, box, tok in hist.get(r[0], []):
+                if overlap(b, box) and (kind == "w" or ps and tok[2] != q):
+                    need.append(tok)
+        for w in writes:
+            b = bank(w)
+            for kind, box, tok in hist.get(w[0], []):
+                if overlap(b, box) and not (adds and tok[2] == q):
+                    need.append(tok)
+        for tok in sorted(need, key=lambda k: -k[4]):
+            if known[q].get(tok[0], 0) < tok[1]:
+                queues[q].wait_ge(T.sem[tok[0]], tok[1])
+                known[q][tok[0]] = tok[1]
+                for s, n in tok[5].items():
+                    known[q][s] = max(known[q].get(s, 0), n)
+
+    def note(q, reads, writes, sem, val):
+        seq[0] += 1
+        tok = (sem, val, q, None, seq[0], dict(known[q]) if q in known else {})
+        for w in writes:
+            b = bank(w)
+            hist[w[0]] = [h for h in hist.get(w[0], []) if not covers(b, h[1])] + [("w", b, tok)]
+        for r in reads:
+            hist.setdefault(r[0], []).append(("r", bank(r), tok))
+
+    def run(q, make, reads, writes, adds=False):
+        waits(q, reads, writes, adds)
+        count[q] += 1
+        make().then_inc(T.sem["q" + q], 1)
+        total["q" + q] = count[q]
+        note(q, reads, writes, "q" + q, count[q])
+
+    def A(r):
+        t = T[r[0]]
+        rows = slice(None) if (r[3], r[4]) == (0, 128) else slice(r[3], r[4])
+        return t[rows, r[1]:r[2]] if r[5] == 1 else t[rows, r[1]:r[2]:r[5]]
+
+    def S8(r):
+        return A(r).bitcast(dt.uint8) if SCRATCH[r[0]][2] == "float8_e4m3fn_x4" else A(r)
+
+    def dma(q, out, in_, outap=None, inap=None):
+        reads, writes = [in_] if in_ else [], [out] if out else []
+        waits(q, reads, writes)
+        sem = "d%d" % ndma[0]
+        ndma[0] += 1
+        queues[q].dma_start(outap if outap is not None else S8(out), inap if inap is not None else S8(in_)).then_inc(T.sem[sem], 16)
+        total[sem] = 16
+        note(q, reads, writes, sem, 16)
+
+    def dmaq(q, out, c, in_, d, n):
+        dma(q, R(out, c, c + n), R(in_, d, d + n))
+        dma(q, R(out + "s", c, c + n), R(in_ + "s", d, d + n))
+
+    def memset(r, v):
+        run("v", lambda: g.vector.memset(A(r), v), [], [r])
+
+    def copy(q, out, in_):
+        if q == "v":
+            run("v", lambda: g.vector.tensor_copy(A(out), A(in_)), [in_], [out])
+        else:
+            run("s", lambda: g.scalar.activation(A(out), A(in_), AF.Copy), [in_], [out])
+
+    def tt(out, a, b, op):
+        run("v", lambda: g.vector.tensor_tensor(A(out), A(a), A(b), op), [a, b], [out])
+
+    def ts(out, a, s1, op0, s2=None, op1=None):
+        reads = [a] + [s for s in (s1, s2) if isinstance(s, tuple)]
+        v1 = A(s1) if isinstance(s1, tuple) else s1
+        v2 = A(s2) if isinstance(s2, tuple) else s2
+        if op1 is None:
+            run("v", lambda: g.vector.tensor_scalar(A(out), A(a), v1, None, op0), reads, [out])
+        else:
+            run("v", lambda: g.vector.tensor_scalar(A(out), A(a), v1, v2, op0, op1), reads, [out])
+
+    def act(out, in_, f, bias=None, scale=None, acc=None):
+        kw = {}
+        if bias is not None:
+            kw["bias"] = A(bias)
+        if scale is not None:
+            kw["scale"] = A(scale)
+        if acc is not None:
+            kw["accum_out"] = A(acc)
+        run("s", lambda: g.scalar.activation(A(out), A(in_), f, **kw), [in_] + [x for x in (bias, scale) if x is not None],
+            [out] + ([acc] if acc is not None else []))
+
+    def turn(out, in_):
+        run("v", lambda: g.vector.transpose(A(out), A(in_)), [in_], [out])
+
+    def total_of(out, in_):
+        run("v", lambda: g.vector.tensor_reduce(A(out), A(in_), AxisListType.X, ADD), [in_], [out])
+
+    def quant(out, c, n, tile, e):
+        o, s, i = R(out, c, c + n), R(out + "s", c, c + n), R(tile, 4 * e, 4 * e + 4 * n)
+        run("v", lambda: g.vector.quantize_mx(A(o), A(s), A(i)), [i], [o, s])
+
+    def mm(ps, b, w, c, x, d, n, start=True, stop=True):
+        o = R(ps, 512 * b, 512 * b + n)
+        l, ls, r, rs = R(w, c, c + 128), R(w + "s", c, c + 128), R(x, d, d + n), R(x + "s", d, d + n)
+        run("t", lambda: g.tensor.matmul_mx(A(o), A(l), A(ls), A(r), A(rs), start, stop), [l, ls, r, rs], [o], not start)
+
+    def pick(out, c, win, width, lst, e, f):
+        n = 16 * (f - e)
+        o, os_, i, is_, l = R(out, c, c + n), R(out + "s", c, c + n), R(win, 0, width), R(win + "s", 0, width), R(lst, e, f)
+        run("v", lambda: g.vector.tensor_copy(A(o).bitcast(dt.uint32), A(i).bitcast(dt.uint32).indirect(A(l))), [i, l], [o])
+        run("s", lambda: g.scalar.activation(A(os_), A(is_).indirect(A(l)), AF.Copy), [is_, l], [os_])
+
+    def iota(out, pattern, base, cm):
+        if SCRATCH[out[0]][2] == "int32":
+            run("g", lambda: g.iota(A(out), pattern, base, cm), [], [out])
+        else:
+            run("g", lambda: g.iota(A(out), pattern, base, cm, allow_small_or_imprecise_dtypes=True), [], [out])
+
+    def bits(es):
+        return sum(1 << e for e in es)
+
+    def dst(r):
+        a = topo.addr(T.cores[r])
+        return DstId(rid=a[0], pnc=a[1])
+
+    shared = [e for e in topo.engines(core, T.cores[peers[0]]) if all(e in topo.engines(core, T.cores[r]) for r in peers)]
+    whole = 1
+    while 2 * whole <= len(shared):
+        whole *= 2
+    part = 1
+    while 2 * part * PEERS <= len(shared):
+        part *= 2
+
+    def slot_at(r):
+        return rank if rank < r else rank - 1
+
+    def to_all(src, place, sem):
+        waits("g", [src], [])
+        t = RemoteDMATransfer(dst_ids=[dst(r) for r in peers], dma_engine_mask=bits(shared[:whole]), remote_sem=T.sem[sem],
+                              srcs=[S8(src)], dsts=[S8(place(r)) for r in peers], alu_op=0)
+        g.remote_dma_fused([t], local_sem=T.sem.ls)
+        total["ls"] = total.get("ls", 0) + whole
+
+    def to_each(src, place, sem):
+        waits("g", [src(r) for r in peers], [])
+        calls = []
+        for i, r in enumerate(peers):
+            calls.append(RemoteDMATransfer(dst_ids=[dst(r)], dma_engine_mask=bits(shared[part * i:part * i + part]), remote_sem=T.sem[sem],
+                                           srcs=[S8(src(r))], dsts=[S8(place(r))], alu_op=0))
+        g.remote_dma_fused(calls, local_sem=T.sem.ls)
+        total["ls"] = total.get("ls", 0) + part * PEERS
+
+    def arrives(regions, sem, per):
+        total[sem] = PEERS * per
+        note("remote", [], regions, sem, PEERS * per)
+
+    dma("y", R("U4"), None, inap=T.u[:, 0:4])
+    dma("s", R("Z4"), None, inap=T.z[:, 0:4])
+    dma("y", R("TX"), None, inap=T.dm[:, :])
+    dma("s", R("TL"), None, inap=T.lv[:, :])
+    dma("y", R("TN"), None, inap=T.nz[:, :])
+    dma("s", R("TW"), None, inap=T.w[:, :])
+    iota(R("PI"), [[0, 1]], 0, 1)
+    memset(R("ONE"), 1.0)
+    memset(R("ZB"), 0.0)
+    memset(R("EYE"), 0.5)
+    run("g", lambda: g.affine_select(A(R("EYE")), A(R("EYE")), [[-1, 128]], EQL, 0.0, 0, 1), [R("EYE")], [R("EYE")])
+    iota(R("IROW"), [[1, 64]], 0, 0)
+    iota(R("N16"), [[0, 8], [1, 16]], 0, 0)
+    iota(R("CROW"), [[16, 4]], 0, 0)
+    iota(R("B28"), [[K, PEERS], [16, 4]], 0, 0)
+    iota(R("HB"), [[HS, PEERS]], 33, 0)
+    iota(R("ROWI"), [[256, 2], [1, 16], [16, 16]], 1, 0)
+    memset(R("UT", 768, 1024), 0.0)
+    memset(R("ZT", 0, 256), 0.0)
+    for c0, c1, v in ((0, 256, 1.0), (256, 768, 0.0), (768, 1536, 1.0)):
+        memset(R("CO", c0, c1), v)
+    for i, (op, v) in enumerate(((AluOpType.bitwise_and, 15), (AluOpType.arith_shift_right, 4), (AluOpType.bitwise_and, 63),
+                                 (AluOpType.bitwise_and, 31), (AluOpType.bitwise_and, 7))):
+        ts(R("II", i, i + 1), R("PI"), v, op)
+    copy("v", R("CC", 0, 5), R("II"))
+    Q16, TGT = R("CC", 0, 1), R("CC", 2, 3)
+    memset(R("SGN", p1=64), 1.0)
+    memset(R("SGN", p0=64), -1.0)
+    memset(R("CTL", 3, 1024, step=4), 0.0)
+    memset(R("CTX", 3, 1024, step=4), 0.0)
+    quant("COQ", 0, 384, "CO", 0)
+    for t in range(4):
+        ts(R("UT", t, 768, step=4), R("ONE"), R("U4", t, t + 1), MUL)
+        act(R("ZT", 256 + t, 1024, step=4), R("ZB"), AF.Identity, bias=R("Z4", t, t + 1))
+    quant("ZQ", 0, 256, "ZT", 0)
+    quant("UQ", 0, 256, "UT", 0)
+    memset(R("ET"), 0.0)
+    memset(R("HT", 256, 512), 0.0)
+    for b in range(4):
+        copy("s", R("ET", 512 * b + b, 512 * b + 512, step=4), R("EYE"))
+    quant("LX1", P, P, "TX", 0)
+    quant("LX1", 0, P, "TL", 0)
+    dmaq("y", "WIN1", PEERS * K, "LX1", 0, 2 * P)
+    dmaq("y", "LXV1", 0, "LX1", 0, 2 * P)
+    for w in ("N1", "B1", "N2", "B2"):
+        dmaq("y", w, K, "LX1", 0, K)
+
+    def local(t):
+        lx, k1 = "LX%d" % t, "K1_%d" % t
+        for typ in "XL":
+            c0, bk, row = (P, 2, "pB") if typ == "X" else (0, 0, "pA")
+            q, qc = ("ZQ", 64) if typ == "X" else ("UQ", 0)
+            for h in range(2):
+                mm("pD", bk + h, lx, c0 + 128 * h, q, qc, 128)
+            mm(row, 0, q, qc, lx, c0, P)
+            act(R("R%sA" % typ), R(row, 0, P), AF.Abs)
+            for h in range(2):
+                act(R("AC", bk + h, bk + h + 1), R("pD", 512 * (bk + h), 512 * (bk + h) + 1), AF.Abs)
+        mm("pC", 0, "UQ", 128, lx, 0, P, True, False)
+        mm("pC", 0, "ZQ", 0, lx, P, P, False, True)
+        for typ in "XL":
+            ra, rm = R("R%sA" % typ), R("RM%s" % typ)
+            run("g", lambda: g.affine_select(A(rm), A(ra), [[0, 2], [1, 128]], GT, -1.0, 0, -1), [ra], [rm])
+        for typ in "XL":
+            bk = 2 if typ == "X" else 0
+            lo, le = (LT, LE) if typ == "X" else (GT, GE)
+            row, rm, ct = "R%sA" % typ, "RM%s" % typ, "CT" + typ
+            a = [R("AC", bk + h, bk + h + 1) for h in range(2)]
+            ts(R(ct, 0, 512, step=4), R(row, 0, 128), a[0], lo)
+            ts(R(ct, 512, 1024, step=4), R(row, 128, 256), a[0], le)
+            ts(R(ct, 1, 1024, step=4), R(row), a[1], lo)
+            ts(R(ct, 2, 512, step=4), R(rm, 0, 128), a[0], EQL)
+            ts(R(ct, 514, 1024, step=4), R(rm, 128, 256), a[1], EQL)
+            quant("CQ" + typ, 0, P, ct, 0)
+        mm("pE", 0, "COQ", 128, "CQX", 0, P, True, False)
+        mm("pE", 0, "COQ", 0, "CQL", 0, P, False, True)
+        ts(R("EQK"), R("pE", 0, P), TGT, EQL)
+        tt(R("PRD"), R("EQK"), R("pC", 0, P), MUL)
+        act(R("JK", 0, P), R("PRD"), AF.Abs, acc=R(k1))
+        to_all(R(k1), lambda r: R("KL%d" % t, slot_at(r), slot_at(r) + 1), "ak%d" % t)
+
+    def constants():
+        memset(R("WT", 0, 512), 256.0)
+        memset(R("WT", 1024, 1536), 256.0)
+        memset(R("WT", 512, 1024), 0.0)
+        memset(R("WT", 1536, 2048), 0.0)
+        ts(R("CC", 5, 6), R("CC", 0, 1), 1.0, ADD)
+        ts(R("CC", 6, 7), R("CC", 1, 2), 16.0, MUL)
+        ts(R("CC", 7, 8), R("CC", 1, 2), 16.0, MUL, 128.0, ADD)
+        ts(R("CC", 8, 9), R("CC", 0, 1), 16.0, MUL)
+        ts(R("CC", 9, 10), R("CC", 1, 2), 8.0, ADD)
+        for m, b, c in ((0, 0, 5), (0, 1, 5), (1, 0, 6), (1, 1, 7), (2, 0, 8), (2, 1, 8), (3, 0, 1), (3, 1, 9)):
+            act(R("WT", 512 * m + b, 512 * m + 512, step=4), R("ZB", 0, 128), AF.Identity, bias=R("CC", c, c + 1))
+        memset(R("OT", 2, 256, step=4), 0.0)
+        memset(R("OT", 3, 256, step=4), 0.0)
+        ts(R("M16"), R("N16"), Q16, EQL)
+        ts(R("KC"), R("CROW"), Q16, ADD)
+        for p in (0, 64):
+            copy("v", R("IC", 0, 1, p, p + 32), R("CC", 3, 4, p, p + 32))
+            ts(R("IC", 1, 2, p, p + 32), R("CC", 3, 4, p, p + 32), 32.0, ADD)
+            memset(R("IC", 0, 2, p + 32, p + 64), 0.0)
+
+    def constants2():
+        quant("NQ", 0, P, "TN", 0)
+        quant("EC", 0, 512, "ET", 0)
+        memset(R("DCOL", p1=64), float(P * rank - 1))
+        memset(R("DCOL", p0=64), float(P * rank - 1 - P))
+        memset(R("BROW", 0, 64), float(2 * P + K + 1))
+        memset(R("BROW", 64, 128), float(2 * P + 1))
+        ts(R("B28"), R("B28"), Q16, ADD)
+        ts(R("HB"), R("HB"), R("CC", 4, 5), ADD)
+        copy("s", R("ROW1"), R("ROWI"))
+        copy("s", R("ROW2"), R("ROWI"))
+
+    def constants3():
+        ch = rank // 2
+        ts(R("HALF"), Q16, 8.0, GE if rank % 2 else LT, float(64 + 16 * rank - 16 * ch), MUL)
+        copy("v", R("CW8", 0, 4), R("KC"))
+        copy("v", R("CW8", 4, 8), R("KC"))
+        for c in (ch, 4 + ch):
+            tt(R("CW8", c, c + 1), R("KC", ch, ch + 1), R("HALF"), ADD)
+        quant("WQ", 0, 128, "TW", 0)
+
+    def post(t):
+        for typ in "XL":
+            bk = 2 if typ == "X" else 0
+            for h in range(2):
+                mm("pD", bk + h, "CQ" + typ, 128 * h, "COQ", 256, 128)
+        tt(R("K1S"), R("K1_%d" % t), R("SGN", 0, 1), MUL)
+        for c, s, d in ((0, 0, 0), (0, 0, 32), (0, 64, 64), (0, 64, 96), (1, 32, 0), (1, 32, 32), (1, 96, 64), (1, 96, 96)):
+            copy("s", R("OKC", c, c + 1, d, d + 32), R("K1S", 0, 1, s, s + 32))
+        for h in range(2):
+            pl, px = R("pD", 512 * h, 512 * h + 1), R("pD", 512 * (2 + h), 512 * (2 + h) + 1)
+            ts(R("OT", 256 + h, 512, step=4), R("IROW"), px, EQL)
+            ts(R("OT", 256 + 2 + h, 512, step=4), R("IROW"), px, EQL)
+            ts(R("OT", h, 256, step=4), R("IROW"), pl, EQL)
+        if t == 1:
+            quant("WTQ", 0, 512, "WT", 0)
+        quant("OQ", 0, 128, "OT", 0)
+        for ps, m in (("pA", 0), ("pB", 2)):
+            mm(ps, 0, "WTQ", 128 * m, "OQ", 0, 128, True, False)
+            mm(ps, 0, "WTQ", 128 * m + 128, "OQ", 0, 128, False, True)
+        tt(R("PM"), R("M16"), R("pB", 0, 128), MUL)
+        tt(R("P64"), R("PM", 0, 128, step=2), R("PM", 1, 128, step=2), ADD)
+        tt(R("P32"), R("P64", 0, 64, step=2), R("P64", 1, 64, step=2), ADD)
+        tt(R("P16"), R("P32", 0, 32, step=2), R("P32", 1, 32, step=2), ADD)
+        tt(R("P8"), R("P16", 0, 16, step=2), R("P16", 1, 16, step=2), ADD)
+        ts(R("PIU%d" % t), R("P8"), 0.0, ADD)
+
+    def merge(t):
+        kl = "KL%d" % t
+        arrives([R(kl)], "ak%d" % t, whole)
+        for s in range(PEERS):
+            o, kc = R("KR", 32 * s, 32 * s + 32), R(kl, s, s + 1)
+            if s % 2:
+                act(o, R("SGN"), AF.Copy, scale=kc)
+            else:
+                ts(o, R("SGN"), kc, MUL)
+        turn(R("KW"), R("KR"))
+        for m in range(2):
+            own = R("OKC", m, m + 1)
+            if rank:
+                ts(R("MM", 224 * m, 224 * m + 32 * rank), R("KW", 0, 32 * rank), own, LE)
+            if rank < PEERS:
+                ts(R("MM", 224 * m + 32 * rank, 224 * m + 224), R("KW", 32 * rank, 224), own, LT)
+            act(R("JK", 256 + 224 * m, 480 + 224 * m), R("MM", 224 * m, 224 * m + 224), AF.Copy, acc=R("XC", m, m + 1))
+        for m in range(2):
+            ts(R("XR", 32 * m, 32 * m + 32), R("ONE", 0, 32), R("XC", m, m + 1), MUL, R("IC", m, m + 1), ADD)
+        turn(R("Y"), R("XR"))
+        copy("s", R("TY", p0=32, p1=64), R("Y", p0=0, p1=32))
+        copy("v", R("TY", p0=0, p1=32), R("Y", p0=32, p1=64))
+        copy("s", R("TY", p0=96, p1=128), R("Y", p0=64, p1=96))
+        copy("v", R("TY", p0=64, p1=96), R("Y", p0=96, p1=128))
+        tt(R("G", 0, 64, 0, 64), R("Y", p1=64), R("TY", p1=64), ADD)
+        tt(R("G", 64, 128, 64, 128), R("Y", p0=64), R("TY", p0=64), ADD)
+        copy("s", R("G", 0, 64, 64, 128), R("G", 0, 64, 0, 64))
+        copy("v", R("G", 64, 128, 0, 64), R("G", 64, 128, 64, 128))
+        for c in range(4):
+            e, u = R("EQ", 128 * c, 128 * c + 128), R("MU", 128 * c, 128 * c + 128)
+            ts(e, R("G"), R("KC", c, c + 1), EQL)
+            tt(u, e, R("pA", 0, 128), MUL)
+            for k in range(2):
+                j = 64 * (2 * c + k)
+                act(R("JK", 512 + j, 576 + j), R("MU", j, j + 64), AF.Copy, acc=R("FLD", 4 * k + c, 4 * k + c + 1))
+        tt(R("FM"), R("FLD", 0, 4), R("FLD", 4, 8), MAX)
+        ts(R("ZU%d" % t), R("FM"), -1.0, ADD)
+        ts(R("INFO%d" % t), R("FM"), 0.0, ADD)
+        pick("Z%d" % t, 0, "LX%d" % t, 2 * P, "ZU%d" % t, 0, 4)
+        to_all(R("INFO%d" % t), lambda r: R("IL%d" % t, 4 * slot_at(r), 4 * slot_at(r) + 4), "ai%d" % t)
+
+    def lists(t, base):
+        ts(R("NU%d" % t), R("FLD", 0, 4), -1.0, ADD)
+        pick("N%d" % t, 0, "NQ", P, "NU%d" % t, 0, 4)
+        for b in range(4):
+            mm("pD", b, "EC", 128 * b, "N%d" % t, 0, 128, True, False)
+        ts(R("FP"), R("FLD"), 0.0, GT, float(base - 1), MUL)
+        tt(R("FO"), R("FP"), R("FLD"), ADD)
+        tt(R("VT"), R("G"), R("BROW"), ADD)
+        ts(R("VM"), R("G"), float(K), LT)
+        tt(R("VU"), R("VT"), R("pA", 0, 128), SUB)
+        tt(R("VT"), R("VU"), R("VM"), MUL)
+        tt(R("VU"), R("VT"), R("pA", 0, 128), ADD)
+        row, off = R("ROW%d" % t), R("PIU%d" % t)
+        run("v", lambda: g.vector.tensor_copy(A(row).indirect(A(off)), A(R("VU"))), [R("VU"), off], [row])
+        for k in range(2):
+            dma("y", R("LST%d" % t, 16 * k, 16 * k + 16), R("ROW%d" % t, 256 * k, 256 * k + 256, 0, 8))
+
+    def numbers(t):
+        for k in range(2):
+            p = 64 * k
+            ts(R("EQN", 0, 64, p, p + 64), R("G", p, p + 64, p, p + 64), R("CC", 2, 3, p, p + 64), EQL)
+            tt(R("PN", 0, 64, p, p + 64), R("EQN", 0, 64, p, p + 64), R("pA", p, p + 64, p, p + 64), MUL)
+        act(R("JK", 1024, 1088), R("PN"), AF.Copy, acc=R("NA", t - 1, t))
+        ts(R("NB", t - 1, t), R("NA", t - 1, t), 0.0, GT, R("DCOL"), MUL)
+        tt(R("NUM", t - 1, t), R("NB", t - 1, t), R("NA", t - 1, t), ADD)
+
+    def renew(t, width):
+        win, lxv, nxt, lab = "WIN%d" % t, "LXV%d" % t, "LX%d" % (t + 1), "LAB%d" % t
+        pick("B%d" % t, 0, win, width, lab, 4, 8)
+        for b in range(4):
+            mm("pD", b, "EC", 128 * b, "B%d" % t, 0, 128, False, True)
+        pick(lxv, 2 * P, win, width, lab, 0, 4)
+        ts(R("PLU%d" % t), R("LST%d" % t), -1.0, ADD)
+        pick(nxt, P, lxv, 2 * P + K, "PLU%d" % t, 16, 32)
+        for b in range(4):
+            copy("sv"[b % 2], R("HT", b, 256, step=4), R("pD", 512 * b, 512 * b + 64))
+        quant(lxv, 2 * P + K, 128, "HT", 0)
+        pick(nxt, 0, lxv, 2 * P + K + 128, "PLU%d" % t, 0, 16)
+
+    local(1)
+    constants()
+    post(1)
+    merge(1)
+    to_all(R("Z1"), lambda r: R("WIN1", K * slot_at(r), K * slot_at(r) + K), "azc")
+    to_all(R("Z1s"), lambda r: R("WIN1s", K * slot_at(r), K * slot_at(r) + K), "azs")
+    constants2()
+    lists(1, PEERS * K)
+    arrives([R("IL1")], "ai1", whole)
+    ts(R("V28"), R("IL1"), 0.0, GT)
+    tt(R("V29"), R("V28"), R("B28"), MUL)
+    tt(R("W12"), R("V29", 0, 12), R("V29", 12, 24), MAX)
+    tt(R("W4", 0, 4), R("W12", 0, 4), R("W12", 4, 8), MAX)
+    tt(R("W4", 4, 8), R("W12", 8, 12), R("V29", 24, 28), MAX)
+    tt(R("W5"), R("W4", 0, 4), R("W4", 4, 8), MAX)
+    for k in (1, 0):
+        tt(R("AB", 4 * k, 4 * k + 4), R("FO", 4 * k, 4 * k + 4), R("W5"), MAX)
+    ts(R("LAB1"), R("AB"), 0.0, ADD)
+    numbers(1)
+    constants3()
+    arrives([R("WIN1", 0, PEERS * K)], "azc", whole)
+    arrives([R("WIN1s", 0, PEERS * K)], "azs", whole)
+    renew(1, PEERS * K + 2 * P)
+
+    local(2)
+    dmaq("y", "WIN2", K + 128, "LX2", 0, 2 * P)
+    dmaq("y", "LXV2", 0, "LX2", 0, 2 * P)
+    post(2)
+    merge(2)
+    for s, sem in (("", "ahc"), ("s", "ahs")):
+        to_each(lambda r: R("Z2" + s, HS * r, HS * r + HS), lambda r: R("HW" + s, 32 + HS * slot_at(r), 32 + HS * slot_at(r) + HS), sem)
+    ch, ce = rank // 2, rank // 2 // 2 * 2
+    pick("HW", 0, "LX2", 2 * P, "ZU2", ce, ce + 2)
+    ts(R("VX"), Q16, float(16 * (ch - ce) + 1), ADD)
+    ts(R("V8", rank, rank + 1), R("FM", ch, ch + 1), 0.0, GT, R("VX"), MUL)
+    lists(2, K + 128)
+    tt(R("AB"), R("FO"), R("CW8"), MAX)
+    ts(R("LAB2"), R("AB"), 0.0, ADD)
+    arrives([R("IL2")], "ai2", whole)
+    ts(R("V7"), R("IL2", ch, 28, step=4), 0.0, GT)
+    if rank:
+        tt(R("V8", 0, rank), R("V7", 0, rank), R("HB", 0, rank), MUL)
+    if rank < PEERS:
+        tt(R("V8", rank + 1, 8), R("V7", rank, 7), R("HB", rank, 7), MUL)
+    total_of(R("VS"), R("V8"))
+    ts(R("HL8"), R("V8"), -1.0, MUL, R("VS"), ADD)
+    ts(R("HLU2"), R("HL8"), 88.0, MIN, -1.0, ADD)
+    arrives([R("HW", 32, 88)], "ahc", part)
+    arrives([R("HWs", 32, 88)], "ahs", part)
+    pick("WIN2", K, "HW", 88, "HLU2", 0, 8)
+    hc = K + HS * (rank % 2)
+    for s, sem in (("", "awc"), ("s", "aws")):
+        to_each(lambda r: R("WIN2" + s, hc + 16 * r, hc + 16 * r + HS), lambda r: R("WIN2" + s, HS * rank, HS * rank + HS), sem)
+    numbers(2)
+    to_all(R("NUM"), lambda r: R("NL", 2 * slot_at(r), 2 * slot_at(r) + 2), "anum")
+    for s, sem in (("", "awc"), ("s", "aws")):
+        arrives([R("WIN2" + s, a, b) for a, b in ((0, HS * rank), (HS * rank + HS, K)) if a < b], sem, part)
+    renew(2, K + 128 + 2 * P)
+
+    arrives([R("NL")], "anum", whole)
+    dma("y", None, R("LX3", P, 2 * P), outap=T.oc[:, 4 * P:8 * P])
+    for k in range(4):
+        dma("y", None, R("LX3s", P, 2 * P, 32 * k, 32 * k + 4), outap=T.osc[4 * k:4 * k + 4, P:2 * P])
+    for h in range(2):
+        mm("pD", h, "WQ", 0, "LX3", 128 * h, 128)
+    dma("y", None, R("LX3", 0, P), outap=T.oc[:, 0:4 * P])
+    for k in range(4):
+        dma("y", None, R("LX3s", 0, P, 32 * k, 32 * k + 4), outap=T.osc[4 * k:4 * k + 4, 0:P])
+    for h in range(2):
+        copy("sv"[h], R("YO", 128 * h, 128 * h + 128), R("pD", 512 * h, 512 * h + 128))
+    dma("s", None, R("YO"), outap=T.y[:, :])
+    for t in range(2):
+        total_of(R("RES", t, t + 1), R("NL", t, 14, step=2))
+    tt(R("RES", 2, 4), R("RES", 0, 2), R("NUM"), ADD)
+    for t in range(2):
+        dma("s", None, R("RES", 2 + t, 3 + t, 0, 64), outap=T.lw[t:t + 1, :])
+        dma("s", None, R("RES", 2 + t, 3 + t, 64, 128), outap=T.sw[t:t + 1, :])
+    for sem in total:
+        if known["g"].get(sem, 0) < total[sem]:
+            g.wait_ge(T.sem[sem], total[sem])

@@ -28,16 +28,17 @@ def _pool(name, d, parts):
 
 
 for _n, _w in (("TL", 1024), ("TX", 1024), ("TN", 1024), ("TW", 512), ("U4", 4), ("Z4", 4), ("UT", 1024), ("ZT", 1024), ("ONE", 192),
-               ("ZB", 192), ("CO", 1536), ("WT", 2048), ("ET", 2048), ("EYE", 128), ("CTL", 1024), ("CTX", 1024), ("OT", 512), ("HT", 512)):
+               ("ZB", 512), ("CO", 1536), ("WT", 2048), ("ET", 2048), ("EYE", 128), ("CTL", 1024), ("CTX", 1024), ("OT", 512), ("HT", 512),
+               ("MSK", 256), ("DS", 512)):
     _sb(_n, _w, "bfloat16")
 _pool("BB", "bfloat16", (("EQK", 256), ("MM", 448), ("EQ", 512), ("EQN", 64)))
 _pool("FC", "float32", (("CC", 16), ("IROW", 64), ("N16", 128), ("M16", 128), ("CROW", 4), ("KC", 4), ("CW8", 8), ("HALF", 1), ("B28", 28),
-                        ("HB", 7), ("IC", 2), ("SGN", 32), ("DCOL", 1), ("BROW", 128), ("ROWI", 512)))
-_pool("FD", "float32", (("AC", 4), ("RLA", 256), ("RXA", 256), ("RML", 256), ("RMX", 256)))
+                        ("WC", 1), ("VX", 1), ("IC", 2), ("SGN", 32), ("DCOL", 1), ("BROW", 128), ("ROWI", 512)))
+_pool("FD", "float32", (("AC", 4), ("RLA", 256), ("RXA", 256)))
 _pool("FB", "float32", (("PRD", 256), ("JK", 1088), ("PM", 128), ("P64", 64), ("P32", 32), ("P16", 16), ("P8", 8), ("K1S", 1), ("OKC", 2),
                         ("KR", 224), ("KW", 224), ("XC", 2), ("XR", 64), ("Y", 64), ("TY", 64), ("G", 128), ("MU", 512), ("FLD", 8), ("FM", 4),
                         ("FO", 8), ("FP", 8), ("VT", 128), ("VM", 128), ("VU", 128), ("PN", 64), ("NA", 2), ("NB", 2), ("V28", 28), ("V29", 28),
-                        ("W12", 12), ("W4", 8), ("W5", 4), ("AB", 8), ("V7", 7), ("V8", 8), ("VS", 1), ("VX", 1), ("HL8", 8)))
+                        ("W12", 12), ("W4", 8), ("W5", 4), ("AB", 8), ("V8", 8), ("VS", 1), ("HL8", 8)))
 for _n, _w in (("NUM", 2), ("NL", 14), ("RES", 4), ("YO", 256)):
     _sb(_n, _w, "float32")
 for _t in "12":
@@ -53,7 +54,7 @@ for _t in "12":
 _sb("PI", 1, "int32")
 _sb("II", 5, "int32")
 for _n, _w in (("UQ", 256), ("ZQ", 256), ("LX1", 512), ("LX2", 512), ("LX3", 512), ("NQ", 256), ("WQ", 128), ("COQ", 384), ("WTQ", 512), ("EC", 512),
-               ("CQL", 256), ("CQX", 256), ("OQ", 128), ("WIN1", PEERS * K + 2 * P), ("WIN2", K + 128 + 2 * P), ("HW", 96)):
+               ("CQL", 256), ("CQX", 256), ("OQ", 128), ("WIN1", PEERS * K + 2 * P), ("WIN2", K + 128 + 2 * P), ("HW", 32 + K)):
     _codes(_n, _w)
 PSUM = {"pA": 1, "pB": 1, "pC": 1, "pD": 4, "pE": 1}
 for _n in PSUM:
@@ -174,10 +175,10 @@ def rank_program(g, core, T, topo):
         if bias is not None:
             kw["bias"] = A(bias)
         if scale is not None:
-            kw["scale"] = A(scale)
+            kw["scale"] = A(scale) if isinstance(scale, tuple) else scale
         if acc is not None:
             kw["accum_out"] = A(acc)
-        run("s", lambda: g.scalar.activation(A(out), A(in_), f, **kw), [in_] + [x for x in (bias, scale) if x is not None],
+        run("s", lambda: g.scalar.activation(A(out), A(in_), f, **kw), [in_] + [x for x in (bias, scale) if isinstance(x, tuple)],
             [out] + ([acc] if acc is not None else []))
 
     def turn(out, in_):
@@ -206,6 +207,9 @@ def rank_program(g, core, T, topo):
             run("g", lambda: g.iota(A(out), pattern, base, cm), [], [out])
         else:
             run("g", lambda: g.iota(A(out), pattern, base, cm, allow_small_or_imprecise_dtypes=True), [], [out])
+
+    def choose(r, pattern, op, fill, cm):
+        run("g", lambda: g.affine_select(A(r), A(r), pattern, op, fill, 0, cm), [r], [r])
 
     def bits(es):
         return sum(1 << e for e in es)
@@ -249,118 +253,109 @@ def rank_program(g, core, T, topo):
     dma("s", R("Z4"), None, inap=T.z[:, 0:4])
     dma("y", R("TX"), None, inap=T.dm[:, :])
     dma("s", R("TL"), None, inap=T.lv[:, :])
-    dma("y", R("TN"), None, inap=T.nz[:, :])
-    dma("s", R("TW"), None, inap=T.w[:, :])
     iota(R("PI"), [[0, 1]], 0, 1)
-    memset(R("ONE"), 1.0)
     memset(R("ZB"), 0.0)
     memset(R("EYE"), 0.5)
-    run("g", lambda: g.affine_select(A(R("EYE")), A(R("EYE")), [[-1, 128]], EQL, 0.0, 0, 1), [R("EYE")], [R("EYE")])
+    memset(R("MSK", 0, 128), 0.5)
+    memset(R("MSK", 128, 256), -0.5)
+    choose(R("EYE"), [[-1, 128]], EQL, 0.0, 1)
+    choose(R("MSK", 0, 128), [[1, 128]], GT, -0.5, -1)
+    choose(R("MSK", 128, 256), [[1, 128]], GT, 0.5, -1)
     iota(R("IROW"), [[1, 64]], 0, 0)
     iota(R("N16"), [[0, 8], [1, 16]], 0, 0)
     iota(R("CROW"), [[16, 4]], 0, 0)
     iota(R("B28"), [[K, PEERS], [16, 4]], 0, 0)
-    iota(R("HB"), [[HS, PEERS]], 33, 0)
     iota(R("ROWI"), [[256, 2], [1, 16], [16, 16]], 1, 0)
-    memset(R("UT", 768, 1024), 0.0)
-    memset(R("ZT", 0, 256), 0.0)
+    memset(R("ONE"), 1.0)
     for c0, c1, v in ((0, 256, 1.0), (256, 768, 0.0), (768, 1536, 1.0)):
         memset(R("CO", c0, c1), v)
+    memset(R("UT", 768, 1024), 0.0)
+    memset(R("ZT", 0, 256), 0.0)
     for i, (op, v) in enumerate(((AluOpType.bitwise_and, 15), (AluOpType.arith_shift_right, 4), (AluOpType.bitwise_and, 63),
                                  (AluOpType.bitwise_and, 31), (AluOpType.bitwise_and, 7))):
         ts(R("II", i, i + 1), R("PI"), v, op)
+    quant("COQ", 0, 384, "CO", 0)
     copy("v", R("CC", 0, 5), R("II"))
     Q16, TGT = R("CC", 0, 1), R("CC", 2, 3)
-    memset(R("SGN", p1=64), 1.0)
-    memset(R("SGN", p0=64), -1.0)
-    memset(R("CTL", 3, 1024, step=4), 0.0)
-    memset(R("CTX", 3, 1024, step=4), 0.0)
-    quant("COQ", 0, 384, "CO", 0)
+    for b in range(4):
+        copy("s", R("ET", 512 * b, 512 * b + 512), R("ZB"))
+    for ct in ("CTL", "CTX"):
+        memset(R(ct, 2, 1024, step=4), 0.0)
+        memset(R(ct, 3, 1024, step=4), 0.0)
+    for m in range(4):
+        memset(R("WT", 512 * m, 512 * m + 512), 0.0 if m % 2 else 256.0)
+    ts(R("CC", 5, 6), R("CC", 0, 1), 1.0, ADD)
+    ts(R("CC", 6, 7), R("CC", 1, 2), 16.0, MUL)
+    ts(R("CC", 7, 8), R("CC", 1, 2), 16.0, MUL, 128.0, ADD)
+    ts(R("CC", 8, 9), R("CC", 0, 1), 16.0, MUL)
+    ts(R("CC", 9, 10), R("CC", 1, 2), 8.0, ADD)
     for t in range(4):
         ts(R("UT", t, 768, step=4), R("ONE"), R("U4", t, t + 1), MUL)
-        act(R("ZT", 256 + t, 1024, step=4), R("ZB"), AF.Identity, bias=R("Z4", t, t + 1))
-    quant("ZQ", 0, 256, "ZT", 0)
+        act(R("ZT", 256 + t, 1024, step=4), R("ZB", 0, 192), AF.Identity, bias=R("Z4", t, t + 1))
     quant("UQ", 0, 256, "UT", 0)
-    memset(R("ET"), 0.0)
-    memset(R("HT", 256, 512), 0.0)
-    for b in range(4):
-        copy("s", R("ET", 512 * b + b, 512 * b + 512, step=4), R("EYE"))
+    quant("ZQ", 0, 256, "ZT", 0)
     quant("LX1", P, P, "TX", 0)
     quant("LX1", 0, P, "TL", 0)
     dmaq("y", "WIN1", PEERS * K, "LX1", 0, 2 * P)
-    dmaq("y", "LXV1", 0, "LX1", 0, 2 * P)
-    for w in ("N1", "B1", "N2", "B2"):
+    dma("y", R("TN"), None, inap=T.nz[:, :])
+    for w in ("N1", "B1"):
         dmaq("y", w, K, "LX1", 0, K)
+    dmaq("y", "LXV1", 0, "LX1", 0, 2 * P)
+    for w in ("N2", "B2"):
+        dmaq("y", w, K, "LX1", 0, K)
+    dmaq("y", "HW", 32 + HS * rank, "LX1", 0, HS)
+    dma("y", R("TW"), None, inap=T.w[:, :])
 
     def local(t):
         lx, k1 = "LX%d" % t, "K1_%d" % t
         for typ in "XL":
-            c0, bk, row = (P, 2, "pB") if typ == "X" else (0, 0, "pA")
+            c0, bk, row, d0 = (P, 2, "pB", 256) if typ == "X" else (0, 0, "pA", 0)
             q, qc = ("ZQ", 64) if typ == "X" else ("UQ", 0)
             for h in range(2):
                 mm("pD", bk + h, lx, c0 + 128 * h, q, qc, 128)
             mm(row, 0, q, qc, lx, c0, P)
-            act(R("R%sA" % typ), R(row, 0, P), AF.Abs)
             for h in range(2):
                 act(R("AC", bk + h, bk + h + 1), R("pD", 512 * (bk + h), 512 * (bk + h) + 1), AF.Abs)
+            act(R("R%sA" % typ), R(row, 0, P), AF.Abs)
+            for h in range(2):
+                act(R("DS", d0 + 128 * h, d0 + 128 * h + 128), R("R%sA" % typ, 128 * h, 128 * h + 128), AF.Sign,
+                    bias=R("AC", bk + h, bk + h + 1), scale=-1.0)
         mm("pC", 0, "UQ", 128, lx, 0, P, True, False)
         mm("pC", 0, "ZQ", 0, lx, P, P, False, True)
         for typ in "XL":
-            ra, rm = R("R%sA" % typ), R("RM%s" % typ)
-            run("g", lambda: g.affine_select(A(rm), A(ra), [[0, 2], [1, 128]], GT, -1.0, 0, -1), [ra], [rm])
-        for typ in "XL":
-            bk = 2 if typ == "X" else 0
-            lo, le = (LT, LE) if typ == "X" else (GT, GE)
-            row, rm, ct = "R%sA" % typ, "RM%s" % typ, "CT" + typ
-            a = [R("AC", bk + h, bk + h + 1) for h in range(2)]
-            ts(R(ct, 0, 512, step=4), R(row, 0, 128), a[0], lo)
-            ts(R(ct, 512, 1024, step=4), R(row, 128, 256), a[0], le)
-            ts(R(ct, 1, 1024, step=4), R(row), a[1], lo)
-            ts(R(ct, 2, 512, step=4), R(rm, 0, 128), a[0], EQL)
-            ts(R(ct, 514, 1024, step=4), R(rm, 128, 256), a[1], EQL)
+            bk, d0, m0 = (2, 256, 128) if typ == "X" else (0, 0, 0)
+            lo, le, on = (LT, LE, GT) if typ == "X" else (GT, GE, LT)
+            row, ct = "R%sA" % typ, "CT" + typ
+            ts(R(ct, 512, 1024, step=4), R(row, 128, 256), R("AC", bk, bk + 1), le)
+            ts(R(ct, 1, 512, step=4), R(row, 0, 128), R("AC", bk + 1, bk + 2), lo)
+            for h in range(2):
+                tt(R(ct, 513 * h, 512 * h + 512, step=4), R("DS", d0 + 128 * h, d0 + 128 * h + 128), R("MSK", m0, m0 + 128), on)
             quant("CQ" + typ, 0, P, ct, 0)
         mm("pE", 0, "COQ", 128, "CQX", 0, P, True, False)
         mm("pE", 0, "COQ", 0, "CQL", 0, P, False, True)
-        ts(R("EQK"), R("pE", 0, P), TGT, EQL)
-        tt(R("PRD"), R("EQK"), R("pC", 0, P), MUL)
+        for h in range(2):
+            ts(R("EQK", 128 * h, 128 * h + 128), R("pE", 128 * h, 128 * h + 128), TGT, EQL)
+        for h in range(2):
+            tt(R("PRD", 128 * h, 128 * h + 128), R("EQK", 128 * h, 128 * h + 128), R("pC", 128 * h, 128 * h + 128), MUL)
         act(R("JK", 0, P), R("PRD"), AF.Abs, acc=R(k1))
         to_all(R(k1), lambda r: R("KL%d" % t, slot_at(r), slot_at(r) + 1), "ak%d" % t)
 
-    def constants():
-        memset(R("WT", 0, 512), 256.0)
-        memset(R("WT", 1024, 1536), 256.0)
-        memset(R("WT", 512, 1024), 0.0)
-        memset(R("WT", 1536, 2048), 0.0)
-        ts(R("CC", 5, 6), R("CC", 0, 1), 1.0, ADD)
-        ts(R("CC", 6, 7), R("CC", 1, 2), 16.0, MUL)
-        ts(R("CC", 7, 8), R("CC", 1, 2), 16.0, MUL, 128.0, ADD)
-        ts(R("CC", 8, 9), R("CC", 0, 1), 16.0, MUL)
-        ts(R("CC", 9, 10), R("CC", 1, 2), 8.0, ADD)
-        for m, b, c in ((0, 0, 5), (0, 1, 5), (1, 0, 6), (1, 1, 7), (2, 0, 8), (2, 1, 8), (3, 0, 1), (3, 1, 9)):
-            act(R("WT", 512 * m + b, 512 * m + 512, step=4), R("ZB", 0, 128), AF.Identity, bias=R("CC", c, c + 1))
-        memset(R("OT", 2, 256, step=4), 0.0)
-        memset(R("OT", 3, 256, step=4), 0.0)
-        ts(R("M16"), R("N16"), Q16, EQL)
-        ts(R("KC"), R("CROW"), Q16, ADD)
+    def small_constants():
+        yield lambda: ts(R("KC"), R("CROW"), Q16, ADD)
         for p in (0, 64):
-            copy("v", R("IC", 0, 1, p, p + 32), R("CC", 3, 4, p, p + 32))
-            ts(R("IC", 1, 2, p, p + 32), R("CC", 3, 4, p, p + 32), 32.0, ADD)
-            memset(R("IC", 0, 2, p + 32, p + 64), 0.0)
+            yield lambda p=p: copy("v", R("IC", 0, 1, p, p + 32), R("CC", 3, 4, p, p + 32))
+            yield lambda p=p: ts(R("IC", 1, 2, p, p + 32), R("CC", 3, 4, p, p + 32), 32.0, ADD)
+            yield lambda p=p: memset(R("IC", 0, 2, p + 32, p + 64), 0.0)
+        yield lambda: memset(R("DCOL", p1=64), float(P * rank - 1))
+        yield lambda: memset(R("DCOL", p0=64), float(P * rank - 1 - P))
+        yield lambda: memset(R("BROW", 0, 64), float(2 * P + K + 1))
+        yield lambda: memset(R("BROW", 64, 128), float(2 * P + 1))
+        yield lambda: ts(R("B28"), R("B28"), Q16, ADD)
 
-    def constants2():
-        quant("NQ", 0, P, "TN", 0)
-        quant("EC", 0, 512, "ET", 0)
-        memset(R("DCOL", p1=64), float(P * rank - 1))
-        memset(R("DCOL", p0=64), float(P * rank - 1 - P))
-        memset(R("BROW", 0, 64), float(2 * P + K + 1))
-        memset(R("BROW", 64, 128), float(2 * P + 1))
-        ts(R("B28"), R("B28"), Q16, ADD)
-        ts(R("HB"), R("HB"), R("CC", 4, 5), ADD)
-        copy("s", R("ROW1"), R("ROWI"))
-        copy("s", R("ROW2"), R("ROWI"))
-
-    def constants3():
+    def late_constants():
         ch = rank // 2
+        ts(R("WC"), R("CC", 4, 5), float(HS * rank + 1), ADD)
+        ts(R("VX"), Q16, float(16 * (ch % 2) - 31), ADD)
         ts(R("HALF"), Q16, 8.0, GE if rank % 2 else LT, float(64 + 16 * rank - 16 * ch), MUL)
         copy("v", R("CW8", 0, 4), R("KC"))
         copy("v", R("CW8", 4, 8), R("KC"))
@@ -373,25 +368,49 @@ def rank_program(g, core, T, topo):
             bk = 2 if typ == "X" else 0
             for h in range(2):
                 mm("pD", bk + h, "CQ" + typ, 128 * h, "COQ", 256, 128)
+        if t == 1:
+            memset(R("SGN", p1=64), 1.0)
+            memset(R("SGN", p0=64), -1.0)
+            for m, b, c in ((0, 0, 5), (0, 1, 5), (1, 0, 6), (1, 1, 7), (2, 0, 8), (2, 1, 8), (3, 0, 1), (3, 1, 9)):
+                act(R("WT", 512 * m + b, 512 * m + 512, step=4), R("ZB", 0, 128), AF.Identity, bias=R("CC", c, c + 1))
+            memset(R("OT", 2, 256, step=4), 0.0)
+            memset(R("OT", 3, 256, step=4), 0.0)
+            ts(R("M16"), R("N16"), Q16, EQL)
         tt(R("K1S"), R("K1_%d" % t), R("SGN", 0, 1), MUL)
-        for c, s, d in ((0, 0, 0), (0, 0, 32), (0, 64, 64), (0, 64, 96), (1, 32, 0), (1, 32, 32), (1, 96, 64), (1, 96, 96)):
-            copy("s", R("OKC", c, c + 1, d, d + 32), R("K1S", 0, 1, s, s + 32))
         for h in range(2):
-            pl, px = R("pD", 512 * h, 512 * h + 1), R("pD", 512 * (2 + h), 512 * (2 + h) + 1)
+            px = R("pD", 512 * (2 + h), 512 * (2 + h) + 1)
             ts(R("OT", 256 + h, 512, step=4), R("IROW"), px, EQL)
             ts(R("OT", 256 + 2 + h, 512, step=4), R("IROW"), px, EQL)
-            ts(R("OT", h, 256, step=4), R("IROW"), pl, EQL)
+        for h in range(2):
+            ts(R("OT", h, 256, step=4), R("IROW"), R("pD", 512 * h, 512 * h + 1), EQL)
         if t == 1:
             quant("WTQ", 0, 512, "WT", 0)
         quant("OQ", 0, 128, "OT", 0)
-        for ps, m in (("pA", 0), ("pB", 2)):
+        for c, s, d in ((0, 0, 0), (0, 0, 32), (0, 64, 64), (0, 64, 96), (1, 32, 0), (1, 32, 32), (1, 96, 64), (1, 96, 96)):
+            copy("s", R("OKC", c, c + 1, d, d + 32), R("K1S", 0, 1, s, s + 32))
+        for ps, m in (("pB", 2), ("pA", 0)):
             mm(ps, 0, "WTQ", 128 * m, "OQ", 0, 128, True, False)
             mm(ps, 0, "WTQ", 128 * m + 128, "OQ", 0, 128, False, True)
+        fill = small_constants() if t == 1 else ()
+        fill = list(fill)
+
+        def some(n):
+            for _ in range(n):
+                if fill:
+                    fill.pop(0)()
+        if t == 1:
+            quant("NQ", 0, P, "TN", 0)
+        some(2)
         tt(R("PM"), R("M16"), R("pB", 0, 128), MUL)
+        some(2)
         tt(R("P64"), R("PM", 0, 128, step=2), R("PM", 1, 128, step=2), ADD)
+        some(2)
         tt(R("P32"), R("P64", 0, 64, step=2), R("P64", 1, 64, step=2), ADD)
+        some(2)
         tt(R("P16"), R("P32", 0, 32, step=2), R("P32", 1, 32, step=2), ADD)
+        some(2)
         tt(R("P8"), R("P16", 0, 16, step=2), R("P16", 1, 16, step=2), ADD)
+        some(9)
         ts(R("PIU%d" % t), R("P8"), 0.0, ADD)
 
     def merge(t):
@@ -422,30 +441,39 @@ def rank_program(g, core, T, topo):
         tt(R("G", 64, 128, 64, 128), R("Y", p0=64), R("TY", p0=64), ADD)
         copy("s", R("G", 0, 64, 64, 128), R("G", 0, 64, 0, 64))
         copy("v", R("G", 64, 128, 0, 64), R("G", 64, 128, 64, 128))
-        for c in range(4):
+        for step in "e0 e1 m0 e2 m1 e3 m2 m3".split():
+            c = int(step[1])
             e, u = R("EQ", 128 * c, 128 * c + 128), R("MU", 128 * c, 128 * c + 128)
-            ts(e, R("G"), R("KC", c, c + 1), EQL)
+            if step[0] == "e":
+                ts(e, R("G"), R("KC", c, c + 1), EQL)
+                continue
             tt(u, e, R("pA", 0, 128), MUL)
             for k in range(2):
-                j = 64 * (2 * c + k)
-                act(R("JK", 512 + j, 576 + j), R("MU", j, j + 64), AF.Copy, acc=R("FLD", 4 * k + c, 4 * k + c + 1))
+                j, f = 64 * (2 * c + k), R("FLD", 4 * k + c, 4 * k + c + 1)
+                if c == 3:
+                    total_of(f, R("MU", j, j + 64))
+                else:
+                    act(R("JK", 512 + j, 576 + j), R("MU", j, j + 64), AF.Copy, acc=f)
         tt(R("FM"), R("FLD", 0, 4), R("FLD", 4, 8), MAX)
         ts(R("ZU%d" % t), R("FM"), -1.0, ADD)
-        ts(R("INFO%d" % t), R("FM"), 0.0, ADD)
+        if t == 1:
+            ts(R("INFO1"), R("FM"), 0.0, ADD)
+        else:
+            ts(R("INFO2"), R("FM"), 0.0, GT, R("WC"), MUL)
         pick("Z%d" % t, 0, "LX%d" % t, 2 * P, "ZU%d" % t, 0, 4)
         to_all(R("INFO%d" % t), lambda r: R("IL%d" % t, 4 * slot_at(r), 4 * slot_at(r) + 4), "ai%d" % t)
 
     def lists(t, base):
         ts(R("NU%d" % t), R("FLD", 0, 4), -1.0, ADD)
+        tt(R("VT"), R("G"), R("BROW"), ADD)
+        ts(R("VM"), R("G"), float(K), LT)
         pick("N%d" % t, 0, "NQ", P, "NU%d" % t, 0, 4)
         for b in range(4):
             mm("pD", b, "EC", 128 * b, "N%d" % t, 0, 128, True, False)
-        ts(R("FP"), R("FLD"), 0.0, GT, float(base - 1), MUL)
-        tt(R("FO"), R("FP"), R("FLD"), ADD)
-        tt(R("VT"), R("G"), R("BROW"), ADD)
-        ts(R("VM"), R("G"), float(K), LT)
         tt(R("VU"), R("VT"), R("pA", 0, 128), SUB)
+        ts(R("FP"), R("FLD"), 0.0, GT, float(base - 1), MUL)
         tt(R("VT"), R("VU"), R("VM"), MUL)
+        tt(R("FO"), R("FP"), R("FLD"), ADD)
         tt(R("VU"), R("VT"), R("pA", 0, 128), ADD)
         row, off = R("ROW%d" % t), R("PIU%d" % t)
         run("v", lambda: g.vector.tensor_copy(A(row).indirect(A(off)), A(R("VU"))), [R("VU"), off], [row])
@@ -456,6 +484,8 @@ def rank_program(g, core, T, topo):
         for k in range(2):
             p = 64 * k
             ts(R("EQN", 0, 64, p, p + 64), R("G", p, p + 64, p, p + 64), R("CC", 2, 3, p, p + 64), EQL)
+        for k in range(2):
+            p = 64 * k
             tt(R("PN", 0, 64, p, p + 64), R("EQN", 0, 64, p, p + 64), R("pA", p, p + 64, p, p + 64), MUL)
         act(R("JK", 1024, 1088), R("PN"), AF.Copy, acc=R("NA", t - 1, t))
         ts(R("NB", t - 1, t), R("NA", t - 1, t), 0.0, GT, R("DCOL"), MUL)
@@ -475,12 +505,16 @@ def rank_program(g, core, T, topo):
         pick(nxt, 0, lxv, 2 * P + K + 128, "PLU%d" % t, 0, 16)
 
     local(1)
-    constants()
     post(1)
     merge(1)
     to_all(R("Z1"), lambda r: R("WIN1", K * slot_at(r), K * slot_at(r) + K), "azc")
     to_all(R("Z1s"), lambda r: R("WIN1s", K * slot_at(r), K * slot_at(r) + K), "azs")
-    constants2()
+    for b in range(4):
+        copy("s", R("ET", 512 * b + b, 512 * b + 512, step=4), R("EYE"))
+    copy("s", R("ROW1"), R("ROWI"))
+    copy("s", R("ROW2"), R("ROWI"))
+    memset(R("HT", 256, 512), 0.0)
+    quant("EC", 0, 512, "ET", 0)
     lists(1, PEERS * K)
     arrives([R("IL1")], "ai1", whole)
     ts(R("V28"), R("IL1"), 0.0, GT)
@@ -493,7 +527,7 @@ def rank_program(g, core, T, topo):
         tt(R("AB", 4 * k, 4 * k + 4), R("FO", 4 * k, 4 * k + 4), R("W5"), MAX)
     ts(R("LAB1"), R("AB"), 0.0, ADD)
     numbers(1)
-    constants3()
+    late_constants()
     arrives([R("WIN1", 0, PEERS * K)], "azc", whole)
     arrives([R("WIN1s", 0, PEERS * K)], "azs", whole)
     renew(1, PEERS * K + 2 * P)
@@ -504,53 +538,50 @@ def rank_program(g, core, T, topo):
     post(2)
     merge(2)
     for s, sem in (("", "ahc"), ("s", "ahs")):
-        to_each(lambda r: R("Z2" + s, HS * r, HS * r + HS), lambda r: R("HW" + s, 32 + HS * slot_at(r), 32 + HS * slot_at(r) + HS), sem)
+        to_each(lambda r: R("Z2" + s, HS * r, HS * r + HS), lambda r: R("HW" + s, 32 + HS * rank, 32 + HS * rank + HS), sem)
     ch, ce = rank // 2, rank // 2 // 2 * 2
     pick("HW", 0, "LX2", 2 * P, "ZU2", ce, ce + 2)
-    ts(R("VX"), Q16, float(16 * (ch - ce) + 1), ADD)
     ts(R("V8", rank, rank + 1), R("FM", ch, ch + 1), 0.0, GT, R("VX"), MUL)
+    numbers(2)
+    to_all(R("NUM"), lambda r: R("NL", 2 * slot_at(r), 2 * slot_at(r) + 2), "anum")
     lists(2, K + 128)
     tt(R("AB"), R("FO"), R("CW8"), MAX)
     ts(R("LAB2"), R("AB"), 0.0, ADD)
     arrives([R("IL2")], "ai2", whole)
-    ts(R("V7"), R("IL2", ch, 28, step=4), 0.0, GT)
-    if rank:
-        tt(R("V8", 0, rank), R("V7", 0, rank), R("HB", 0, rank), MUL)
-    if rank < PEERS:
-        tt(R("V8", rank + 1, 8), R("V7", rank, 7), R("HB", rank, 7), MUL)
+    for a, b in ((0, rank), (rank, PEERS)):
+        if a < b:
+            ts(R("V8", a + (a == rank), b + (a == rank)) if rank else R("V8", 1, N), R("IL2", 4 * a + ch, 4 * b, step=4), 0.0, ADD)
     total_of(R("VS"), R("V8"))
     ts(R("HL8"), R("V8"), -1.0, MUL, R("VS"), ADD)
-    ts(R("HLU2"), R("HL8"), 88.0, MIN, -1.0, ADD)
-    arrives([R("HW", 32, 88)], "ahc", part)
-    arrives([R("HWs", 32, 88)], "ahs", part)
-    pick("WIN2", K, "HW", 88, "HLU2", 0, 8)
+    ts(R("HLU2"), R("HL8"), float(K), MIN, 31.0, ADD)
+    arrives([R("HW" + s, 32 + a, 32 + b) for s in ("",) for a, b in ((0, HS * rank), (HS * rank + HS, K)) if a < b], "ahc", part)
+    arrives([R("HWs", 32 + a, 32 + b) for a, b in ((0, HS * rank), (HS * rank + HS, K)) if a < b], "ahs", part)
+    pick("WIN2", K, "HW", 32 + K, "HLU2", 0, 8)
     hc = K + HS * (rank % 2)
     for s, sem in (("", "awc"), ("s", "aws")):
         to_each(lambda r: R("WIN2" + s, hc + 16 * r, hc + 16 * r + HS), lambda r: R("WIN2" + s, HS * rank, HS * rank + HS), sem)
-    numbers(2)
-    to_all(R("NUM"), lambda r: R("NL", 2 * slot_at(r), 2 * slot_at(r) + 2), "anum")
-    for s, sem in (("", "awc"), ("s", "aws")):
-        arrives([R("WIN2" + s, a, b) for a, b in ((0, HS * rank), (HS * rank + HS, K)) if a < b], sem, part)
-    renew(2, K + 128 + 2 * P)
-
     arrives([R("NL")], "anum", whole)
-    dma("y", None, R("LX3", P, 2 * P), outap=T.oc[:, 4 * P:8 * P])
-    for k in range(4):
-        dma("y", None, R("LX3s", P, 2 * P, 32 * k, 32 * k + 4), outap=T.osc[4 * k:4 * k + 4, P:2 * P])
-    for h in range(2):
-        mm("pD", h, "WQ", 0, "LX3", 128 * h, 128)
-    dma("y", None, R("LX3", 0, P), outap=T.oc[:, 0:4 * P])
-    for k in range(4):
-        dma("y", None, R("LX3s", 0, P, 32 * k, 32 * k + 4), outap=T.osc[4 * k:4 * k + 4, 0:P])
-    for h in range(2):
-        copy("sv"[h], R("YO", 128 * h, 128 * h + 128), R("pD", 512 * h, 512 * h + 128))
-    dma("s", None, R("YO"), outap=T.y[:, :])
     for t in range(2):
         total_of(R("RES", t, t + 1), R("NL", t, 14, step=2))
     tt(R("RES", 2, 4), R("RES", 0, 2), R("NUM"), ADD)
     for t in range(2):
-        dma("s", None, R("RES", 2 + t, 3 + t, 0, 64), outap=T.lw[t:t + 1, :])
-        dma("s", None, R("RES", 2 + t, 3 + t, 64, 128), outap=T.sw[t:t + 1, :])
+        dma("y", None, R("RES", 2 + t, 3 + t, 0, 64), outap=T.lw[t:t + 1, :])
+        dma("y", None, R("RES", 2 + t, 3 + t, 64, 128), outap=T.sw[t:t + 1, :])
+    for s, sem in (("", "awc"), ("s", "aws")):
+        arrives([R("WIN2" + s, a, b) for a, b in ((0, HS * rank), (HS * rank + HS, K)) if a < b], sem, part)
+    renew(2, K + 128 + 2 * P)
+
+    for h in range(2):
+        mm("pD", h, "WQ", 0, "LX3", 128 * h, 128)
+    dma("y", None, R("LX3", P, 2 * P), outap=T.oc[:, 4 * P:8 * P])
+    for k in range(4):
+        dma("y", None, R("LX3s", P, 2 * P, 32 * k, 32 * k + 4), outap=T.osc[4 * k:4 * k + 4, P:2 * P])
+    dma("y", None, R("LX3", 0, P), outap=T.oc[:, 0:4 * P])
+    for h in range(2):
+        copy("sv"[h], R("YO", 128 * h, 128 * h + 128), R("pD", 512 * h, 512 * h + 128))
+    for k in range(4):
+        dma("y", None, R("LX3s", 0, P, 32 * k, 32 * k + 4), outap=T.osc[4 * k:4 * k + 4, 0:P])
+    dma("s", None, R("YO"), outap=T.y[:, :])
     for sem in total:
         if known["g"].get(sem, 0) < total[sem]:
             g.wait_ge(T.sem[sem], total[sem])

@@ -28,17 +28,17 @@ def _pool(name, d, parts):
 
 
 for _n, _w in (("TL", 1024), ("TX", 1024), ("TN", 1024), ("TW", 512), ("U4", 4), ("Z4", 4), ("UT", 1024), ("ZT", 1024), ("ONE", 192),
-               ("ZB", 512), ("CO", 1536), ("WT", 2048), ("ET", 2048), ("EYE", 128), ("CTL", 1024), ("CTX", 1024), ("OT", 512), ("HT", 512),
+               ("ZB", 512), ("CO", 1536), ("WT", 2816), ("ET", 2048), ("EYE", 128), ("CTL", 1024), ("CTX", 1024), ("OT", 768), ("HT", 512),
                ("MSK", 256), ("DS", 512)):
     _sb(_n, _w, "bfloat16")
-_pool("BB", "bfloat16", (("EQK", 256), ("MM", 448), ("EQ", 512), ("EQN", 64)))
+_pool("BB", "bfloat16", (("EQK", 256), ("MM", 448), ("EQ", 256), ("EQN", 64)))
 _pool("FC", "float32", (("CC", 16), ("IROW", 64), ("N16", 128), ("M16", 128), ("CROW", 4), ("KC", 4), ("CW8", 8), ("HALF", 1), ("B28", 28),
                         ("WC", 1), ("VX", 1), ("IC", 2), ("SGN", 32), ("DCOL", 1), ("BROW", 128), ("ROWI", 512)))
 _pool("FD", "float32", (("AC", 4), ("RLA", 256), ("RXA", 256)))
 _pool("FB", "float32", (("PRD", 256), ("JK", 1088), ("PM", 128), ("P64", 64), ("P32", 32), ("P16", 16), ("P8", 8), ("K1S", 1), ("OKC", 2),
-                        ("KR", 224), ("KW", 224), ("XC", 2), ("XR", 64), ("Y", 64), ("TY", 64), ("G", 128), ("MU", 512), ("FLD", 8), ("FM", 4),
-                        ("FO", 8), ("FP", 8), ("VT", 128), ("VM", 128), ("VU", 128), ("PN", 64), ("NA", 2), ("NB", 2), ("V28", 28), ("V29", 28),
-                        ("W12", 12), ("W4", 8), ("W5", 4), ("AB", 8), ("V8", 8), ("VS", 1), ("HL8", 8)))
+                        ("KR", 224), ("KW", 224), ("XC", 2), ("XR", 64), ("Y", 64), ("TY", 64), ("GS", 64), ("G", 128), ("MU", 256), ("FS", 4),
+                        ("SW", 4), ("FLD", 8), ("FM", 4), ("FO", 8), ("FP", 8), ("VT", 128), ("VM", 128), ("VU", 128), ("PN", 64), ("NA", 2),
+                        ("NB", 2), ("V28", 28), ("V29", 28), ("W12", 12), ("W4", 8), ("W5", 4), ("AB", 8), ("V8", 8), ("VS", 1), ("HL8", 8)))
 for _n, _w in (("NUM", 2), ("NL", 14), ("RES", 4), ("YO", 256)):
     _sb(_n, _w, "float32")
 for _t in "12":
@@ -53,8 +53,8 @@ for _t in "12":
     _codes("N" + _t, 128)
 _sb("PI", 1, "int32")
 _sb("II", 5, "int32")
-for _n, _w in (("UQ", 256), ("ZQ", 256), ("LX1", 512), ("LX2", 512), ("LX3", 512), ("NQ", 256), ("WQ", 128), ("COQ", 384), ("WTQ", 512), ("EC", 512),
-               ("CQL", 256), ("CQX", 256), ("OQ", 128), ("WIN1", PEERS * K + 2 * P), ("WIN2", K + 128 + 2 * P), ("HW", 32 + K)):
+for _n, _w in (("UQ", 256), ("ZQ", 256), ("LX1", 512), ("LX2", 512), ("LX3", 512), ("NQ", 256), ("WQ", 128), ("COQ", 384), ("WTQ", 704), ("EC", 512),
+               ("CQL", 256), ("CQX", 256), ("OQ", 192), ("WIN1", PEERS * K + 2 * P), ("WIN2", K + 128 + 2 * P), ("HW", 32 + K)):
     _codes(_n, _w)
 PSUM = {"pA": 1, "pB": 1, "pC": 1, "pD": 4, "pE": 1}
 for _n in PSUM:
@@ -105,16 +105,16 @@ def rank_program(g, core, T, topo):
             for kind, box, tok in hist.get(w[0], []):
                 if overlap(b, box) and not (adds and tok[2] == q):
                     need.append(tok)
-        for tok in sorted(need, key=lambda k: -k[4]):
+        for tok in sorted(need, key=lambda k: -k[3]):
             if known[q].get(tok[0], 0) < tok[1]:
                 queues[q].wait_ge(T.sem[tok[0]], tok[1])
                 known[q][tok[0]] = tok[1]
-                for s, n in tok[5].items():
+                for s, n in tok[4].items():
                     known[q][s] = max(known[q].get(s, 0), n)
 
     def note(q, reads, writes, sem, val):
         seq[0] += 1
-        tok = (sem, val, q, None, seq[0], dict(known[q]) if q in known else {})
+        tok = (sem, val, q, seq[0], dict(known[q]) if q in known else {})
         for w in writes:
             b = bank(w)
             hist[w[0]] = [h for h in hist.get(w[0], []) if not covers(b, h[1])] + [("w", b, tok)]
@@ -249,24 +249,27 @@ def rank_program(g, core, T, topo):
         total[sem] = PEERS * per
         note("remote", [], regions, sem, PEERS * per)
 
+    ch = rank // 2
     dma("y", R("U4"), None, inap=T.u[:, 0:4])
     dma("s", R("Z4"), None, inap=T.z[:, 0:4])
     dma("y", R("TX"), None, inap=T.dm[:, :])
-    dma("s", R("TL"), None, inap=T.lv[:, :])
+    dma("y", R("TL"), None, inap=T.lv[:, :])
     iota(R("PI"), [[0, 1]], 0, 1)
-    memset(R("ZB"), 0.0)
-    memset(R("EYE"), 0.5)
     memset(R("MSK", 0, 128), 0.5)
     memset(R("MSK", 128, 256), -0.5)
-    choose(R("EYE"), [[-1, 128]], EQL, 0.0, 1)
     choose(R("MSK", 0, 128), [[1, 128]], GT, -0.5, -1)
     choose(R("MSK", 128, 256), [[1, 128]], GT, 0.5, -1)
-    iota(R("IROW"), [[1, 64]], 0, 0)
-    iota(R("N16"), [[0, 8], [1, 16]], 0, 0)
+    memset(R("ZB"), 0.0)
+    memset(R("ONE"), 1.0)
+    memset(R("EYE"), 0.5)
     iota(R("CROW"), [[16, 4]], 0, 0)
     iota(R("B28"), [[K, PEERS], [16, 4]], 0, 0)
+    iota(R("IROW"), [[1, 64]], 0, 0)
+    iota(R("N16"), [[0, 8], [1, 16]], 0, 0)
+    for a, b in ((64, 192), (256, 384), (448, 704)):
+        iota(R("WT", 4 * a, 4 * b), [[0, 4 * (b - a)]], 1, 0)
+    choose(R("EYE"), [[-1, 128]], EQL, 0.0, 1)
     iota(R("ROWI"), [[256, 2], [1, 16], [16, 16]], 1, 0)
-    memset(R("ONE"), 1.0)
     for c0, c1, v in ((0, 256, 1.0), (256, 768, 0.0), (768, 1536, 1.0)):
         memset(R("CO", c0, c1), v)
     memset(R("UT", 768, 1024), 0.0)
@@ -274,48 +277,48 @@ def rank_program(g, core, T, topo):
     for i, (op, v) in enumerate(((AluOpType.bitwise_and, 15), (AluOpType.arith_shift_right, 4), (AluOpType.bitwise_and, 63),
                                  (AluOpType.bitwise_and, 31), (AluOpType.bitwise_and, 7))):
         ts(R("II", i, i + 1), R("PI"), v, op)
-    quant("COQ", 0, 384, "CO", 0)
-    copy("v", R("CC", 0, 5), R("II"))
-    Q16, TGT = R("CC", 0, 1), R("CC", 2, 3)
     for b in range(4):
         copy("s", R("ET", 512 * b, 512 * b + 512), R("ZB"))
-    for ct in ("CTL", "CTX"):
-        memset(R(ct, 2, 1024, step=4), 0.0)
-        memset(R(ct, 3, 1024, step=4), 0.0)
-    for m in range(4):
-        memset(R("WT", 512 * m, 512 * m + 512), 0.0 if m % 2 else 256.0)
+    for a in (0, 192, 384):
+        memset(R("WT", 4 * a, 4 * a + 256), 0.0)
+    copy("v", R("CC", 0, 5), R("II"))
+    Q16, TGT = R("CC", 0, 1), R("CC", 2, 3)
+    memset(R("OT"), 0.0)
     ts(R("CC", 5, 6), R("CC", 0, 1), 1.0, ADD)
     ts(R("CC", 6, 7), R("CC", 1, 2), 16.0, MUL)
     ts(R("CC", 7, 8), R("CC", 1, 2), 16.0, MUL, 128.0, ADD)
     ts(R("CC", 8, 9), R("CC", 0, 1), 16.0, MUL)
     ts(R("CC", 9, 10), R("CC", 1, 2), 8.0, ADD)
+    memset(R("OT", 258, 512, step=4), 1.0)
+    ts(R("KC"), R("CROW"), Q16, ADD)
+    ts(R("HALF"), Q16, 8.0, GE if rank % 2 else LT, float(64 + 16 * rank - 16 * ch), MUL)
+    ts(R("WC"), R("CC", 4, 5), float(HS * rank + 1), ADD)
+    ts(R("VX"), Q16, float(16 * (ch % 2) - 31), ADD)
     for t in range(4):
         ts(R("UT", t, 768, step=4), R("ONE"), R("U4", t, t + 1), MUL)
         act(R("ZT", 256 + t, 1024, step=4), R("ZB", 0, 192), AF.Identity, bias=R("Z4", t, t + 1))
-    quant("UQ", 0, 256, "UT", 0)
     quant("ZQ", 0, 256, "ZT", 0)
+    quant("UQ", 0, 256, "UT", 0)
     quant("LX1", P, P, "TX", 0)
+    for ct in ("CTX", "CTL"):
+        memset(R(ct, 2, 1024, step=4), 0.0)
+        memset(R(ct, 3, 1024, step=4), 0.0)
+    quant("COQ", 0, 384, "CO", 0)
     quant("LX1", 0, P, "TL", 0)
     dmaq("y", "WIN1", PEERS * K, "LX1", 0, 2 * P)
     dma("y", R("TN"), None, inap=T.nz[:, :])
-    for w in ("N1", "B1"):
-        dmaq("y", w, K, "LX1", 0, K)
-    dmaq("y", "LXV1", 0, "LX1", 0, 2 * P)
-    for w in ("N2", "B2"):
-        dmaq("y", w, K, "LX1", 0, K)
-    dmaq("y", "HW", 32 + HS * rank, "LX1", 0, HS)
-    dma("y", R("TW"), None, inap=T.w[:, :])
 
     def local(t):
         lx, k1 = "LX%d" % t, "K1_%d" % t
         for typ in "XL":
             c0, bk, row, d0 = (P, 2, "pB", 256) if typ == "X" else (0, 0, "pA", 0)
             q, qc = ("ZQ", 64) if typ == "X" else ("UQ", 0)
+            at = (("pE", 0), ("pC", 0)) if typ == "X" else (("pD", 0), ("pD", 1))
             for h in range(2):
-                mm("pD", bk + h, lx, c0 + 128 * h, q, qc, 128)
+                mm(at[h][0], at[h][1], lx, c0 + 128 * h, q, qc, 128)
             mm(row, 0, q, qc, lx, c0, P)
             for h in range(2):
-                act(R("AC", bk + h, bk + h + 1), R("pD", 512 * (bk + h), 512 * (bk + h) + 1), AF.Abs)
+                act(R("AC", bk + h, bk + h + 1), R(at[h][0], 512 * at[h][1], 512 * at[h][1] + 1), AF.Abs)
             act(R("R%sA" % typ), R(row, 0, P), AF.Abs)
             for h in range(2):
                 act(R("DS", d0 + 128 * h, d0 + 128 * h + 128), R("R%sA" % typ, 128 * h, 128 * h + 128), AF.Sign,
@@ -337,31 +340,21 @@ def rank_program(g, core, T, topo):
             ts(R("EQK", 128 * h, 128 * h + 128), R("pE", 128 * h, 128 * h + 128), TGT, EQL)
         for h in range(2):
             tt(R("PRD", 128 * h, 128 * h + 128), R("EQK", 128 * h, 128 * h + 128), R("pC", 128 * h, 128 * h + 128), MUL)
+        if t == 1:
+            for m, b, c in ((448, 0, 8), (448, 1, 8), (576, 0, 1), (576, 1, 9), (64, 0, 5), (64, 1, 5), (256, 0, 6), (256, 1, 7)):
+                act(R("WT", 4 * m + b, 4 * m + 512, step=4), R("ZB", 0, 128), AF.Identity, bias=R("CC", c, c + 1))
         act(R("JK", 0, P), R("PRD"), AF.Abs, acc=R(k1))
         to_all(R(k1), lambda r: R("KL%d" % t, slot_at(r), slot_at(r) + 1), "ak%d" % t)
 
     def small_constants():
-        yield lambda: ts(R("KC"), R("CROW"), Q16, ADD)
+        out = [lambda: ts(R("M16"), R("N16"), Q16, EQL), lambda: ts(R("B28"), R("B28"), Q16, ADD)]
         for p in (0, 64):
-            yield lambda p=p: copy("v", R("IC", 0, 1, p, p + 32), R("CC", 3, 4, p, p + 32))
-            yield lambda p=p: ts(R("IC", 1, 2, p, p + 32), R("CC", 3, 4, p, p + 32), 32.0, ADD)
-            yield lambda p=p: memset(R("IC", 0, 2, p + 32, p + 64), 0.0)
-        yield lambda: memset(R("DCOL", p1=64), float(P * rank - 1))
-        yield lambda: memset(R("DCOL", p0=64), float(P * rank - 1 - P))
-        yield lambda: memset(R("BROW", 0, 64), float(2 * P + K + 1))
-        yield lambda: memset(R("BROW", 64, 128), float(2 * P + 1))
-        yield lambda: ts(R("B28"), R("B28"), Q16, ADD)
-
-    def late_constants():
-        ch = rank // 2
-        ts(R("WC"), R("CC", 4, 5), float(HS * rank + 1), ADD)
-        ts(R("VX"), Q16, float(16 * (ch % 2) - 31), ADD)
-        ts(R("HALF"), Q16, 8.0, GE if rank % 2 else LT, float(64 + 16 * rank - 16 * ch), MUL)
-        copy("v", R("CW8", 0, 4), R("KC"))
-        copy("v", R("CW8", 4, 8), R("KC"))
-        for c in (ch, 4 + ch):
-            tt(R("CW8", c, c + 1), R("KC", ch, ch + 1), R("HALF"), ADD)
-        quant("WQ", 0, 128, "TW", 0)
+            out.append(lambda p=p: copy("v", R("IC", 0, 1, p, p + 32), R("CC", 3, 4, p, p + 32)))
+            out.append(lambda p=p: ts(R("IC", 1, 2, p, p + 32), R("CC", 3, 4, p, p + 32), 32.0, ADD))
+            out.append(lambda p=p: memset(R("IC", 0, 2, p + 32, p + 64), 0.0))
+        out += [lambda: memset(R("DCOL", p1=64), float(P * rank - 1)), lambda: memset(R("DCOL", p0=64), float(P * rank - 1 - P)),
+                lambda: memset(R("BROW", 0, 64), float(2 * P + K + 1)), lambda: memset(R("BROW", 64, 128), float(2 * P + 1))]
+        return out
 
     def post(t):
         for typ in "XL":
@@ -371,28 +364,26 @@ def rank_program(g, core, T, topo):
         if t == 1:
             memset(R("SGN", p1=64), 1.0)
             memset(R("SGN", p0=64), -1.0)
-            for m, b, c in ((0, 0, 5), (0, 1, 5), (1, 0, 6), (1, 1, 7), (2, 0, 8), (2, 1, 8), (3, 0, 1), (3, 1, 9)):
-                act(R("WT", 512 * m + b, 512 * m + 512, step=4), R("ZB", 0, 128), AF.Identity, bias=R("CC", c, c + 1))
-            memset(R("OT", 2, 256, step=4), 0.0)
-            memset(R("OT", 3, 256, step=4), 0.0)
-            ts(R("M16"), R("N16"), Q16, EQL)
+            quant("WTQ", 448, 256, "WT", 448)
+        for c, bk in ((256, 2), (0, 0)):
+            for h in range(2):
+                ts(R("OT", c + h, c + 256, step=4), R("IROW"), R("pD", 512 * (bk + h), 512 * (bk + h) + 1), EQL)
+        quant("OQ", 0, 192, "OT", 0)
         tt(R("K1S"), R("K1_%d" % t), R("SGN", 0, 1), MUL)
-        for h in range(2):
-            px = R("pD", 512 * (2 + h), 512 * (2 + h) + 1)
-            ts(R("OT", 256 + h, 512, step=4), R("IROW"), px, EQL)
-            ts(R("OT", 256 + 2 + h, 512, step=4), R("IROW"), px, EQL)
-        for h in range(2):
-            ts(R("OT", h, 256, step=4), R("IROW"), R("pD", 512 * h, 512 * h + 1), EQL)
-        if t == 1:
-            quant("WTQ", 0, 512, "WT", 0)
-        quant("OQ", 0, 128, "OT", 0)
         for c, s, d in ((0, 0, 0), (0, 0, 32), (0, 64, 64), (0, 64, 96), (1, 32, 0), (1, 32, 32), (1, 96, 64), (1, 96, 96)):
             copy("s", R("OKC", c, c + 1, d, d + 32), R("K1S", 0, 1, s, s + 32))
-        for ps, m in (("pB", 2), ("pA", 0)):
-            mm(ps, 0, "WTQ", 128 * m, "OQ", 0, 128, True, False)
-            mm(ps, 0, "WTQ", 128 * m + 128, "OQ", 0, 128, False, True)
-        fill = small_constants() if t == 1 else ()
-        fill = list(fill)
+        copy("s", R("ROW%d" % t), R("ROWI"))
+        if t == 1:
+            for b in range(4):
+                copy("s", R("ET", 512 * b + b, 512 * b + 512, step=4), R("EYE"))
+            quant("WTQ", 0, 448, "WT", 0)
+        mm("pB", 0, "WTQ", 448, "OQ", 0, 128, True, False)
+        mm("pB", 0, "WTQ", 576, "OQ", 0, 128, False, True)
+        for i, (c, d) in enumerate(((128, 0), (320, 0), (0, 64), (192, 64))):
+            mm("pC", 0, "WTQ", c, "OQ", d, 128, i == 0, i == 3)
+        mm("pA", 0, "WTQ", 64, "OQ", 0, 128, True, False)
+        mm("pA", 0, "WTQ", 256, "OQ", 0, 128, False, True)
+        fill = small_constants() if t == 1 else []
 
         def some(n):
             for _ in range(n):
@@ -416,6 +407,13 @@ def rank_program(g, core, T, topo):
     def merge(t):
         kl = "KL%d" % t
         arrives([R(kl)], "ak%d" % t, whole)
+        if t == 1:
+            waits("y", [R(kl)], [])
+            dmaq("y", "LXV1", 0, "LX1", 0, 2 * P)
+            for w in ("N1", "B1", "N2", "B2"):
+                dmaq("y", w, K, "LX1", 0, K)
+            dmaq("y", "HW", 32 + HS * rank, "LX1", 0, HS)
+            dma("y", R("TW"), None, inap=T.w[:, :])
         for s in range(PEERS):
             o, kc = R("KR", 32 * s, 32 * s + 32), R(kl, s, s + 1)
             if s % 2:
@@ -437,24 +435,21 @@ def rank_program(g, core, T, topo):
         copy("v", R("TY", p0=0, p1=32), R("Y", p0=32, p1=64))
         copy("s", R("TY", p0=96, p1=128), R("Y", p0=64, p1=96))
         copy("v", R("TY", p0=64, p1=96), R("Y", p0=96, p1=128))
-        tt(R("G", 0, 64, 0, 64), R("Y", p1=64), R("TY", p1=64), ADD)
-        tt(R("G", 64, 128, 64, 128), R("Y", p0=64), R("TY", p0=64), ADD)
-        copy("s", R("G", 0, 64, 64, 128), R("G", 0, 64, 0, 64))
-        copy("v", R("G", 64, 128, 0, 64), R("G", 64, 128, 64, 128))
+        tt(R("GS"), R("Y"), R("TY"), ADD)
         for step in "e0 e1 m0 e2 m1 e3 m2 m3".split():
             c = int(step[1])
-            e, u = R("EQ", 128 * c, 128 * c + 128), R("MU", 128 * c, 128 * c + 128)
+            e, u = R("EQ", 64 * c, 64 * c + 64), R("MU", 64 * c, 64 * c + 64)
             if step[0] == "e":
-                ts(e, R("G"), R("KC", c, c + 1), EQL)
+                ts(e, R("GS"), R("KC", c, c + 1), EQL)
                 continue
-            tt(u, e, R("pA", 0, 128), MUL)
-            for k in range(2):
-                j, f = 64 * (2 * c + k), R("FLD", 4 * k + c, 4 * k + c + 1)
-                if c == 3:
-                    total_of(f, R("MU", j, j + 64))
-                else:
-                    act(R("JK", 512 + j, 576 + j), R("MU", j, j + 64), AF.Copy, acc=f)
-        tt(R("FM"), R("FLD", 0, 4), R("FLD", 4, 8), MAX)
+            tt(u, e, R("pC", 0, 64), MUL)
+            if c == 3:
+                total_of(R("FS", 3, 4), u)
+            else:
+                act(R("JK", 512 + 64 * c, 576 + 64 * c), u, AF.Copy, acc=R("FS", c, c + 1))
+        copy("s", R("SW", p0=64), R("FS", p1=64))
+        copy("v", R("SW", p1=64), R("FS", p0=64))
+        tt(R("FM"), R("FS"), R("SW"), MAX)
         ts(R("ZU%d" % t), R("FM"), -1.0, ADD)
         if t == 1:
             ts(R("INFO1"), R("FM"), 0.0, ADD)
@@ -464,14 +459,23 @@ def rank_program(g, core, T, topo):
         to_all(R("INFO%d" % t), lambda r: R("IL%d" % t, 4 * slot_at(r), 4 * slot_at(r) + 4), "ai%d" % t)
 
     def lists(t, base):
-        ts(R("NU%d" % t), R("FLD", 0, 4), -1.0, ADD)
+        a, b = t - 1, t
+        ts(R("EQN"), R("GS"), TGT, EQL)
+        for q, o, i in (("v", R("FLD", 0, 4, 0, 64), R("FS", p1=64)), ("s", R("FLD", 0, 4, 64, 128), R("FS", p1=64)),
+                        ("v", R("FLD", 4, 8, 64, 128), R("FS", p0=64)), ("s", R("FLD", 4, 8, 0, 64), R("FS", p0=64)),
+                        ("v", R("G", 0, 64, 0, 64), R("GS", p1=64)), ("s", R("G", 0, 64, 64, 128), R("GS", p1=64)),
+                        ("v", R("G", 64, 128, 64, 128), R("GS", p0=64)), ("s", R("G", 64, 128, 0, 64), R("GS", p0=64))):
+            copy(q, o, i)
+        tt(R("PN"), R("EQN"), R("pC", 0, 64), MUL)
+        act(R("JK", 1024, 1088), R("PN"), AF.Copy, acc=R("NA", a, b))
         tt(R("VT"), R("G"), R("BROW"), ADD)
         ts(R("VM"), R("G"), float(K), LT)
-        pick("N%d" % t, 0, "NQ", P, "NU%d" % t, 0, 4)
-        for b in range(4):
-            mm("pD", b, "EC", 128 * b, "N%d" % t, 0, 128, True, False)
+        ts(R("NB", a, b), R("NA", a, b), 0.0, GT, R("DCOL"), MUL)
         tt(R("VU"), R("VT"), R("pA", 0, 128), SUB)
         ts(R("FP"), R("FLD"), 0.0, GT, float(base - 1), MUL)
+        tt(R("NUM", a, b), R("NB", a, b), R("NA", a, b), ADD)
+        if t == 2:
+            to_all(R("NUM"), lambda r: R("NL", 2 * slot_at(r), 2 * slot_at(r) + 2), "anum")
         tt(R("VT"), R("VU"), R("VM"), MUL)
         tt(R("FO"), R("FP"), R("FLD"), ADD)
         tt(R("VU"), R("VT"), R("pA", 0, 128), ADD)
@@ -479,17 +483,12 @@ def rank_program(g, core, T, topo):
         run("v", lambda: g.vector.tensor_copy(A(row).indirect(A(off)), A(R("VU"))), [R("VU"), off], [row])
         for k in range(2):
             dma("y", R("LST%d" % t, 16 * k, 16 * k + 16), R("ROW%d" % t, 256 * k, 256 * k + 256, 0, 8))
-
-    def numbers(t):
-        for k in range(2):
-            p = 64 * k
-            ts(R("EQN", 0, 64, p, p + 64), R("G", p, p + 64, p, p + 64), R("CC", 2, 3, p, p + 64), EQL)
-        for k in range(2):
-            p = 64 * k
-            tt(R("PN", 0, 64, p, p + 64), R("EQN", 0, 64, p, p + 64), R("pA", p, p + 64, p, p + 64), MUL)
-        act(R("JK", 1024, 1088), R("PN"), AF.Copy, acc=R("NA", t - 1, t))
-        ts(R("NB", t - 1, t), R("NA", t - 1, t), 0.0, GT, R("DCOL"), MUL)
-        tt(R("NUM", t - 1, t), R("NB", t - 1, t), R("NA", t - 1, t), ADD)
+        ts(R("NU%d" % t), R("FLD", 0, 4), -1.0, ADD)
+        pick("N%d" % t, 0, "NQ", P, "NU%d" % t, 0, 4)
+        if t == 1:
+            quant("EC", 0, 512, "ET", 0)
+        for k in range(4):
+            mm("pD", k, "EC", 128 * k, "N%d" % t, 0, 128, True, False)
 
     def renew(t, width):
         win, lxv, nxt, lab = "WIN%d" % t, "LXV%d" % t, "LX%d" % (t + 1), "LAB%d" % t
@@ -509,12 +508,6 @@ def rank_program(g, core, T, topo):
     merge(1)
     to_all(R("Z1"), lambda r: R("WIN1", K * slot_at(r), K * slot_at(r) + K), "azc")
     to_all(R("Z1s"), lambda r: R("WIN1s", K * slot_at(r), K * slot_at(r) + K), "azs")
-    for b in range(4):
-        copy("s", R("ET", 512 * b + b, 512 * b + 512, step=4), R("EYE"))
-    copy("s", R("ROW1"), R("ROWI"))
-    copy("s", R("ROW2"), R("ROWI"))
-    memset(R("HT", 256, 512), 0.0)
-    quant("EC", 0, 512, "ET", 0)
     lists(1, PEERS * K)
     arrives([R("IL1")], "ai1", whole)
     ts(R("V28"), R("IL1"), 0.0, GT)
@@ -526,8 +519,7 @@ def rank_program(g, core, T, topo):
     for k in (1, 0):
         tt(R("AB", 4 * k, 4 * k + 4), R("FO", 4 * k, 4 * k + 4), R("W5"), MAX)
     ts(R("LAB1"), R("AB"), 0.0, ADD)
-    numbers(1)
-    late_constants()
+    memset(R("HT", 256, 512), 0.0)
     arrives([R("WIN1", 0, PEERS * K)], "azc", whole)
     arrives([R("WIN1s", 0, PEERS * K)], "azs", whole)
     renew(1, PEERS * K + 2 * P)
@@ -539,27 +531,30 @@ def rank_program(g, core, T, topo):
     merge(2)
     for s, sem in (("", "ahc"), ("s", "ahs")):
         to_each(lambda r: R("Z2" + s, HS * r, HS * r + HS), lambda r: R("HW" + s, 32 + HS * rank, 32 + HS * rank + HS), sem)
-    ch, ce = rank // 2, rank // 2 // 2 * 2
-    pick("HW", 0, "LX2", 2 * P, "ZU2", ce, ce + 2)
+    pick("HW", 0, "LX2", 2 * P, "ZU2", ch // 2 * 2, ch // 2 * 2 + 2)
     ts(R("V8", rank, rank + 1), R("FM", ch, ch + 1), 0.0, GT, R("VX"), MUL)
-    numbers(2)
-    to_all(R("NUM"), lambda r: R("NL", 2 * slot_at(r), 2 * slot_at(r) + 2), "anum")
     lists(2, K + 128)
+    for c in (0, 4):
+        copy("v", R("CW8", c, c + 4), R("KC"))
+        tt(R("CW8", c + ch, c + ch + 1), R("KC", ch, ch + 1), R("HALF"), ADD)
     tt(R("AB"), R("FO"), R("CW8"), MAX)
     ts(R("LAB2"), R("AB"), 0.0, ADD)
     arrives([R("IL2")], "ai2", whole)
-    for a, b in ((0, rank), (rank, PEERS)):
-        if a < b:
-            ts(R("V8", a + (a == rank), b + (a == rank)) if rank else R("V8", 1, N), R("IL2", 4 * a + ch, 4 * b, step=4), 0.0, ADD)
+    if rank:
+        ts(R("V8", 0, rank), R("IL2", ch, 4 * rank, step=4), 0.0, ADD)
+    if rank < PEERS:
+        ts(R("V8", rank + 1, N), R("IL2", 4 * rank + ch, 4 * PEERS, step=4), 0.0, ADD)
     total_of(R("VS"), R("V8"))
     ts(R("HL8"), R("V8"), -1.0, MUL, R("VS"), ADD)
     ts(R("HLU2"), R("HL8"), float(K), MIN, 31.0, ADD)
-    arrives([R("HW" + s, 32 + a, 32 + b) for s in ("",) for a, b in ((0, HS * rank), (HS * rank + HS, K)) if a < b], "ahc", part)
-    arrives([R("HWs", 32 + a, 32 + b) for a, b in ((0, HS * rank), (HS * rank + HS, K)) if a < b], "ahs", part)
+    others = [(a, b) for a, b in ((0, HS * rank), (HS * rank + HS, K)) if a < b]
+    for s, sem in (("", "ahc"), ("s", "ahs")):
+        arrives([R("HW" + s, 32 + a, 32 + b) for a, b in others], sem, part)
     pick("WIN2", K, "HW", 32 + K, "HLU2", 0, 8)
     hc = K + HS * (rank % 2)
     for s, sem in (("", "awc"), ("s", "aws")):
         to_each(lambda r: R("WIN2" + s, hc + 16 * r, hc + 16 * r + HS), lambda r: R("WIN2" + s, HS * rank, HS * rank + HS), sem)
+    quant("WQ", 0, 128, "TW", 0)
     arrives([R("NL")], "anum", whole)
     for t in range(2):
         total_of(R("RES", t, t + 1), R("NL", t, 14, step=2))
@@ -568,7 +563,7 @@ def rank_program(g, core, T, topo):
         dma("y", None, R("RES", 2 + t, 3 + t, 0, 64), outap=T.lw[t:t + 1, :])
         dma("y", None, R("RES", 2 + t, 3 + t, 64, 128), outap=T.sw[t:t + 1, :])
     for s, sem in (("", "awc"), ("s", "aws")):
-        arrives([R("WIN2" + s, a, b) for a, b in ((0, HS * rank), (HS * rank + HS, K)) if a < b], sem, part)
+        arrives([R("WIN2" + s, a, b) for a, b in others], sem, part)
     renew(2, K + 128 + 2 * P)
 
     for h in range(2):
@@ -581,7 +576,8 @@ def rank_program(g, core, T, topo):
         copy("sv"[h], R("YO", 128 * h, 128 * h + 128), R("pD", 512 * h, 512 * h + 128))
     for k in range(4):
         dma("y", None, R("LX3s", 0, P, 32 * k, 32 * k + 4), outap=T.osc[4 * k:4 * k + 4, 0:P])
-    dma("s", None, R("YO"), outap=T.y[:, :])
+    for h in range(2):
+        dma("sy"[h], None, R("YO", 128 * h, 128 * h + 128), outap=T.y[:, 128 * h:128 * h + 128])
     for sem in total:
         if known["g"].get(sem, 0) < total[sem]:
             g.wait_ge(T.sem[sem], total[sem])

@@ -28,17 +28,17 @@ def _pool(name, d, parts):
 
 
 for _n, _w in (("TL", 1024), ("TX", 1024), ("TN", 1024), ("TW", 512), ("U4", 4), ("Z4", 4), ("UT", 1024), ("ZT", 1024), ("ONE", 192),
-               ("ZB", 512), ("CO", 1536), ("WT", 2816), ("ET", 2048), ("EYE", 128), ("CTL", 1024), ("CTX", 1024), ("OT", 768), ("HT", 512),
+               ("ZB", 192), ("CO", 512), ("WT", 2816), ("ET", 2048), ("EYE", 128), ("CT", 1024), ("OT", 768), ("HT", 512),
                ("MSK", 256), ("DS", 512)):
     _sb(_n, _w, "bfloat16")
 _pool("BB", "bfloat16", (("EQK", 256), ("MM", 448), ("EQ", 256), ("EQN", 64)))
 _pool("FC", "float32", (("CC", 16), ("IROW", 64), ("N16", 128), ("M16", 128), ("CROW", 4), ("KC", 4), ("CW8", 8), ("HALF", 1), ("B28", 28),
-                        ("WC", 1), ("VX", 1), ("IC", 2), ("SGN", 32), ("DCOL", 1), ("BROW", 128), ("ROWI", 512)))
+                        ("WC", 1), ("VX", 1), ("IC", 2), ("SGN", 32), ("DCOL", 1), ("BROW", 1)))
 _pool("FD", "float32", (("AC", 4), ("RLA", 256), ("RXA", 256)))
-_pool("FB", "float32", (("PRD", 256), ("JK", 1088), ("PM", 128), ("P64", 64), ("P32", 32), ("P16", 16), ("P8", 8), ("K1S", 1), ("OKC", 2),
+_pool("FB", "float32", (("PRD", 256), ("JK", 768), ("PM", 128), ("P8", 8), ("K1S", 1), ("OKC", 2), ("D0", 64),
                         ("KR", 224), ("KW", 224), ("XC", 2), ("XR", 64), ("Y", 64), ("TY", 64), ("GS", 64), ("G", 128), ("MU", 256), ("FS", 4),
-                        ("SW", 4), ("FLD", 8), ("FM", 4), ("FO", 8), ("FP", 8), ("VT", 128), ("VM", 128), ("VU", 128), ("PN", 64), ("NA", 2),
-                        ("NB", 2), ("V28", 28), ("V29", 28), ("W12", 12), ("W4", 8), ("W5", 4), ("AB", 8), ("V8", 8), ("VS", 1), ("HL8", 8)))
+                        ("SW", 4), ("FLD", 8), ("FM", 4), ("FO", 8), ("FP", 8), ("VT", 64), ("VM", 64), ("VU", 64), ("VV", 64), ("PN", 64),
+                        ("NA", 2), ("NB", 2), ("V28", 28), ("V29", 28), ("W5", 4), ("AB", 8), ("V8", 8), ("VS", 1), ("HL8", 8)))
 for _n, _w in (("NUM", 2), ("NL", 14), ("RES", 4), ("YO", 256)):
     _sb(_n, _w, "float32")
 for _t in "12":
@@ -53,8 +53,8 @@ for _t in "12":
     _codes("N" + _t, 128)
 _sb("PI", 1, "int32")
 _sb("II", 5, "int32")
-for _n, _w in (("UQ", 256), ("ZQ", 256), ("LX1", 512), ("LX2", 512), ("LX3", 512), ("NQ", 256), ("WQ", 128), ("COQ", 384), ("WTQ", 704), ("EC", 512),
-               ("CQL", 256), ("CQX", 256), ("OQ", 192), ("WIN1", PEERS * K + 2 * P), ("WIN2", K + 128 + 2 * P), ("HW", 32 + K)):
+for _n, _w in (("UQ", 256), ("ZQ", 256), ("LX1", 512), ("LX2", 512), ("LX3", 512), ("NQ", 256), ("WQ", 128), ("COQ", 128), ("WTQ", 704), ("EC", 512),
+               ("CQ", 256), ("OQ", 192), ("WIN1", PEERS * K + 2 * P), ("WIN2", K + 128 + 2 * P), ("HW", 32 + K)):
     _codes(_n, _w)
 PSUM = {"pA": 1, "pB": 1, "pC": 1, "pD": 4, "pE": 1}
 for _n in PSUM:
@@ -184,8 +184,9 @@ def rank_program(g, core, T, topo):
     def turn(out, in_):
         run("v", lambda: g.vector.transpose(A(out), A(in_)), [in_], [out])
 
-    def total_of(out, in_):
-        run("v", lambda: g.vector.tensor_reduce(A(out), A(in_), AxisListType.X, ADD), [in_], [out])
+    def total_of(out, in_, sizes=False):
+        kw = {"apply_absolute_value": True} if sizes else {}
+        run("v", lambda: g.vector.tensor_reduce(A(out), A(in_), AxisListType.X, ADD, **kw), [in_], [out])
 
     def quant(out, c, n, tile, e):
         o, s, i = R(out, c, c + n), R(out + "s", c, c + n), R(tile, 4 * e, 4 * e + 4 * n)
@@ -255,56 +256,47 @@ def rank_program(g, core, T, topo):
     dma("y", R("TX"), None, inap=T.dm[:, :])
     dma("y", R("TL"), None, inap=T.lv[:, :])
     iota(R("PI"), [[0, 1]], 0, 1)
+    iota(R("WT", 4 * 448, 4 * 704), [[0, 4 * 256]], 1, 0)
+    memset(R("ZB"), 0.0)
+    memset(R("ZT", 0, 256), 0.0)
     memset(R("MSK", 0, 128), 0.5)
     memset(R("MSK", 128, 256), -0.5)
-    choose(R("MSK", 0, 128), [[1, 128]], GT, -0.5, -1)
     choose(R("MSK", 128, 256), [[1, 128]], GT, 0.5, -1)
-    memset(R("ZB"), 0.0)
+    choose(R("MSK", 0, 128), [[1, 128]], GT, -0.5, -1)
     memset(R("ONE"), 1.0)
-    memset(R("EYE"), 0.5)
-    iota(R("CROW"), [[16, 4]], 0, 0)
-    iota(R("B28"), [[K, PEERS], [16, 4]], 0, 0)
-    iota(R("IROW"), [[1, 64]], 0, 0)
-    iota(R("N16"), [[0, 8], [1, 16]], 0, 0)
-    for a, b in ((64, 192), (256, 384), (448, 704)):
-        iota(R("WT", 4 * a, 4 * b), [[0, 4 * (b - a)]], 1, 0)
-    choose(R("EYE"), [[-1, 128]], EQL, 0.0, 1)
-    iota(R("ROWI"), [[256, 2], [1, 16], [16, 16]], 1, 0)
-    for c0, c1, v in ((0, 256, 1.0), (256, 768, 0.0), (768, 1536, 1.0)):
-        memset(R("CO", c0, c1), v)
     memset(R("UT", 768, 1024), 0.0)
-    memset(R("ZT", 0, 256), 0.0)
     for i, (op, v) in enumerate(((AluOpType.bitwise_and, 15), (AluOpType.arith_shift_right, 4), (AluOpType.bitwise_and, 63),
                                  (AluOpType.bitwise_and, 31), (AluOpType.bitwise_and, 7))):
         ts(R("II", i, i + 1), R("PI"), v, op)
-    for b in range(4):
-        copy("s", R("ET", 512 * b, 512 * b + 512), R("ZB"))
-    for a in (0, 192, 384):
-        memset(R("WT", 4 * a, 4 * a + 256), 0.0)
+    memset(R("CO"), 0.0)
+    for c in (0, 1, 258, 259):
+        memset(R("CO", c, c // 256 * 256 + 256, step=4), 1.0)
     copy("v", R("CC", 0, 5), R("II"))
     Q16, TGT = R("CC", 0, 1), R("CC", 2, 3)
-    memset(R("OT"), 0.0)
+    iota(R("CROW"), [[16, 4]], 0, 0)
+    iota(R("N16"), [[0, 8], [1, 16]], 0, 0)
+    for a in (64, 256):
+        iota(R("WT", 4 * a, 4 * a + 512), [[0, 512]], 1, 0)
+    iota(R("IROW"), [[1, 64]], 0, 0)
+    iota(R("B28"), [[K, PEERS], [16, 4]], 0, 0)
+    for t in range(4):
+        act(R("ZT", 256 + t, 1024, step=4), R("ZB"), AF.Identity, bias=R("Z4", t, t + 1))
+        ts(R("UT", t, 768, step=4), R("ONE"), R("U4", t, t + 1), MUL)
+    quant("UQ", 0, 256, "UT", 0)
+    quant("ZQ", 0, 256, "ZT", 0)
+    quant("LX1", P, P, "TX", 0)
+    ts(R("CC", 8, 9), R("CC", 0, 1), 16.0, MUL)
+    ts(R("CC", 9, 10), R("CC", 1, 2), 8.0, ADD)
+    quant("COQ", 0, 128, "CO", 0)
+    for m, b, c in ((448, 0, 8), (448, 1, 8), (576, 0, 1), (576, 1, 9)):
+        act(R("WT", 4 * m + b, 4 * m + 512, step=4), R("ZB", 0, 128), AF.Identity, bias=R("CC", c, c + 1))
+    quant("LX1", 0, P, "TL", 0)
     ts(R("CC", 5, 6), R("CC", 0, 1), 1.0, ADD)
     ts(R("CC", 6, 7), R("CC", 1, 2), 16.0, MUL)
     ts(R("CC", 7, 8), R("CC", 1, 2), 16.0, MUL, 128.0, ADD)
-    ts(R("CC", 8, 9), R("CC", 0, 1), 16.0, MUL)
-    ts(R("CC", 9, 10), R("CC", 1, 2), 8.0, ADD)
-    memset(R("OT", 258, 512, step=4), 1.0)
-    ts(R("KC"), R("CROW"), Q16, ADD)
-    ts(R("HALF"), Q16, 8.0, GE if rank % 2 else LT, float(64 + 16 * rank - 16 * ch), MUL)
-    ts(R("WC"), R("CC", 4, 5), float(HS * rank + 1), ADD)
-    ts(R("VX"), Q16, float(16 * (ch % 2) - 31), ADD)
-    for t in range(4):
-        ts(R("UT", t, 768, step=4), R("ONE"), R("U4", t, t + 1), MUL)
-        act(R("ZT", 256 + t, 1024, step=4), R("ZB", 0, 192), AF.Identity, bias=R("Z4", t, t + 1))
-    quant("ZQ", 0, 256, "ZT", 0)
-    quant("UQ", 0, 256, "UT", 0)
-    quant("LX1", P, P, "TX", 0)
-    for ct in ("CTX", "CTL"):
-        memset(R(ct, 2, 1024, step=4), 0.0)
-        memset(R(ct, 3, 1024, step=4), 0.0)
-    quant("COQ", 0, 384, "CO", 0)
-    quant("LX1", 0, P, "TL", 0)
+    for a in (0, 192, 384):
+        memset(R("WT", 4 * a, 4 * a + 256), 0.0)
+    memset(R("EYE"), 0.5)
     dmaq("y", "WIN1", PEERS * K, "LX1", 0, 2 * P)
     dma("y", R("TN"), None, inap=T.nz[:, :])
 
@@ -328,81 +320,77 @@ def rank_program(g, core, T, topo):
         for typ in "XL":
             bk, d0, m0 = (2, 256, 128) if typ == "X" else (0, 0, 0)
             lo, le, on = (LT, LE, GT) if typ == "X" else (GT, GE, LT)
-            row, ct = "R%sA" % typ, "CT" + typ
-            ts(R(ct, 512, 1024, step=4), R(row, 128, 256), R("AC", bk, bk + 1), le)
-            ts(R(ct, 1, 512, step=4), R(row, 0, 128), R("AC", bk + 1, bk + 2), lo)
+            row = "R%sA" % typ
+            ts(R("CT", 512 + bk, 1024, step=4), R(row, 128, 256), R("AC", bk, bk + 1), le)
+            ts(R("CT", bk + 1, 512, step=4), R(row, 0, 128), R("AC", bk + 1, bk + 2), lo)
             for h in range(2):
-                tt(R(ct, 513 * h, 512 * h + 512, step=4), R("DS", d0 + 128 * h, d0 + 128 * h + 128), R("MSK", m0, m0 + 128), on)
-            quant("CQ" + typ, 0, P, ct, 0)
-        mm("pE", 0, "COQ", 128, "CQX", 0, P, True, False)
-        mm("pE", 0, "COQ", 0, "CQL", 0, P, False, True)
+                tt(R("CT", 513 * h + bk, 512 * h + 512, step=4), R("DS", d0 + 128 * h, d0 + 128 * h + 128), R("MSK", m0, m0 + 128), on)
+            if t == 1 and typ == "X":
+                for p in (0, 64):
+                    memset(R("SGN", p0=p, p1=p + 64), -1.0 if p else 1.0)
+        quant("CQ", 0, P, "CT", 0)
+        mm("pE", 0, "COQ", 0, "CQ", 0, P)
+        if t == 1:
+            memset(R("OT"), 0.0)
+            memset(R("OT", 258, 512, step=4), 1.0)
+            quant("WTQ", 448, 256, "WT", 448)
+            for m, b, c in ((64, 0, 5), (64, 1, 5), (256, 0, 6), (256, 1, 7)):
+                act(R("WT", 4 * m + b, 4 * m + 512, step=4), R("ZB", 0, 128), AF.Identity, bias=R("CC", c, c + 1))
         for h in range(2):
             ts(R("EQK", 128 * h, 128 * h + 128), R("pE", 128 * h, 128 * h + 128), TGT, EQL)
         for h in range(2):
             tt(R("PRD", 128 * h, 128 * h + 128), R("EQK", 128 * h, 128 * h + 128), R("pC", 128 * h, 128 * h + 128), MUL)
-        if t == 1:
-            for m, b, c in ((448, 0, 8), (448, 1, 8), (576, 0, 1), (576, 1, 9), (64, 0, 5), (64, 1, 5), (256, 0, 6), (256, 1, 7)):
-                act(R("WT", 4 * m + b, 4 * m + 512, step=4), R("ZB", 0, 128), AF.Identity, bias=R("CC", c, c + 1))
-        act(R("JK", 0, P), R("PRD"), AF.Abs, acc=R(k1))
+        total_of(R(k1), R("PRD"), True)
         to_all(R(k1), lambda r: R("KL%d" % t, slot_at(r), slot_at(r) + 1), "ak%d" % t)
 
-    def small_constants():
-        out = [lambda: ts(R("M16"), R("N16"), Q16, EQL), lambda: ts(R("B28"), R("B28"), Q16, ADD)]
+    def early_constants():
+        ts(R("KC"), R("CROW"), Q16, ADD)
+        ts(R("M16"), R("N16"), Q16, EQL)
         for p in (0, 64):
-            out.append(lambda p=p: copy("v", R("IC", 0, 1, p, p + 32), R("CC", 3, 4, p, p + 32)))
-            out.append(lambda p=p: ts(R("IC", 1, 2, p, p + 32), R("CC", 3, 4, p, p + 32), 32.0, ADD))
-            out.append(lambda p=p: memset(R("IC", 0, 2, p + 32, p + 64), 0.0))
-        out += [lambda: memset(R("DCOL", p1=64), float(P * rank - 1)), lambda: memset(R("DCOL", p0=64), float(P * rank - 1 - P)),
-                lambda: memset(R("BROW", 0, 64), float(2 * P + K + 1)), lambda: memset(R("BROW", 64, 128), float(2 * P + 1))]
-        return out
+            copy("v", R("IC", 0, 1, p, p + 32), R("CC", 3, 4, p, p + 32))
+            ts(R("IC", 1, 2, p, p + 32), R("CC", 3, 4, p, p + 32), 32.0, ADD)
+            memset(R("IC", 0, 2, p + 32, p + 64), 0.0)
+            memset(R("BROW", p0=p, p1=p + 64), float(2 * P + 1 if p else 2 * P + K + 1))
+
+    def late_constants():
+        ts(R("HALF"), Q16, 8.0, GE if rank % 2 else LT, float(64 + 16 * rank - 16 * ch), MUL)
+        ts(R("WC"), R("CC", 4, 5), float(HS * rank + 1), ADD)
+        ts(R("VX"), Q16, float(16 * (ch % 2) - 31), ADD)
+        memset(R("DCOL", p1=64), float(P * rank - 1))
+        memset(R("DCOL", p0=64), float(P * rank - 1 - P))
+        for c in (0, 4):
+            copy("v", R("CW8", c, c + 4), R("KC"))
+        for c in (0, 4):
+            tt(R("CW8", c + ch, c + ch + 1), R("KC", ch, ch + 1), R("HALF"), ADD)
 
     def post(t):
-        for typ in "XL":
-            bk = 2 if typ == "X" else 0
-            for h in range(2):
-                mm("pD", bk + h, "CQ" + typ, 128 * h, "COQ", 256, 128)
+        for h in range(2):
+            mm("pD", h, "CQ", 128 * h, "COQ", 0, 128)
+        iota(R("ROW%d" % t), [[256, 2], [1, 16], [16, 16]], 1, 0)
         if t == 1:
-            memset(R("SGN", p1=64), 1.0)
-            memset(R("SGN", p0=64), -1.0)
-            quant("WTQ", 448, 256, "WT", 448)
-        for c, bk in ((256, 2), (0, 0)):
+            choose(R("EYE"), [[-1, 128]], EQL, 0.0, 1)
+            iota(R("ET", 0, 1024), [[0, 1024]], 0, 0)
+        for c in (256, 0):
             for h in range(2):
-                ts(R("OT", c + h, c + 256, step=4), R("IROW"), R("pD", 512 * (bk + h), 512 * (bk + h) + 1), EQL)
-        quant("OQ", 0, 192, "OT", 0)
+                ts(R("OT", c + h, c + 256, step=4), R("IROW"), R("pD", 512 * h + c // 4, 512 * h + c // 4 + 1), EQL)
         tt(R("K1S"), R("K1_%d" % t), R("SGN", 0, 1), MUL)
+        quant("OQ", 0, 192, "OT", 0)
         for c, s, d in ((0, 0, 0), (0, 0, 32), (0, 64, 64), (0, 64, 96), (1, 32, 0), (1, 32, 32), (1, 96, 64), (1, 96, 96)):
             copy("s", R("OKC", c, c + 1, d, d + 32), R("K1S", 0, 1, s, s + 32))
-        copy("s", R("ROW%d" % t), R("ROWI"))
         if t == 1:
-            for b in range(4):
-                copy("s", R("ET", 512 * b + b, 512 * b + 512, step=4), R("EYE"))
             quant("WTQ", 0, 448, "WT", 0)
         mm("pB", 0, "WTQ", 448, "OQ", 0, 128, True, False)
         mm("pB", 0, "WTQ", 576, "OQ", 0, 128, False, True)
         for i, (c, d) in enumerate(((128, 0), (320, 0), (0, 64), (192, 64))):
             mm("pC", 0, "WTQ", c, "OQ", d, 128, i == 0, i == 3)
-        mm("pA", 0, "WTQ", 64, "OQ", 0, 128, True, False)
-        mm("pA", 0, "WTQ", 256, "OQ", 0, 128, False, True)
-        fill = small_constants() if t == 1 else []
-
-        def some(n):
-            for _ in range(n):
-                if fill:
-                    fill.pop(0)()
         if t == 1:
-            quant("NQ", 0, P, "TN", 0)
-        some(2)
+            early_constants()
         tt(R("PM"), R("M16"), R("pB", 0, 128), MUL)
-        some(2)
-        tt(R("P64"), R("PM", 0, 128, step=2), R("PM", 1, 128, step=2), ADD)
-        some(2)
-        tt(R("P32"), R("P64", 0, 64, step=2), R("P64", 1, 64, step=2), ADD)
-        some(2)
-        tt(R("P16"), R("P32", 0, 32, step=2), R("P32", 1, 32, step=2), ADD)
-        some(2)
-        tt(R("P8"), R("P16", 0, 16, step=2), R("P16", 1, 16, step=2), ADD)
-        some(9)
-        ts(R("PIU%d" % t), R("P8"), 0.0, ADD)
+        if t == 1:
+            for b in (2, 3):
+                memset(R("ET", 512 * b, 512 * b + 512), 0.0)
+        else:
+            list_numbers(1)
 
     def merge(t):
         kl = "KL%d" % t
@@ -414,41 +402,60 @@ def rank_program(g, core, T, topo):
                 dmaq("y", w, K, "LX1", 0, K)
             dmaq("y", "HW", 32 + HS * rank, "LX1", 0, HS)
             dma("y", R("TW"), None, inap=T.w[:, :])
+        rest = [lambda c=c: total_of(R("P8", c, c + 1), R("PM", 16 * c, 16 * c + 16)) for c in range(8)]
+        rest.append(lambda: ts(R("D0"), R("pC", 0, 64), -1.0, MUL, R("BROW"), ADD))
+        rest.append(lambda: ts(R("PIU%d" % t), R("P8"), 0.0, ADD))
+
+        def fill(n=1):
+            for _ in range(n):
+                if rest:
+                    rest.pop(0)()
         for s in range(PEERS):
             o, kc = R("KR", 32 * s, 32 * s + 32), R(kl, s, s + 1)
-            if s % 2:
+            if s in (1, 3):
                 act(o, R("SGN"), AF.Copy, scale=kc)
             else:
                 ts(o, R("SGN"), kc, MUL)
+        fill()
         turn(R("KW"), R("KR"))
+        fill()
         for m in range(2):
             own = R("OKC", m, m + 1)
             if rank:
                 ts(R("MM", 224 * m, 224 * m + 32 * rank), R("KW", 0, 32 * rank), own, LE)
             if rank < PEERS:
                 ts(R("MM", 224 * m + 32 * rank, 224 * m + 224), R("KW", 32 * rank, 224), own, LT)
-            act(R("JK", 256 + 224 * m, 480 + 224 * m), R("MM", 224 * m, 224 * m + 224), AF.Copy, acc=R("XC", m, m + 1))
-        for m in range(2):
+            if m == 0:
+                act(R("JK", 256, 480), R("MM", 0, 224), AF.Copy, acc=R("XC", 0, 1))
+            else:
+                fill()
+                total_of(R("XC", 1, 2), R("MM", 224, 448))
+                fill()
+        for m in (1, 0):
             ts(R("XR", 32 * m, 32 * m + 32), R("ONE", 0, 32), R("XC", m, m + 1), MUL, R("IC", m, m + 1), ADD)
+        fill()
         turn(R("Y"), R("XR"))
-        copy("s", R("TY", p0=32, p1=64), R("Y", p0=0, p1=32))
-        copy("v", R("TY", p0=0, p1=32), R("Y", p0=32, p1=64))
-        copy("s", R("TY", p0=96, p1=128), R("Y", p0=64, p1=96))
-        copy("v", R("TY", p0=64, p1=96), R("Y", p0=96, p1=128))
+        fill()
+        for p in (32, 0, 96, 64):
+            o = p - 32 if p % 64 else p + 32
+            copy("v", R("TY", p0=p, p1=p + 32), R("Y", p0=o, p1=o + 32))
+        fill()
         tt(R("GS"), R("Y"), R("TY"), ADD)
-        for step in "e0 e1 m0 e2 m1 e3 m2 m3".split():
+        for step in "e0 e1 m0 m1 e2 e3 m2 m3".split():
             c = int(step[1])
             e, u = R("EQ", 64 * c, 64 * c + 64), R("MU", 64 * c, 64 * c + 64)
             if step[0] == "e":
                 ts(e, R("GS"), R("KC", c, c + 1), EQL)
                 continue
             tt(u, e, R("pC", 0, 64), MUL)
-            if c == 3:
-                total_of(R("FS", 3, 4), u)
+            if c >= 2:
+                total_of(R("FS", c, c + 1), u)
             else:
                 act(R("JK", 512 + 64 * c, 576 + 64 * c), u, AF.Copy, acc=R("FS", c, c + 1))
-        copy("s", R("SW", p0=64), R("FS", p1=64))
+        fill()
+        copy("v", R("SW", p0=64), R("FS", p1=64))
         copy("v", R("SW", p1=64), R("FS", p0=64))
+        fill()
         tt(R("FM"), R("FS"), R("SW"), MAX)
         ts(R("ZU%d" % t), R("FM"), -1.0, ADD)
         if t == 1:
@@ -456,39 +463,44 @@ def rank_program(g, core, T, topo):
         else:
             ts(R("INFO2"), R("FM"), 0.0, GT, R("WC"), MUL)
         pick("Z%d" % t, 0, "LX%d" % t, 2 * P, "ZU%d" % t, 0, 4)
+        fill(9)
         to_all(R("INFO%d" % t), lambda r: R("IL%d" % t, 4 * slot_at(r), 4 * slot_at(r) + 4), "ai%d" % t)
 
-    def lists(t, base):
-        a, b = t - 1, t
-        ts(R("EQN"), R("GS"), TGT, EQL)
-        for q, o, i in (("v", R("FLD", 0, 4, 0, 64), R("FS", p1=64)), ("s", R("FLD", 0, 4, 64, 128), R("FS", p1=64)),
-                        ("v", R("FLD", 4, 8, 64, 128), R("FS", p0=64)), ("s", R("FLD", 4, 8, 0, 64), R("FS", p0=64)),
-                        ("v", R("G", 0, 64, 0, 64), R("GS", p1=64)), ("s", R("G", 0, 64, 64, 128), R("GS", p1=64)),
-                        ("v", R("G", 64, 128, 64, 128), R("GS", p0=64)), ("s", R("G", 64, 128, 0, 64), R("GS", p0=64))):
-            copy(q, o, i)
-        tt(R("PN"), R("EQN"), R("pC", 0, 64), MUL)
-        act(R("JK", 1024, 1088), R("PN"), AF.Copy, acc=R("NA", a, b))
-        tt(R("VT"), R("G"), R("BROW"), ADD)
-        ts(R("VM"), R("G"), float(K), LT)
-        ts(R("NB", a, b), R("NA", a, b), 0.0, GT, R("DCOL"), MUL)
-        tt(R("VU"), R("VT"), R("pA", 0, 128), SUB)
-        ts(R("FP"), R("FLD"), 0.0, GT, float(base - 1), MUL)
-        tt(R("NUM", a, b), R("NB", a, b), R("NA", a, b), ADD)
-        if t == 2:
-            to_all(R("NUM"), lambda r: R("NL", 2 * slot_at(r), 2 * slot_at(r) + 2), "anum")
-        tt(R("VT"), R("VU"), R("VM"), MUL)
-        tt(R("FO"), R("FP"), R("FLD"), ADD)
-        tt(R("VU"), R("VT"), R("pA", 0, 128), ADD)
+    def list_places(t):
         row, off = R("ROW%d" % t), R("PIU%d" % t)
-        run("v", lambda: g.vector.tensor_copy(A(row).indirect(A(off)), A(R("VU"))), [R("VU"), off], [row])
+        ts(R("VM"), R("GS"), float(K), LT)
+        tt(R("VT"), R("GS"), R("D0"), ADD)
+        tt(R("VU"), R("VT"), R("VM"), MUL)
+        tt(R("VV"), R("VU"), R("pC", 0, 64), ADD)
+        for c, p in ((0, 0), (0, 64), (64, 64), (64, 0)):
+            copy("v", R("G", c, c + 64, p, p + 64), R("VV", p0=c, p1=c + 64))
+        run("v", lambda: g.vector.tensor_copy(A(row).indirect(A(off)), A(R("G"))), [R("G"), off], [row])
         for k in range(2):
             dma("y", R("LST%d" % t, 16 * k, 16 * k + 16), R("ROW%d" % t, 256 * k, 256 * k + 256, 0, 8))
+
+    def list_slots(t, base):
+        for c, p in ((0, 0), (0, 64), (4, 64), (4, 0)):
+            copy("s", R("FLD", c, c + 4, p, p + 64), R("FS", p0=16 * c, p1=16 * c + 64))
         ts(R("NU%d" % t), R("FLD", 0, 4), -1.0, ADD)
+        ts(R("FP"), R("FLD"), 0.0, GT, float(base - 1), MUL)
         pick("N%d" % t, 0, "NQ", P, "NU%d" % t, 0, 4)
+        tt(R("FO"), R("FP"), R("FLD"), ADD)
         if t == 1:
             quant("EC", 0, 512, "ET", 0)
         for k in range(4):
             mm("pD", k, "EC", 128 * k, "N%d" % t, 0, 128, True, False)
+
+    def list_own(t):
+        ts(R("EQN"), R("GS"), TGT, EQL)
+        tt(R("PN"), R("EQN"), R("pC", 0, 64), MUL)
+
+    def list_numbers(t):
+        a, b = t - 1, t
+        total_of(R("NA", a, b), R("PN"))
+        ts(R("NB", a, b), R("NA", a, b), 0.0, GT, R("DCOL"), MUL)
+        tt(R("NUM", a, b), R("NB", a, b), R("NA", a, b), ADD)
+        if t == 2:
+            to_all(R("NUM"), lambda r: R("NL", 2 * slot_at(r), 2 * slot_at(r) + 2), "anum")
 
     def renew(t, width):
         win, lxv, nxt, lab = "WIN%d" % t, "LXV%d" % t, "LX%d" % (t + 1), "LAB%d" % t
@@ -508,21 +520,26 @@ def rank_program(g, core, T, topo):
     merge(1)
     to_all(R("Z1"), lambda r: R("WIN1", K * slot_at(r), K * slot_at(r) + K), "azc")
     to_all(R("Z1s"), lambda r: R("WIN1s", K * slot_at(r), K * slot_at(r) + K), "azs")
-    lists(1, PEERS * K)
+    for b in range(4):
+        copy("s", R("ET", 512 * b + b, 512 * b + 512, step=4), R("EYE"))
+    list_places(1)
+    quant("NQ", 0, P, "TN", 0)
+    ts(R("B28"), R("B28"), Q16, ADD)
+    list_slots(1, PEERS * K)
     arrives([R("IL1")], "ai1", whole)
     ts(R("V28"), R("IL1"), 0.0, GT)
     tt(R("V29"), R("V28"), R("B28"), MUL)
-    tt(R("W12"), R("V29", 0, 12), R("V29", 12, 24), MAX)
-    tt(R("W4", 0, 4), R("W12", 0, 4), R("W12", 4, 8), MAX)
-    tt(R("W4", 4, 8), R("W12", 8, 12), R("V29", 24, 28), MAX)
-    tt(R("W5"), R("W4", 0, 4), R("W4", 4, 8), MAX)
+    for c in range(4):
+        total_of(R("W5", c, c + 1), R("V29", c, 28, step=4))
     for k in (1, 0):
         tt(R("AB", 4 * k, 4 * k + 4), R("FO", 4 * k, 4 * k + 4), R("W5"), MAX)
     ts(R("LAB1"), R("AB"), 0.0, ADD)
     memset(R("HT", 256, 512), 0.0)
+    list_own(1)
     arrives([R("WIN1", 0, PEERS * K)], "azc", whole)
     arrives([R("WIN1s", 0, PEERS * K)], "azs", whole)
     renew(1, PEERS * K + 2 * P)
+    late_constants()
 
     local(2)
     dmaq("y", "WIN2", K + 128, "LX2", 0, 2 * P)
@@ -533,12 +550,7 @@ def rank_program(g, core, T, topo):
         to_each(lambda r: R("Z2" + s, HS * r, HS * r + HS), lambda r: R("HW" + s, 32 + HS * rank, 32 + HS * rank + HS), sem)
     pick("HW", 0, "LX2", 2 * P, "ZU2", ch // 2 * 2, ch // 2 * 2 + 2)
     ts(R("V8", rank, rank + 1), R("FM", ch, ch + 1), 0.0, GT, R("VX"), MUL)
-    lists(2, K + 128)
-    for c in (0, 4):
-        copy("v", R("CW8", c, c + 4), R("KC"))
-        tt(R("CW8", c + ch, c + ch + 1), R("KC", ch, ch + 1), R("HALF"), ADD)
-    tt(R("AB"), R("FO"), R("CW8"), MAX)
-    ts(R("LAB2"), R("AB"), 0.0, ADD)
+    list_places(2)
     arrives([R("IL2")], "ai2", whole)
     if rank:
         ts(R("V8", 0, rank), R("IL2", ch, 4 * rank, step=4), 0.0, ADD)
@@ -554,14 +566,12 @@ def rank_program(g, core, T, topo):
     hc = K + HS * (rank % 2)
     for s, sem in (("", "awc"), ("s", "aws")):
         to_each(lambda r: R("WIN2" + s, hc + 16 * r, hc + 16 * r + HS), lambda r: R("WIN2" + s, HS * rank, HS * rank + HS), sem)
+    list_slots(2, K + 128)
+    tt(R("AB"), R("FO"), R("CW8"), MAX)
+    ts(R("LAB2"), R("AB"), 0.0, ADD)
+    list_own(2)
+    list_numbers(2)
     quant("WQ", 0, 128, "TW", 0)
-    arrives([R("NL")], "anum", whole)
-    for t in range(2):
-        total_of(R("RES", t, t + 1), R("NL", t, 14, step=2))
-    tt(R("RES", 2, 4), R("RES", 0, 2), R("NUM"), ADD)
-    for t in range(2):
-        dma("y", None, R("RES", 2 + t, 3 + t, 0, 64), outap=T.lw[t:t + 1, :])
-        dma("y", None, R("RES", 2 + t, 3 + t, 64, 128), outap=T.sw[t:t + 1, :])
     for s, sem in (("", "awc"), ("s", "aws")):
         arrives([R("WIN2" + s, a, b) for a, b in others], sem, part)
     renew(2, K + 128 + 2 * P)
@@ -571,13 +581,20 @@ def rank_program(g, core, T, topo):
     dma("y", None, R("LX3", P, 2 * P), outap=T.oc[:, 4 * P:8 * P])
     for k in range(4):
         dma("y", None, R("LX3s", P, 2 * P, 32 * k, 32 * k + 4), outap=T.osc[4 * k:4 * k + 4, P:2 * P])
+    arrives([R("NL")], "anum", whole)
+    for t in range(2):
+        total_of(R("RES", t, t + 1), R("NL", t, 14, step=2))
+    tt(R("RES", 2, 4), R("RES", 0, 2), R("NUM"), ADD)
     dma("y", None, R("LX3", 0, P), outap=T.oc[:, 0:4 * P])
     for h in range(2):
         copy("sv"[h], R("YO", 128 * h, 128 * h + 128), R("pD", 512 * h, 512 * h + 128))
     for k in range(4):
         dma("y", None, R("LX3s", 0, P, 32 * k, 32 * k + 4), outap=T.osc[4 * k:4 * k + 4, 0:P])
-    for h in range(2):
-        dma("sy"[h], None, R("YO", 128 * h, 128 * h + 128), outap=T.y[:, 128 * h:128 * h + 128])
+    dma("s", None, R("YO", 0, 128), outap=T.y[:, 0:128])
+    for t in range(2):
+        dma("s", None, R("RES", 2 + t, 3 + t, 0, 64), outap=T.lw[t:t + 1, :])
+        dma("s", None, R("RES", 2 + t, 3 + t, 64, 128), outap=T.sw[t:t + 1, :])
+    dma("y", None, R("YO", 128, 256), outap=T.y[:, 128:256])
     for sem in total:
         if known["g"].get(sem, 0) < total[sem]:
             g.wait_ge(T.sem[sem], total[sem])

@@ -27,34 +27,34 @@ def _pool(name, d, parts):
     SCRATCH[name] = ("sbuf", [128, at], d)
 
 
-for _n, _w in (("TL", 1024), ("TX", 1024), ("TN", 1024), ("TW", 512), ("U4", 4), ("Z4", 4), ("UT", 1024), ("ZT", 1024), ("ONE", 192),
-               ("ZB", 192), ("CO", 512), ("WT", 2816), ("ET", 2048), ("EYE", 128), ("CT", 1024), ("OT", 768), ("HT", 512),
+for _n, _w in (("TL", 1024), ("TX", 1024), ("TN", 1024), ("TW", 512), ("U4", 4), ("Z4", 4), ("UT", 1280), ("ONE", 128),
+               ("ZB", 128), ("CO", 512), ("WT", 2816), ("ET", 2048), ("EYE", 128), ("CT", 1024), ("OT", 768), ("HT", 512),
                ("MSK", 256), ("DS", 512)):
     _sb(_n, _w, "bfloat16")
 _pool("BB", "bfloat16", (("EQK", 256), ("MM", 448), ("EQ", 256), ("EQN", 64)))
-_pool("FC", "float32", (("CC", 16), ("IROW", 64), ("N16", 128), ("M16", 128), ("CROW", 4), ("KC", 4), ("CW8", 8), ("HALF", 1), ("B28", 28),
-                        ("WC", 1), ("VX", 1), ("IC", 2), ("SGN", 32), ("DCOL", 1), ("BROW", 1)))
+_pool("FC", "float32", (("CC", 16), ("IROW", 64), ("N16", 64), ("M16", 64), ("RB", 256), ("BDN", 1), ("BDP", 1), ("CROW", 4), ("KC", 4), ("CW8", 8),
+                        ("HALF", 1), ("WA", 1), ("WC", 1), ("VX", 1), ("IC", 2), ("SGN", 32), ("DCOL", 1), ("BROW", 1)))
 _pool("FD", "float32", (("AC", 4), ("RLA", 256), ("RXA", 256)))
-_pool("FB", "float32", (("PRD", 256), ("JK", 768), ("PM", 128), ("P8", 8), ("K1S", 1), ("OKC", 2), ("D0", 64),
-                        ("KR", 224), ("KW", 224), ("XC", 2), ("XR", 64), ("Y", 64), ("TY", 64), ("GS", 64), ("G", 128), ("MU", 256), ("FS", 4),
+_pool("FB", "float32", (("PRD", 256), ("JK", 768), ("PM", 64), ("P8", 4), ("K1S", 1), ("OKC", 2), ("D0", 64),
+                        ("KR", 224), ("KW", 224), ("XC", 2), ("XR", 64), ("Y", 64), ("TY", 64), ("GS", 64), ("MU", 256), ("FS", 4),
                         ("SW", 4), ("FLD", 8), ("FM", 4), ("FO", 8), ("FP", 8), ("VT", 64), ("VM", 64), ("VU", 64), ("VV", 64), ("PN", 64),
-                        ("NA", 2), ("NB", 2), ("V28", 28), ("V29", 28), ("W5", 4), ("AB", 8), ("V8", 8), ("VS", 1), ("HL8", 8)))
+                        ("NA", 2), ("NB", 2), ("V28", 28), ("W5", 4), ("W6", 4), ("AB", 8), ("V8", 8), ("VS", 1), ("HL8", 8)))
 for _n, _w in (("NUM", 2), ("NL", 14), ("RES", 4), ("YO", 256)):
     _sb(_n, _w, "float32")
 for _t in "12":
-    for _n, _w in (("K1_", 1), ("KL", 7), ("ROW", 512), ("LST", 32)):
+    for _n, _w in (("K1_", 1), ("KL", 7), ("ROW", 256), ("LST", 32)):
         _sb(_n + _t, _w, "float32")
     for _n, _w in (("INFO", 4), ("IL", 28)):
         _sb(_n + _t, _w, "uint16")
-    _pool("UB" + _t, "uint16", tuple((_n + _t, _w) for _n, _w in (("PIU", 8), ("ZU", 4), ("NU", 4), ("LAB", 8), ("PLU", 32), ("HLU", 8))))
+    _pool("UB" + _t, "uint16", tuple((_n + _t, _w) for _n, _w in (("PIU", 4), ("ZU", 4), ("NU", 4), ("LAB", 8), ("PLU", 32), ("HLU", 8))))
     _codes("Z" + _t, K)
     _codes("LXV" + _t, 2 * P + K + 128)
     _codes("B" + _t, 128)
     _codes("N" + _t, 128)
 _sb("PI", 1, "int32")
 _sb("II", 5, "int32")
-for _n, _w in (("UQ", 256), ("ZQ", 256), ("LX1", 512), ("LX2", 512), ("LX3", 512), ("NQ", 256), ("WQ", 128), ("COQ", 128), ("WTQ", 704), ("EC", 512),
-               ("CQ", 256), ("OQ", 192), ("WIN1", PEERS * K + 2 * P), ("WIN2", K + 128 + 2 * P), ("HW", 32 + K)):
+for _n, _w in (("UQ", 320), ("LX1", 512), ("LX2", 512), ("LX3", 512), ("NQ", 256), ("WQ", 128), ("COQ", 128), ("WTQ", 704), ("EC", 512),
+               ("CQ", 256), ("OQ", 192), ("WIN1", N * K + 2 * P), ("WIN2", K + 128 + 2 * P), ("HW", 32 + K)):
     _codes(_n, _w)
 PSUM = {"pA": 1, "pB": 1, "pC": 1, "pD": 4, "pE": 1}
 for _n in PSUM:
@@ -173,13 +173,16 @@ def rank_program(g, core, T, topo):
     def act(out, in_, f, bias=None, scale=None, acc=None):
         kw = {}
         if bias is not None:
-            kw["bias"] = A(bias)
+            kw["bias"] = A(bias) if isinstance(bias, tuple) else bias
         if scale is not None:
             kw["scale"] = A(scale) if isinstance(scale, tuple) else scale
         if acc is not None:
             kw["accum_out"] = A(acc)
         run("s", lambda: g.scalar.activation(A(out), A(in_), f, **kw), [in_] + [x for x in (bias, scale) if isinstance(x, tuple)],
             [out] + ([acc] if acc is not None else []))
+
+    def fills(r, v):
+        act(r, R("ZB", 0, r[2] - r[1], r[3], r[4]), AF.Identity, bias=float(v))
 
     def turn(out, in_):
         run("v", lambda: g.vector.transpose(A(out), A(in_)), [in_], [out])
@@ -197,11 +200,17 @@ def rank_program(g, core, T, topo):
         l, ls, r, rs = R(w, c, c + 128), R(w + "s", c, c + 128), R(x, d, d + n), R(x + "s", d, d + n)
         run("t", lambda: g.tensor.matmul_mx(A(o), A(l), A(ls), A(r), A(rs), start, stop), [l, ls, r, rs], [o], not start)
 
-    def pick(out, c, win, width, lst, e, f):
-        n = 16 * (f - e)
-        o, os_, i, is_, l = R(out, c, c + n), R(out + "s", c, c + n), R(win, 0, width), R(win + "s", 0, width), R(lst, e, f)
+    def pick_codes(out, c, win, width, lst, e, f):
+        o, i, l = R(out, c, c + 16 * (f - e)), R(win, 0, width), R(lst, e, f)
         run("v", lambda: g.vector.tensor_copy(A(o).bitcast(dt.uint32), A(i).bitcast(dt.uint32).indirect(A(l))), [i, l], [o])
-        run("s", lambda: g.scalar.activation(A(os_), A(is_).indirect(A(l)), AF.Copy), [is_, l], [os_])
+
+    def pick_scales(out, c, win, width, lst, e, f):
+        o, i, l = R(out + "s", c, c + 16 * (f - e)), R(win + "s", 0, width), R(lst, e, f)
+        run("s", lambda: g.scalar.activation(A(o), A(i).indirect(A(l)), AF.Copy), [i, l], [o])
+
+    def pick(*a):
+        pick_codes(*a)
+        pick_scales(*a)
 
     def iota(out, pattern, base, cm):
         if SCRATCH[out[0]][2] == "int32":
@@ -258,13 +267,19 @@ def rank_program(g, core, T, topo):
     iota(R("PI"), [[0, 1]], 0, 1)
     iota(R("WT", 4 * 448, 4 * 704), [[0, 4 * 256]], 1, 0)
     memset(R("ZB"), 0.0)
-    memset(R("ZT", 0, 256), 0.0)
+    for p in (0, 64):
+        fills(R("SGN", p0=p, p1=p + 64), -1.0 if p else 1.0)
+        fills(R("BROW", p0=p, p1=p + 64), 2 * P + 1 if p else 2 * P + K + 1)
+        fills(R("BDN", p0=p, p1=p + 64), -P if p else 0)
+        fills(R("BDP", p0=p, p1=p + 64), P if p else 0)
+        fills(R("DCOL", p0=p, p1=p + 64), P * rank - 1 - P if p else P * rank - 1)
+        fills(R("IC", 0, 2, p + 32, p + 64), 0.0)
     memset(R("MSK", 0, 128), 0.5)
     memset(R("MSK", 128, 256), -0.5)
     choose(R("MSK", 128, 256), [[1, 128]], GT, 0.5, -1)
     choose(R("MSK", 0, 128), [[1, 128]], GT, -0.5, -1)
     memset(R("ONE"), 1.0)
-    memset(R("UT", 768, 1024), 0.0)
+    memset(R("UT", 512, 768), 0.0)
     for i, (op, v) in enumerate(((AluOpType.bitwise_and, 15), (AluOpType.arith_shift_right, 4), (AluOpType.bitwise_and, 63),
                                  (AluOpType.bitwise_and, 31), (AluOpType.bitwise_and, 7))):
         ts(R("II", i, i + 1), R("PI"), v, op)
@@ -274,102 +289,99 @@ def rank_program(g, core, T, topo):
     copy("v", R("CC", 0, 5), R("II"))
     Q16, TGT = R("CC", 0, 1), R("CC", 2, 3)
     iota(R("CROW"), [[16, 4]], 0, 0)
-    iota(R("N16"), [[0, 8], [1, 16]], 0, 0)
+    iota(R("N16"), [[0, 4], [1, 16]], 0, 0)
     for a in (64, 256):
         iota(R("WT", 4 * a, 4 * a + 512), [[0, 512]], 1, 0)
     iota(R("IROW"), [[1, 64]], 0, 0)
-    iota(R("B28"), [[K, PEERS], [16, 4]], 0, 0)
+    iota(R("ET", 0, 512), [[0, 512]], 0, 0)
     for t in range(4):
-        act(R("ZT", 256 + t, 1024, step=4), R("ZB"), AF.Identity, bias=R("Z4", t, t + 1))
-        ts(R("UT", t, 768, step=4), R("ONE"), R("U4", t, t + 1), MUL)
-    quant("UQ", 0, 256, "UT", 0)
-    quant("ZQ", 0, 256, "ZT", 0)
+        if t < 2:
+            act(R("UT", 768 + t, 1280, step=4), R("ZB"), AF.Identity, bias=R("Z4", t, t + 1))
+        else:
+            ts(R("UT", 768 + t, 1280, step=4), R("ONE"), R("Z4", t, t + 1), MUL)
+        ts(R("UT", t, 512, step=4), R("ONE"), R("U4", t, t + 1), MUL)
+    quant("UQ", 0, 320, "UT", 0)
     quant("LX1", P, P, "TX", 0)
-    ts(R("CC", 8, 9), R("CC", 0, 1), 16.0, MUL)
-    ts(R("CC", 9, 10), R("CC", 1, 2), 8.0, ADD)
+    for o, i, m, a in ((8, 0, 16.0, 0.0), (9, 1, 1.0, 8.0), (5, 0, 1.0, 1.0), (6, 1, 16.0, 0.0), (7, 1, 16.0, 128.0)):
+        act(R("CC", o, o + 1), R("CC", i, i + 1), AF.Identity, bias=a, scale=m)
     quant("COQ", 0, 128, "CO", 0)
-    for m, b, c in ((448, 0, 8), (448, 1, 8), (576, 0, 1), (576, 1, 9)):
-        act(R("WT", 4 * m + b, 4 * m + 512, step=4), R("ZB", 0, 128), AF.Identity, bias=R("CC", c, c + 1))
     quant("LX1", 0, P, "TL", 0)
-    ts(R("CC", 5, 6), R("CC", 0, 1), 1.0, ADD)
-    ts(R("CC", 6, 7), R("CC", 1, 2), 16.0, MUL)
-    ts(R("CC", 7, 8), R("CC", 1, 2), 16.0, MUL, 128.0, ADD)
     for a in (0, 192, 384):
         memset(R("WT", 4 * a, 4 * a + 256), 0.0)
     memset(R("EYE"), 0.5)
-    dmaq("y", "WIN1", PEERS * K, "LX1", 0, 2 * P)
+    dmaq("y", "WIN1", N * K, "LX1", 0, 2 * P)
     dma("y", R("TN"), None, inap=T.nz[:, :])
+
+    def compare(typ):
+        bk, d0, m0 = (2, 256, 128) if typ == "X" else (0, 0, 0)
+        lo, le, on = (LT, LE, GT) if typ == "X" else (GT, GE, LT)
+        row = "R%sA" % typ
+        ts(R("CT", 512 + bk, 1024, step=4), R(row, 128, 256), R("AC", bk, bk + 1), le)
+        ts(R("CT", bk + 1, 512, step=4), R(row, 0, 128), R("AC", bk + 1, bk + 2), lo)
+        for h in range(2):
+            tt(R("CT", 513 * h + bk, 512 * h + 512, step=4), R("DS", d0 + 128 * h, d0 + 128 * h + 128), R("MSK", m0, m0 + 128), on)
 
     def local(t):
         lx, k1 = "LX%d" % t, "K1_%d" % t
         for typ in "XL":
             c0, bk, row, d0 = (P, 2, "pB", 256) if typ == "X" else (0, 0, "pA", 0)
-            q, qc = ("ZQ", 64) if typ == "X" else ("UQ", 0)
+            q, qc = "UQ", 192 if typ == "X" else 0
             at = (("pE", 0), ("pC", 0)) if typ == "X" else (("pD", 0), ("pD", 1))
-            for h in range(2):
-                mm(at[h][0], at[h][1], lx, c0 + 128 * h, q, qc, 128)
             mm(row, 0, q, qc, lx, c0, P)
             for h in range(2):
-                act(R("AC", bk + h, bk + h + 1), R(at[h][0], 512 * at[h][1], 512 * at[h][1] + 1), AF.Abs)
+                mm(at[h][0], at[h][1], lx, c0 + 128 * h, q, qc, 128)
             act(R("R%sA" % typ), R(row, 0, P), AF.Abs)
+            if t == 2 and typ == "X":
+                pick_scales("LX2", 0, "LXV1", 2 * P + K + 128, "PLU1", 0, 16)
+            for h in range(2):
+                total_of(R("AC", bk + h, bk + h + 1), R(at[h][0], 512 * at[h][1], 512 * at[h][1] + 1), True)
             for h in range(2):
                 act(R("DS", d0 + 128 * h, d0 + 128 * h + 128), R("R%sA" % typ, 128 * h, 128 * h + 128), AF.Sign,
                     bias=R("AC", bk + h, bk + h + 1), scale=-1.0)
-        mm("pC", 0, "UQ", 128, lx, 0, P, True, False)
-        mm("pC", 0, "ZQ", 0, lx, P, P, False, True)
-        for typ in "XL":
-            bk, d0, m0 = (2, 256, 128) if typ == "X" else (0, 0, 0)
-            lo, le, on = (LT, LE, GT) if typ == "X" else (GT, GE, LT)
-            row = "R%sA" % typ
-            ts(R("CT", 512 + bk, 1024, step=4), R(row, 128, 256), R("AC", bk, bk + 1), le)
-            ts(R("CT", bk + 1, 512, step=4), R(row, 0, 128), R("AC", bk + 1, bk + 2), lo)
-            for h in range(2):
-                tt(R("CT", 513 * h + bk, 512 * h + 512, step=4), R("DS", d0 + 128 * h, d0 + 128 * h + 128), R("MSK", m0, m0 + 128), on)
-            if t == 1 and typ == "X":
-                for p in (0, 64):
-                    memset(R("SGN", p0=p, p1=p + 64), -1.0 if p else 1.0)
+            compare(typ)
+        mm("pC", 0, "UQ", 64, lx, 0, P, True, False)
+        mm("pC", 0, "UQ", 128, lx, P, P, False, True)
         quant("CQ", 0, P, "CT", 0)
-        mm("pE", 0, "COQ", 0, "CQ", 0, P)
+        for h in range(2):
+            mm(("pE", "pA")[h], 0, "COQ", 0, "CQ", 128 * h, 128)
         if t == 1:
             memset(R("OT"), 0.0)
             memset(R("OT", 258, 512, step=4), 1.0)
-            quant("WTQ", 448, 256, "WT", 448)
-            for m, b, c in ((64, 0, 5), (64, 1, 5), (256, 0, 6), (256, 1, 7)):
+            for m, b, c in ((448, 0, 8), (448, 1, 8), (576, 0, 1), (576, 1, 9), (64, 0, 5), (64, 1, 5), (256, 0, 6), (256, 1, 7)):
                 act(R("WT", 4 * m + b, 4 * m + 512, step=4), R("ZB", 0, 128), AF.Identity, bias=R("CC", c, c + 1))
         for h in range(2):
-            ts(R("EQK", 128 * h, 128 * h + 128), R("pE", 128 * h, 128 * h + 128), TGT, EQL)
+            ts(R("EQK", 128 * h, 128 * h + 128), R(("pE", "pA")[h], 0, 128), TGT, EQL)
         for h in range(2):
             tt(R("PRD", 128 * h, 128 * h + 128), R("EQK", 128 * h, 128 * h + 128), R("pC", 128 * h, 128 * h + 128), MUL)
         total_of(R(k1), R("PRD"), True)
         to_all(R(k1), lambda r: R("KL%d" % t, slot_at(r), slot_at(r) + 1), "ak%d" % t)
 
     def early_constants():
-        ts(R("KC"), R("CROW"), Q16, ADD)
+        act(R("KC"), R("CROW"), AF.Identity, bias=Q16)
+        act(R("WA"), Q16, AF.Identity, bias=float(K * rank))
         ts(R("M16"), R("N16"), Q16, EQL)
         for p in (0, 64):
-            copy("v", R("IC", 0, 1, p, p + 32), R("CC", 3, 4, p, p + 32))
-            ts(R("IC", 1, 2, p, p + 32), R("CC", 3, 4, p, p + 32), 32.0, ADD)
-            memset(R("IC", 0, 2, p + 32, p + 64), 0.0)
-            memset(R("BROW", p0=p, p1=p + 64), float(2 * P + 1 if p else 2 * P + K + 1))
+            for m in range(2):
+                act(R("IC", m, m + 1, p, p + 32), R("CC", 3, 4, p, p + 32), AF.Identity, bias=32.0 * m)
 
     def late_constants():
         ts(R("HALF"), Q16, 8.0, GE if rank % 2 else LT, float(64 + 16 * rank - 16 * ch), MUL)
-        ts(R("WC"), R("CC", 4, 5), float(HS * rank + 1), ADD)
-        ts(R("VX"), Q16, float(16 * (ch % 2) - 31), ADD)
-        memset(R("DCOL", p1=64), float(P * rank - 1))
-        memset(R("DCOL", p0=64), float(P * rank - 1 - P))
+        act(R("WC"), R("CC", 4, 5), AF.Identity, bias=float(HS * rank + 1))
+        act(R("VX"), Q16, AF.Identity, bias=float(16 * (ch % 2) - 31))
         for c in (0, 4):
-            copy("v", R("CW8", c, c + 4), R("KC"))
+            copy("s", R("CW8", c, c + 4), R("KC"))
         for c in (0, 4):
-            tt(R("CW8", c + ch, c + ch + 1), R("KC", ch, ch + 1), R("HALF"), ADD)
+            act(R("CW8", c + ch, c + ch + 1), R("KC", ch, ch + 1), AF.Identity, bias=R("HALF"))
 
     def post(t):
         for h in range(2):
             mm("pD", h, "CQ", 128 * h, "COQ", 0, 128)
-        iota(R("ROW%d" % t), [[256, 2], [1, 16], [16, 16]], 1, 0)
         if t == 1:
+            iota(R("RB"), [[1, 16], [16, 16]], 1, 0)
             choose(R("EYE"), [[-1, 128]], EQL, 0.0, 1)
-            iota(R("ET", 0, 1024), [[0, 1024]], 0, 0)
+            iota(R("ET", 512, 1024), [[0, 512]], 0, 0)
+            for b in range(4):
+                fills(R("HT", 256 + 64 * b, 320 + 64 * b), 0.0)
         for c in (256, 0):
             for h in range(2):
                 ts(R("OT", c + h, c + 256, step=4), R("IROW"), R("pD", 512 * h + c // 4, 512 * h + c // 4 + 1), EQL)
@@ -378,6 +390,7 @@ def rank_program(g, core, T, topo):
         for c, s, d in ((0, 0, 0), (0, 0, 32), (0, 64, 64), (0, 64, 96), (1, 32, 0), (1, 32, 32), (1, 96, 64), (1, 96, 96)):
             copy("s", R("OKC", c, c + 1, d, d + 32), R("K1S", 0, 1, s, s + 32))
         if t == 1:
+            quant("WTQ", 448, 256, "WT", 448)
             quant("WTQ", 0, 448, "WT", 0)
         mm("pB", 0, "WTQ", 448, "OQ", 0, 128, True, False)
         mm("pB", 0, "WTQ", 576, "OQ", 0, 128, False, True)
@@ -385,10 +398,13 @@ def rank_program(g, core, T, topo):
             mm("pC", 0, "WTQ", c, "OQ", d, 128, i == 0, i == 3)
         if t == 1:
             early_constants()
-        tt(R("PM"), R("M16"), R("pB", 0, 128), MUL)
+        for p in (0, 64):
+            tt(R("PM", p0=p, p1=p + 64), R("M16", p0=p, p1=p + 64), R("pB", p, p + 64, p, p + 64), MUL)
         if t == 1:
+            late_constants()
             for b in (2, 3):
                 memset(R("ET", 512 * b, 512 * b + 512), 0.0)
+            quant("NQ", 0, P, "TN", 0)
         else:
             list_numbers(1)
 
@@ -401,10 +417,11 @@ def rank_program(g, core, T, topo):
             for w in ("N1", "B1", "N2", "B2"):
                 dmaq("y", w, K, "LX1", 0, K)
             dmaq("y", "HW", 32 + HS * rank, "LX1", 0, HS)
+            dmaq("y", "WIN1", K * rank, "LX1", 0, K)
             dma("y", R("TW"), None, inap=T.w[:, :])
-        rest = [lambda c=c: total_of(R("P8", c, c + 1), R("PM", 16 * c, 16 * c + 16)) for c in range(8)]
+        rest = [lambda c=c: total_of(R("P8", c, c + 1), R("PM", 16 * c, 16 * c + 16)) for c in range(4)]
         rest.append(lambda: ts(R("D0"), R("pC", 0, 64), -1.0, MUL, R("BROW"), ADD))
-        rest.append(lambda: ts(R("PIU%d" % t), R("P8"), 0.0, ADD))
+        rest.append(lambda: ts(R("PIU%d" % t), R("P8"), R("BDN"), ADD))
 
         def fill(n=1):
             for _ in range(n):
@@ -412,7 +429,7 @@ def rank_program(g, core, T, topo):
                     rest.pop(0)()
         for s in range(PEERS):
             o, kc = R("KR", 32 * s, 32 * s + 32), R(kl, s, s + 1)
-            if s in (1, 3):
+            if s in (1, 3, 5):
                 act(o, R("SGN"), AF.Copy, scale=kc)
             else:
                 ts(o, R("SGN"), kc, MUL)
@@ -431,6 +448,9 @@ def rank_program(g, core, T, topo):
                 fill()
                 total_of(R("XC", 1, 2), R("MM", 224, 448))
                 fill()
+        if t == 1:
+            for n in "12":
+                act(R("ROW" + n), R("RB"), AF.Identity, bias=R("BDP"))
         for m in (1, 0):
             ts(R("XR", 32 * m, 32 * m + 32), R("ONE", 0, 32), R("XC", m, m + 1), MUL, R("IC", m, m + 1), ADD)
         fill()
@@ -459,7 +479,7 @@ def rank_program(g, core, T, topo):
         tt(R("FM"), R("FS"), R("SW"), MAX)
         ts(R("ZU%d" % t), R("FM"), -1.0, ADD)
         if t == 1:
-            ts(R("INFO1"), R("FM"), 0.0, ADD)
+            ts(R("INFO1"), R("FM"), 0.0, GT, R("WA"), MUL)
         else:
             ts(R("INFO2"), R("FM"), 0.0, GT, R("WC"), MUL)
         pick("Z%d" % t, 0, "LX%d" % t, 2 * P, "ZU%d" % t, 0, 4)
@@ -472,11 +492,9 @@ def rank_program(g, core, T, topo):
         tt(R("VT"), R("GS"), R("D0"), ADD)
         tt(R("VU"), R("VT"), R("VM"), MUL)
         tt(R("VV"), R("VU"), R("pC", 0, 64), ADD)
-        for c, p in ((0, 0), (0, 64), (64, 64), (64, 0)):
-            copy("v", R("G", c, c + 64, p, p + 64), R("VV", p0=c, p1=c + 64))
-        run("v", lambda: g.vector.tensor_copy(A(row).indirect(A(off)), A(R("G"))), [R("G"), off], [row])
+        run("v", lambda: g.vector.tensor_copy(A(row).indirect(A(off)), A(R("VV"))), [R("VV"), off], [row])
         for k in range(2):
-            dma("y", R("LST%d" % t, 16 * k, 16 * k + 16), R("ROW%d" % t, 256 * k, 256 * k + 256, 0, 8))
+            dma("y", R("LST%d" % t, 16 * k, 16 * k + 16), R("ROW%d" % t, 0, 256, 64 * k, 64 * k + 8))
 
     def list_slots(t, base):
         for c, p in ((0, 0), (0, 64), (4, 64), (4, 0)):
@@ -513,33 +531,33 @@ def rank_program(g, core, T, topo):
         for b in range(4):
             copy("sv"[b % 2], R("HT", b, 256, step=4), R("pD", 512 * b, 512 * b + 64))
         quant(lxv, 2 * P + K, 128, "HT", 0)
-        pick(nxt, 0, lxv, 2 * P + K + 128, "PLU%d" % t, 0, 16)
+        if t == 1:
+            pick_codes(nxt, 0, lxv, 2 * P + K + 128, "PLU1", 0, 16)
+        else:
+            for h in range(2):
+                pick(nxt, 128 * h, lxv, 2 * P + K + 128, "PLU2", 8 * h, 8 * h + 8)
 
     local(1)
     post(1)
     merge(1)
-    to_all(R("Z1"), lambda r: R("WIN1", K * slot_at(r), K * slot_at(r) + K), "azc")
-    to_all(R("Z1s"), lambda r: R("WIN1s", K * slot_at(r), K * slot_at(r) + K), "azs")
+    to_all(R("Z1"), lambda r: R("WIN1", K * rank, K * rank + K), "azc")
+    to_all(R("Z1s"), lambda r: R("WIN1s", K * rank, K * rank + K), "azs")
     for b in range(4):
         copy("s", R("ET", 512 * b + b, 512 * b + 512, step=4), R("EYE"))
     list_places(1)
-    quant("NQ", 0, P, "TN", 0)
-    ts(R("B28"), R("B28"), Q16, ADD)
-    list_slots(1, PEERS * K)
+    list_slots(1, N * K)
     arrives([R("IL1")], "ai1", whole)
-    ts(R("V28"), R("IL1"), 0.0, GT)
-    tt(R("V29"), R("V28"), R("B28"), MUL)
+    ts(R("V28"), R("IL1"), 0.0, ADD)
     for c in range(4):
-        total_of(R("W5", c, c + 1), R("V29", c, 28, step=4))
+        total_of(R("W5", c, c + 1), R("V28", c, 28, step=4))
+    tt(R("W6"), R("W5"), R("CROW"), ADD)
     for k in (1, 0):
-        tt(R("AB", 4 * k, 4 * k + 4), R("FO", 4 * k, 4 * k + 4), R("W5"), MAX)
+        tt(R("AB", 4 * k, 4 * k + 4), R("FO", 4 * k, 4 * k + 4), R("W6"), MAX)
     ts(R("LAB1"), R("AB"), 0.0, ADD)
-    memset(R("HT", 256, 512), 0.0)
     list_own(1)
-    arrives([R("WIN1", 0, PEERS * K)], "azc", whole)
-    arrives([R("WIN1s", 0, PEERS * K)], "azs", whole)
-    renew(1, PEERS * K + 2 * P)
-    late_constants()
+    for s, sem in (("", "azc"), ("s", "azs")):
+        arrives([R("WIN1" + s, K * r, K * r + K) for r in peers], sem, whole)
+    renew(1, N * K + 2 * P)
 
     local(2)
     dmaq("y", "WIN2", K + 128, "LX2", 0, 2 * P)

from concourse.bass import DstId, RemoteDMATransfer
from concourse.mybir import dt, AluOpType, AxisListType, ActivationFunctionType as AF

N, P, K = 8, 256, 64
PEERS = N - 1
HS = K // N

SCRATCH, VIEW = {}, {}
SEMAPHORES = ["qv", "qs", "qt", "qg", "ls", "ak1", "ak2", "ai1", "ai2", "azc", "azs", "ahc", "ahs", "awc", "aws", "anum"] + ["d%d" % i for i in range(48)]


def _sb(name, w, d):
    SCRATCH[name] = ("sbuf", [128, w], d)
    VIEW[name] = (name, 0, w)


def _codes(name, w):
    _sb(name, w, "float8_e4m3fn_x4")
    _sb(name + "s", w, "uint8")


def _pool(name, d, parts):
    at = 0
    for n, w in parts:
        VIEW[n] = (name, at, w)
        at += (w + 15) // 16 * 16
    SCRATCH[name] = ("sbuf", [128, at], d)


for _n, _w in (("TL", 1024), ("TX", 1024), ("TN", 1024), ("TW", 512), ("U4", 4), ("Z4", 4), ("UT", 1280), ("ONE", 128),
               ("ZB", 128), ("CO", 512), ("WT", 2816), ("ET", 2048), ("EYE", 128), ("CT", 1024), ("OT", 768), ("HT", 512),
               ("MSK", 256), ("DS", 512)):
    _sb(_n, _w, "bfloat16")
_pool("BB", "bfloat16", (("EQK", 256), ("MM", 448), ("EQ", 256), ("EQN", 64)))
_pool("FC", "float32", (("CC", 16), ("IROW", 64), ("N16", 64), ("M16", 64), ("RB", 256), ("BDN", 1), ("BDP", 1), ("CROW", 4), ("KC", 4), ("CW8", 8),
                        ("HALF", 1), ("WA", 1), ("WC", 1), ("VX", 1), ("IC", 2), ("SGN", 32), ("DCOL", 1), ("BROW", 1)))
_pool("FD", "float32", (("AC", 4), ("RLA", 256), ("RXA", 256)))
_pool("FB", "float32", (("PRD", 256), ("JK", 768), ("PM", 64), ("P8", 4), ("K1S", 1), ("OKC", 2), ("D0", 64),
                        ("KR", 224), ("KW", 224), ("XC", 2), ("XR", 64), ("Y", 64), ("TY", 64), ("GS", 64), ("MU", 256), ("FS", 4),
                        ("SW", 4), ("FLD", 8), ("FM", 4), ("FO", 8), ("FP", 8), ("VT", 64), ("VM", 64), ("VU", 64), ("VV", 64), ("PN", 64),
                        ("NA", 2), ("NB", 2), ("V28", 28), ("W5", 4), ("W6", 4), ("AB", 8), ("V8", 8), ("VS", 1), ("HL8", 8)))
for _n, _w in (("NUM", 2), ("NL", 14), ("RES", 4), ("YO", 256)):
    _sb(_n, _w, "float32")
for _t in "12":
    for _n, _w in (("K1_", 1), ("KL", 7), ("ROW", 256), ("LST", 32)):
        _sb(_n + _t, _w, "float32")
    for _n, _w in (("INFO", 4), ("IL", 28)):
        _sb(_n + _t, _w, "uint16")
    _pool("UB" + _t, "uint16", tuple((_n + _t, _w) for _n, _w in (("PIU", 4), ("ZU", 4), ("NU", 4), ("LAB", 8), ("PLU", 32), ("HLU", 8))))
    _codes("Z" + _t, K)
    _codes("LXV" + _t, 2 * P + K + 128)
    _codes("B" + _t, 128)
    _codes("N" + _t, 128)
_sb("PI", 1, "int32")
_sb("II", 5, "int32")
for _n, _w in (("UQ", 320), ("LX1", 512), ("LX2", 512), ("LX3", 512), ("NQ", 256), ("WQ", 128), ("COQ", 128), ("WTQ", 704), ("EC", 512),
               ("CQ", 256), ("OQ", 192), ("WIN1", N * K + 2 * P), ("WIN2", K + 128 + 2 * P), ("HW", 32 + K)):
    _codes(_n, _w)
PSUM = {"pA": 1, "pB": 1, "pC": 1, "pD": 4, "pE": 1}
for _n in PSUM:
    SCRATCH[_n] = ("psum", [128, 512 * PSUM[_n]], "float32")
    VIEW[_n] = (_n, 0, 512 * PSUM[_n])

ADD, SUB, MUL, MAX, MIN = AluOpType.add, AluOpType.subtract, AluOpType.mult, AluOpType.max, AluOpType.min
GT, GE, LT, LE, EQL = AluOpType.is_gt, AluOpType.is_ge, AluOpType.is_lt, AluOpType.is_le, AluOpType.is_equal


def R(name, c0=0, c1=None, p0=0, p1=128, step=1):
    buf, at, width = VIEW[name]
    return (buf, at + c0, at + (width if c1 is None else c1), p0, p1, step)


def overlap(a, b):
    if a[4] <= b[3] or b[4] <= a[3] or a[2] <= b[1] or b[2] <= a[1]:
        return False
    return not (a[5] == b[5] and a[5] > 1 and (a[1] - b[1]) % a[5])


def covers(a, b):
    return a[5] == 1 and a[1] <= b[1] and a[2] >= b[2] and a[3] <= b[3] and a[4] >= b[4]


def bank(r):
    return (r[0], r[1] // 512 * 512, (r[2] + 511) // 512 * 512, 0, 128, 1) if r[0] in PSUM else r


def rank_program(g, core, T, topo):
    rank = T.rank_of(core)
    if rank is None:
        return
    peers = [r for r in range(N) if r != rank]
    queues = {"v": g.vector, "s": g.scalar, "t": g.tensor, "g": g, "y": g.sync}
    hist, known, count, total = {}, {q: {} for q in queues}, {q: 0 for q in queues}, {}
    seq, ndma = [0], [0]

    def waits(q, reads, writes, adds=False):
        need = []
        for r in reads:
            b, ps = bank(r), r[0] in PSUM
            for kind, box, tok in hist.get(r[0], []):
                if overlap(b, box) and (kind == "w" or ps and tok[2] != q):
                    need.append(tok)
        for w in writes:
            b = bank(w)
            for kind, box, tok in hist.get(w[0], []):
                if overlap(b, box) and not (adds and tok[2] == q):
                    need.append(tok)
        for tok in sorted(need, key=lambda k: -k[3]):
            if known[q].get(tok[0], 0) < tok[1]:
                queues[q].wait_ge(T.sem[tok[0]], tok[1])
                known[q][tok[0]] = tok[1]
                for s, n in tok[4].items():
                    known[q][s] = max(known[q].get(s, 0), n)

    def note(q, reads, writes, sem, val):
        seq[0] += 1
        tok = (sem, val, q, seq[0], dict(known[q]) if q in known else {})
        for w in writes:
            b = bank(w)
            hist[w[0]] = [h for h in hist.get(w[0], []) if not covers(b, h[1])] + [("w", b, tok)]
        for r in reads:
            hist.setdefault(r[0], []).append(("r", bank(r), tok))

    def run(q, make, reads, writes, adds=False):
        waits(q, reads, writes, adds)
        count[q] += 1
        make().then_inc(T.sem["q" + q], 1)
        total["q" + q] = count[q]
        note(q, reads, writes, "q" + q, count[q])

    def A(r):
        t = T[r[0]]
        rows = slice(None) if (r[3], r[4]) == (0, 128) else slice(r[3], r[4])
        return t[rows, r[1]:r[2]] if r[5] == 1 else t[rows, r[1]:r[2]:r[5]]

    def S8(r):
        return A(r).bitcast(dt.uint8) if SCRATCH[r[0]][2] == "float8_e4m3fn_x4" else A(r)

    def dma(q, out, in_, outap=None, inap=None):
        reads, writes = [in_] if in_ else [], [out] if out else []
        waits(q, reads, writes)
        sem = "d%d" % ndma[0]
        ndma[0] += 1
        queues[q].dma_start(outap if outap is not None else S8(out), inap if inap is not None else S8(in_)).then_inc(T.sem[sem], 16)
        total[sem] = 16
        note(q, reads, writes, sem, 16)

    def dmaq(q, out, c, in_, d, n):
        dma(q, R(out, c, c + n), R(in_, d, d + n))
        dma(q, R(out + "s", c, c + n), R(in_ + "s", d, d + n))

    def memset(r, v):
        run("v", lambda: g.vector.memset(A(r), v), [], [r])

    def copy(q, out, in_):
        if q == "v":
            run("v", lambda: g.vector.tensor_copy(A(out), A(in_)), [in_], [out])
        else:
            run("s", lambda: g.scalar.activation(A(out), A(in_), AF.Copy), [in_], [out])

    def tt(out, a, b, op):
        run("v", lambda: g.vector.tensor_tensor(A(out), A(a), A(b), op), [a, b], [out])

    def ts(out, a, s1, op0, s2=None, op1=None):
        reads = [a] + [s for s in (s1, s2) if isinstance(s, tuple)]
        v1 = A(s1) if isinstance(s1, tuple) else s1
        v2 = A(s2) if isinstance(s2, tuple) else s2
        if op1 is None:
            run("v", lambda: g.vector.tensor_scalar(A(out), A(a), v1, None, op0), reads, [out])
        else:
            run("v", lambda: g.vector.tensor_scalar(A(out), A(a), v1, v2, op0, op1), reads, [out])

    def act(out, in_, f, bias=None, scale=None, acc=None):
        kw = {}
        if bias is not None:
            kw["bias"] = A(bias) if isinstance(bias, tuple) else bias
        if scale is not None:
            kw["scale"] = A(scale) if isinstance(scale, tuple) else scale
        if acc is not None:
            kw["accum_out"] = A(acc)
        run("s", lambda: g.scalar.activation(A(out), A(in_), f, **kw), [in_] + [x for x in (bias, scale) if isinstance(x, tuple)],
            [out] + ([acc] if acc is not None else []))

    def fills(r, v):
        act(r, R("ZB", 0, r[2] - r[1], r[3], r[4]), AF.Identity, bias=float(v))

    def turn(out, in_):
        run("v", lambda: g.vector.transpose(A(out), A(in_)), [in_], [out])

    def total_of(out, in_, sizes=False):
        kw = {"apply_absolute_value": True} if sizes else {}
        run("v", lambda: g.vector.tensor_reduce(A(out), A(in_), AxisListType.X, ADD, **kw), [in_], [out])

    def quant(out, c, n, tile, e):
        o, s, i = R(out, c, c + n), R(out + "s", c, c + n), R(tile, 4 * e, 4 * e + 4 * n)
        run("v", lambda: g.vector.quantize_mx(A(o), A(s), A(i)), [i], [o, s])

    def mm(ps, b, w, c, x, d, n, start=True, stop=True):
        o = R(ps, 512 * b, 512 * b + n)
        l, ls, r, rs = R(w, c, c + 128), R(w + "s", c, c + 128), R(x, d, d + n), R(x + "s", d, d + n)
        run("t", lambda: g.tensor.matmul_mx(A(o), A(l), A(ls), A(r), A(rs), start, stop), [l, ls, r, rs], [o], not start)

    def pick_codes(out, c, win, width, lst, e, f):
        o, i, l = R(out, c, c + 16 * (f - e)), R(win, 0, width), R(lst, e, f)
        run("v", lambda: g.vector.tensor_copy(A(o).bitcast(dt.uint32), A(i).bitcast(dt.uint32).indirect(A(l))), [i, l], [o])

    def pick_scales(out, c, win, width, lst, e, f):
        o, i, l = R(out + "s", c, c + 16 * (f - e)), R(win + "s", 0, width), R(lst, e, f)
        run("s", lambda: g.scalar.activation(A(o), A(i).indirect(A(l)), AF.Copy), [i, l], [o])

    def pick(*a):
        pick_codes(*a)
        pick_scales(*a)

    def iota(out, pattern, base, cm):
        if SCRATCH[out[0]][2] == "int32":
            run("g", lambda: g.iota(A(out), pattern, base, cm), [], [out])
        else:
            run("g", lambda: g.iota(A(out), pattern, base, cm, allow_small_or_imprecise_dtypes=True), [], [out])

    def choose(r, pattern, op, fill, cm):
        run("g", lambda: g.affine_select(A(r), A(r), pattern, op, fill, 0, cm), [r], [r])

    def bits(es):
        return sum(1 << e for e in es)

    def dst(r):
        a = topo.addr(T.cores[r])
        return DstId(rid=a[0], pnc=a[1])

    shared = [e for e in topo.engines(core, T.cores[peers[0]]) if all(e in topo.engines(core, T.cores[r]) for r in peers)]
    whole = 1
    while 2 * whole <= len(shared):
        whole *= 2
    part = 1
    while 2 * part * PEERS <= len(shared):
        part *= 2

    def slot_at(r):
        return rank if rank < r else rank - 1

    def to_all(src, place, sem):
        waits("g", [src], [])
        t = RemoteDMATransfer(dst_ids=[dst(r) for r in peers], dma_engine_mask=bits(shared[:whole]), remote_sem=T.sem[sem],
                              srcs=[S8(src)], dsts=[S8(place(r)) for r in peers], alu_op=0)
        g.remote_dma_fused([t], local_sem=T.sem.ls)
        total["ls"] = total.get("ls", 0) + whole

    def to_each(src, place, sem):
        waits("g", [src(r) for r in peers], [])
        calls = []
        for i, r in enumerate(peers):
            calls.append(RemoteDMATransfer(dst_ids=[dst(r)], dma_engine_mask=bits(shared[part * i:part * i + part]), remote_sem=T.sem[sem],
                                           srcs=[S8(src(r))], dsts=[S8(place(r))], alu_op=0))
        g.remote_dma_fused(calls, local_sem=T.sem.ls)
        total["ls"] = total.get("ls", 0) + part * PEERS

    def arrives(regions, sem, per):
        total[sem] = PEERS * per
        note("remote", [], regions, sem, PEERS * per)

    ch = rank // 2
    dma("y", R("U4"), None, inap=T.u[:, 0:4])
    dma("s", R("Z4"), None, inap=T.z[:, 0:4])
    dma("y", R("TX"), None, inap=T.dm[:, :])
    dma("y", R("TL"), None, inap=T.lv[:, :])
    iota(R("PI"), [[0, 1]], 0, 1)
    iota(R("WT", 4 * 448, 4 * 704), [[0, 4 * 256]], 1, 0)
    memset(R("ZB"), 0.0)
    for p in (0, 64):
        fills(R("SGN", p0=p, p1=p + 64), -1.0 if p else 1.0)
        fills(R("BROW", p0=p, p1=p + 64), 2 * P + 1 if p else 2 * P + K + 1)
        fills(R("BDN", p0=p, p1=p + 64), -P if p else 0)
        fills(R("BDP", p0=p, p1=p + 64), P if p else 0)
        fills(R("DCOL", p0=p, p1=p + 64), P * rank - 1 - P if p else P * rank - 1)
        fills(R("IC", 0, 2, p + 32, p + 64), 0.0)
    memset(R("MSK", 0, 128), 0.5)
    memset(R("MSK", 128, 256), -0.5)
    choose(R("MSK", 128, 256), [[1, 128]], GT, 0.5, -1)
    choose(R("MSK", 0, 128), [[1, 128]], GT, -0.5, -1)
    memset(R("ONE"), 1.0)
    memset(R("UT", 512, 768), 0.0)
    for i, (op, v) in enumerate(((AluOpType.bitwise_and, 15), (AluOpType.arith_shift_right, 4), (AluOpType.bitwise_and, 63),
                                 (AluOpType.bitwise_and, 31), (AluOpType.bitwise_and, 7))):
        ts(R("II", i, i + 1), R("PI"), v, op)
    memset(R("CO"), 0.0)
    for c in (0, 1, 258, 259):
        memset(R("CO", c, c // 256 * 256 + 256, step=4), 1.0)
    copy("v", R("CC", 0, 5), R("II"))
    Q16, TGT = R("CC", 0, 1), R("CC", 2, 3)
    iota(R("CROW"), [[16, 4]], 0, 0)
    iota(R("N16"), [[0, 4], [1, 16]], 0, 0)
    for a in (64, 256):
        iota(R("WT", 4 * a, 4 * a + 512), [[0, 512]], 1, 0)
    iota(R("IROW"), [[1, 64]], 0, 0)
    iota(R("ET", 0, 512), [[0, 512]], 0, 0)
    for t in range(4):
        if t < 2:
            act(R("UT", 768 + t, 1280, step=4), R("ZB"), AF.Identity, bias=R("Z4", t, t + 1))
        else:
            ts(R("UT", 768 + t, 1280, step=4), R("ONE"), R("Z4", t, t + 1), MUL)
        ts(R("UT", t, 512, step=4), R("ONE"), R("U4", t, t + 1), MUL)
    quant("UQ", 0, 320, "UT", 0)
    quant("LX1", P, P, "TX", 0)
    for o, i, m, a in ((8, 0, 16.0, 0.0), (9, 1, 1.0, 8.0), (5, 0, 1.0, 1.0), (6, 1, 16.0, 0.0), (7, 1, 16.0, 128.0)):
        act(R("CC", o, o + 1), R("CC", i, i + 1), AF.Identity, bias=a, scale=m)
    quant("COQ", 0, 128, "CO", 0)
    quant("LX1", 0, P, "TL", 0)
    for a in (0, 192, 384):
        memset(R("WT", 4 * a, 4 * a + 256), 0.0)
    memset(R("EYE"), 0.5)
    dmaq("y", "WIN1", N * K, "LX1", 0, 2 * P)
    dma("y", R("TN"), None, inap=T.nz[:, :])

    def compare(typ):
        bk, d0, m0 = (2, 256, 128) if typ == "X" else (0, 0, 0)
        lo, le, on = (LT, LE, GT) if typ == "X" else (GT, GE, LT)
        row = "R%sA" % typ
        ts(R("CT", 512 + bk, 1024, step=4), R(row, 128, 256), R("AC", bk, bk + 1), le)
        ts(R("CT", bk + 1, 512, step=4), R(row, 0, 128), R("AC", bk + 1, bk + 2), lo)
        for h in range(2):
            tt(R("CT", 513 * h + bk, 512 * h + 512, step=4), R("DS", d0 + 128 * h, d0 + 128 * h + 128), R("MSK", m0, m0 + 128), on)

    def local(t):
        lx, k1 = "LX%d" % t, "K1_%d" % t
        for typ in "XL":
            c0, bk, row, d0 = (P, 2, "pB", 256) if typ == "X" else (0, 0, "pA", 0)
            q, qc = "UQ", 192 if typ == "X" else 0
            at = (("pE", 0), ("pC", 0)) if typ == "X" else (("pD", 0), ("pD", 1))
            mm(row, 0, q, qc, lx, c0, P)
            for h in range(2):
                mm(at[h][0], at[h][1], lx, c0 + 128 * h, q, qc, 128)
            act(R("R%sA" % typ), R(row, 0, P), AF.Abs)
            if t == 2 and typ == "X":
                pick_scales("LX2", 0, "LXV1", 2 * P + K + 128, "PLU1", 0, 16)
            for h in range(2):
                total_of(R("AC", bk + h, bk + h + 1), R(at[h][0], 512 * at[h][1], 512 * at[h][1] + 1), True)
            for h in range(2):
                act(R("DS", d0 + 128 * h, d0 + 128 * h + 128), R("R%sA" % typ, 128 * h, 128 * h + 128), AF.Sign,
                    bias=R("AC", bk + h, bk + h + 1), scale=-1.0)
            compare(typ)
        mm("pC", 0, "UQ", 64, lx, 0, P, True, False)
        mm("pC", 0, "UQ", 128, lx, P, P, False, True)
        quant("CQ", 0, P, "CT", 0)
        for h in range(2):
            mm(("pE", "pA")[h], 0, "COQ", 0, "CQ", 128 * h, 128)
        if t == 1:
            memset(R("OT"), 0.0)
            memset(R("OT", 258, 512, step=4), 1.0)
            for m, b, c in ((448, 0, 8), (448, 1, 8), (576, 0, 1), (576, 1, 9), (64, 0, 5), (64, 1, 5), (256, 0, 6), (256, 1, 7)):
                act(R("WT", 4 * m + b, 4 * m + 512, step=4), R("ZB", 0, 128), AF.Identity, bias=R("CC", c, c + 1))
        for h in range(2):
            ts(R("EQK", 128 * h, 128 * h + 128), R(("pE", "pA")[h], 0, 128), TGT, EQL)
        for h in range(2):
            tt(R("PRD", 128 * h, 128 * h + 128), R("EQK", 128 * h, 128 * h + 128), R("pC", 128 * h, 128 * h + 128), MUL)
        total_of(R(k1), R("PRD"), True)
        to_all(R(k1), lambda r: R("KL%d" % t, slot_at(r), slot_at(r) + 1), "ak%d" % t)

    def early_constants():
        act(R("KC"), R("CROW"), AF.Identity, bias=Q16)
        act(R("WA"), Q16, AF.Identity, bias=float(K * rank))
        ts(R("M16"), R("N16"), Q16, EQL)
        for p in (0, 64):
            for m in range(2):
                act(R("IC", m, m + 1, p, p + 32), R("CC", 3, 4, p, p + 32), AF.Identity, bias=32.0 * m)

    def late_constants():
        ts(R("HALF"), Q16, 8.0, GE if rank % 2 else LT, float(64 + 16 * rank - 16 * ch), MUL)
        act(R("WC"), R("CC", 4, 5), AF.Identity, bias=float(HS * rank + 1))
        act(R("VX"), Q16, AF.Identity, bias=float(16 * (ch % 2) - 31))
        for c in (0, 4):
            copy("s", R("CW8", c, c + 4), R("KC"))
        for c in (0, 4):
            act(R("CW8", c + ch, c + ch + 1), R("KC", ch, ch + 1), AF.Identity, bias=R("HALF"))

    def post(t):
        for h in range(2):
            mm("pD", h, "CQ", 128 * h, "COQ", 0, 128)
        if t == 1:
            iota(R("RB"), [[1, 16], [16, 16]], 1, 0)
            choose(R("EYE"), [[-1, 128]], EQL, 0.0, 1)
            iota(R("ET", 512, 1024), [[0, 512]], 0, 0)
            for b in range(4):
                fills(R("HT", 256 + 64 * b, 320 + 64 * b), 0.0)
        for c in (256, 0):
            for h in range(2):
                ts(R("OT", c + h, c + 256, step=4), R("IROW"), R("pD", 512 * h + c // 4, 512 * h + c // 4 + 1), EQL)
        tt(R("K1S"), R("K1_%d" % t), R("SGN", 0, 1), MUL)
        quant("OQ", 0, 192, "OT", 0)
        for c, s, d in ((0, 0, 0), (0, 0, 32), (0, 64, 64), (0, 64, 96), (1, 32, 0), (1, 32, 32), (1, 96, 64), (1, 96, 96)):
            copy("s", R("OKC", c, c + 1, d, d + 32), R("K1S", 0, 1, s, s + 32))
        if t == 1:
            quant("WTQ", 448, 256, "WT", 448)
            quant("WTQ", 0, 448, "WT", 0)
        mm("pB", 0, "WTQ", 448, "OQ", 0, 128, True, False)
        mm("pB", 0, "WTQ", 576, "OQ", 0, 128, False, True)
        for i, (c, d) in enumerate(((128, 0), (320, 0), (0, 64), (192, 64))):
            mm("pC", 0, "WTQ", c, "OQ", d, 128, i == 0, i == 3)
        if t == 1:
            early_constants()
        for p in (0, 64):
            tt(R("PM", p0=p, p1=p + 64), R("M16", p0=p, p1=p + 64), R("pB", p, p + 64, p, p + 64), MUL)
        if t == 1:
            late_constants()
            for b in (2, 3):
                memset(R("ET", 512 * b, 512 * b + 512), 0.0)
            quant("NQ", 0, P, "TN", 0)
        else:
            list_numbers(1)

    def merge(t):
        kl = "KL%d" % t
        arrives([R(kl)], "ak%d" % t, whole)
        if t == 1:
            waits("y", [R(kl)], [])
            dmaq("y", "LXV1", 0, "LX1", 0, 2 * P)
            for w in ("N1", "B1", "N2", "B2"):
                dmaq("y", w, K, "LX1", 0, K)
            dmaq("y", "HW", 32 + HS * rank, "LX1", 0, HS)
            dmaq("y", "WIN1", K * rank, "LX1", 0, K)
            dma("y", R("TW"), None, inap=T.w[:, :])
        rest = [lambda c=c: total_of(R("P8", c, c + 1), R("PM", 16 * c, 16 * c + 16)) for c in range(4)]
        rest.append(lambda: ts(R("D0"), R("pC", 0, 64), -1.0, MUL, R("BROW"), ADD))
        rest.append(lambda: ts(R("PIU%d" % t), R("P8"), R("BDN"), ADD))

        def fill(n=1):
            for _ in range(n):
                if rest:
                    rest.pop(0)()
        for s in range(PEERS):
            o, kc = R("KR", 32 * s, 32 * s + 32), R(kl, s, s + 1)
            if s in (1, 3, 5):
                act(o, R("SGN"), AF.Copy, scale=kc)
            else:
                ts(o, R("SGN"), kc, MUL)
        fill()
        turn(R("KW"), R("KR"))
        fill()
        for m in range(2):
            own = R("OKC", m, m + 1)
            if rank:
                ts(R("MM", 224 * m, 224 * m + 32 * rank), R("KW", 0, 32 * rank), own, LE)
            if rank < PEERS:
                ts(R("MM", 224 * m + 32 * rank, 224 * m + 224), R("KW", 32 * rank, 224), own, LT)
            if m == 0:
                act(R("JK", 256, 480), R("MM", 0, 224), AF.Copy, acc=R("XC", 0, 1))
            else:
                fill()
                total_of(R("XC", 1, 2), R("MM", 224, 448))
                fill()
        if t == 1:
            for n in "12":
                act(R("ROW" + n), R("RB"), AF.Identity, bias=R("BDP"))
        for m in (1, 0):
            ts(R("XR", 32 * m, 32 * m + 32), R("ONE", 0, 32), R("XC", m, m + 1), MUL, R("IC", m, m + 1), ADD)
        fill()
        turn(R("Y"), R("XR"))
        fill()
        for p in (32, 0, 96, 64):
            o = p - 32 if p % 64 else p + 32
            copy("v", R("TY", p0=p, p1=p + 32), R("Y", p0=o, p1=o + 32))
        fill()
        tt(R("GS"), R("Y"), R("TY"), ADD)
        for step in "e0 e1 m0 m1 e2 e3 m2 m3".split():
            c = int(step[1])
            e, u = R("EQ", 64 * c, 64 * c + 64), R("MU", 64 * c, 64 * c + 64)
            if step[0] == "e":
                ts(e, R("GS"), R("KC", c, c + 1), EQL)
                continue
            tt(u, e, R("pC", 0, 64), MUL)
            if c >= 2:
                total_of(R("FS", c, c + 1), u)
            else:
                act(R("JK", 512 + 64 * c, 576 + 64 * c), u, AF.Copy, acc=R("FS", c, c + 1))
        fill()
        copy("v", R("SW", p0=64), R("FS", p1=64))
        copy("v", R("SW", p1=64), R("FS", p0=64))
        fill()
        tt(R("FM"), R("FS"), R("SW"), MAX)
        ts(R("ZU%d" % t), R("FM"), -1.0, ADD)
        if t == 1:
            ts(R("INFO1"), R("FM"), 0.0, GT, R("WA"), MUL)
        else:
            ts(R("INFO2"), R("FM"), 0.0, GT, R("WC"), MUL)
        pick("Z%d" % t, 0, "LX%d" % t, 2 * P, "ZU%d" % t, 0, 4)
        fill(9)
        to_all(R("INFO%d" % t), lambda r: R("IL%d" % t, 4 * slot_at(r), 4 * slot_at(r) + 4), "ai%d" % t)

    def list_places(t):
        row, off = R("ROW%d" % t), R("PIU%d" % t)
        ts(R("VM"), R("GS"), float(K), LT)
        tt(R("VT"), R("GS"), R("D0"), ADD)
        tt(R("VU"), R("VT"), R("VM"), MUL)
        tt(R("VV"), R("VU"), R("pC", 0, 64), ADD)
        run("v", lambda: g.vector.tensor_copy(A(row).indirect(A(off)), A(R("VV"))), [R("VV"), off], [row])
        for k in range(2):
            dma("y", R("LST%d" % t, 16 * k, 16 * k + 16), R("ROW%d" % t, 0, 256, 64 * k, 64 * k + 8))

    def list_slots(t, base):
        for c, p in ((0, 0), (0, 64), (4, 64), (4, 0)):
            copy("s", R("FLD", c, c + 4, p, p + 64), R("FS", p0=16 * c, p1=16 * c + 64))
        ts(R("NU%d" % t), R("FLD", 0, 4), -1.0, ADD)
        ts(R("FP"), R("FLD"), 0.0, GT, float(base - 1), MUL)
        pick("N%d" % t, 0, "NQ", P, "NU%d" % t, 0, 4)
        tt(R("FO"), R("FP"), R("FLD"), ADD)
        if t == 1:
            quant("EC", 0, 512, "ET", 0)
        for k in range(4):
            mm("pD", k, "EC", 128 * k, "N%d" % t, 0, 128, True, False)

    def list_own(t):
        ts(R("EQN"), R("GS"), TGT, EQL)
        tt(R("PN"), R("EQN"), R("pC", 0, 64), MUL)

    def list_numbers(t):
        a, b = t - 1, t
        total_of(R("NA", a, b), R("PN"))
        ts(R("NB", a, b), R("NA", a, b), 0.0, GT, R("DCOL"), MUL)
        tt(R("NUM", a, b), R("NB", a, b), R("NA", a, b), ADD)
        if t == 2:
            to_all(R("NUM"), lambda r: R("NL", 2 * slot_at(r), 2 * slot_at(r) + 2), "anum")

    def renew(t, width):
        win, lxv, nxt, lab = "WIN%d" % t, "LXV%d" % t, "LX%d" % (t + 1), "LAB%d" % t
        pick("B%d" % t, 0, win, width, lab, 4, 8)
        for b in range(4):
            mm("pD", b, "EC", 128 * b, "B%d" % t, 0, 128, False, True)
        pick(lxv, 2 * P, win, width, lab, 0, 4)
        ts(R("PLU%d" % t), R("LST%d" % t), -1.0, ADD)
        pick(nxt, P, lxv, 2 * P + K, "PLU%d" % t, 16, 32)
        for b in range(4):
            copy("sv"[b % 2], R("HT", b, 256, step=4), R("pD", 512 * b, 512 * b + 64))
        quant(lxv, 2 * P + K, 128, "HT", 0)
        if t == 1:
            pick_codes(nxt, 0, lxv, 2 * P + K + 128, "PLU1", 0, 16)
        else:
            for h in range(2):
                pick(nxt, 128 * h, lxv, 2 * P + K + 128, "PLU2", 8 * h, 8 * h + 8)

    local(1)
    post(1)
    merge(1)
    to_all(R("Z1"), lambda r: R("WIN1", K * rank, K * rank + K), "azc")
    to_all(R("Z1s"), lambda r: R("WIN1s", K * rank, K * rank + K), "azs")
    for b in range(4):
        copy("s", R("ET", 512 * b + b, 512 * b + 512, step=4), R("EYE"))
    list_places(1)
    list_slots(1, N * K)
    arrives([R("IL1")], "ai1", whole)
    ts(R("V28"), R("IL1"), 0.0, ADD)
    for c in range(4):
        total_of(R("W5", c, c + 1), R("V28", c, 28, step=4))
    tt(R("W6"), R("W5"), R("CROW"), ADD)
    for k in (1, 0):
        tt(R("AB", 4 * k, 4 * k + 4), R("FO", 4 * k, 4 * k + 4), R("W6"), MAX)
    ts(R("LAB1"), R("AB"), 0.0, ADD)
    list_own(1)
    for s, sem in (("", "azc"), ("s", "azs")):
        arrives([R("WIN1" + s, K * r, K * r + K) for r in peers], sem, whole)
    renew(1, N * K + 2 * P)

    local(2)
    dmaq("y", "WIN2", K + 128, "LX2", 0, 2 * P)
    dmaq("y", "LXV2", 0, "LX2", 0, 2 * P)
    post(2)
    merge(2)
    for s, sem in (("", "ahc"), ("s", "ahs")):
        to_each(lambda r: R("Z2" + s, HS * r, HS * r + HS), lambda r: R("HW" + s, 32 + HS * rank, 32 + HS * rank + HS), sem)
    pick("HW", 0, "LX2", 2 * P, "ZU2", ch // 2 * 2, ch // 2 * 2 + 2)
    ts(R("V8", rank, rank + 1), R("FM", ch, ch + 1), 0.0, GT, R("VX"), MUL)
    list_places(2)
    arrives([R("IL2")], "ai2", whole)
    if rank:
        ts(R("V8", 0, rank), R("IL2", ch, 4 * rank, step=4), 0.0, ADD)
    if rank < PEERS:
        ts(R("V8", rank + 1, N), R("IL2", 4 * rank + ch, 4 * PEERS, step=4), 0.0, ADD)
    total_of(R("VS"), R("V8"))
    ts(R("HL8"), R("V8"), -1.0, MUL, R("VS"), ADD)
    ts(R("HLU2"), R("HL8"), float(K), MIN, 31.0, ADD)
    others = [(a, b) for a, b in ((0, HS * rank), (HS * rank + HS, K)) if a < b]
    for s, sem in (("", "ahc"), ("s", "ahs")):
        arrives([R("HW" + s, 32 + a, 32 + b) for a, b in others], sem, part)
    pick("WIN2", K, "HW", 32 + K, "HLU2", 0, 8)
    hc = K + HS * (rank % 2)
    for s, sem in (("", "awc"), ("s", "aws")):
        to_each(lambda r: R("WIN2" + s, hc + 16 * r, hc + 16 * r + HS), lambda r: R("WIN2" + s, HS * rank, HS * rank + HS), sem)
    list_slots(2, K + 128)
    tt(R("AB"), R("FO"), R("CW8"), MAX)
    ts(R("LAB2"), R("AB"), 0.0, ADD)
    list_own(2)
    list_numbers(2)
    quant("WQ", 0, 128, "TW", 0)
    for s, sem in (("", "awc"), ("s", "aws")):
        arrives([R("WIN2" + s, a, b) for a, b in others], sem, part)
    renew(2, K + 128 + 2 * P)

    for h in range(2):
        mm("pD", h, "WQ", 0, "LX3", 128 * h, 128)
    dma("y", None, R("LX3", P, 2 * P), outap=T.oc[:, 4 * P:8 * P])
    for k in range(4):
        dma("y", None, R("LX3s", P, 2 * P, 32 * k, 32 * k + 4), outap=T.osc[4 * k:4 * k + 4, P:2 * P])
    arrives([R("NL")], "anum", whole)
    for t in range(2):
        total_of(R("RES", t, t + 1), R("NL", t, 14, step=2))
    tt(R("RES", 2, 4), R("RES", 0, 2), R("NUM"), ADD)
    dma("y", None, R("LX3", 0, P), outap=T.oc[:, 0:4 * P])
    for h in range(2):
        copy("sv"[h], R("YO", 128 * h, 128 * h + 128), R("pD", 512 * h, 512 * h + 128))
    for k in range(4):
        dma("y", None, R("LX3s", 0, P, 32 * k, 32 * k + 4), outap=T.osc[4 * k:4 * k + 4, 0:P])
    dma("s", None, R("YO", 0, 128), outap=T.y[:, 0:128])
    for t in range(2):
        dma("s", None, R("RES", 2 + t, 3 + t, 0, 64), outap=T.lw[t:t + 1, :])
        dma("s", None, R("RES", 2 + t, 3 + t, 64, 128), outap=T.sw[t:t + 1, :])
    dma("y", None, R("YO", 128, 256), outap=T.y[:, 128:256])
    for sem in total:
        if known["g"].get(sem, 0) < total[sem]:
            g.wait_ge(T.sem[sem], total[sem])
